import numpy as np, ml_dtypes
CORES = [8,136,40,168]
N = 4
BF = ml_dtypes.bfloat16
def gentries(a):
    return np.ascontiguousarray(a.reshape(8, 16, -1).transpose(0, 2, 1)).reshape(8, -1)
def gtable(e):
    e = np.asarray(e); return np.ascontiguousarray(e.reshape(8, -1, 16).transpose(0, 2, 1)).reshape(128, -1).astype(np.int32)
V, L, CAP, RO, LO, HI = 3072, 96, 320, 3, 240, 440
SHIFTS = (1, 3)
GH = L * len(SHIFTS)
SZ = np.array([LO // 20, (LO + HI) // 16, HI // 5, 127])
def fold(v):
    return np.abs((v + 127) % 508 - 254) - 127
def steps(rng, a, b):
    u = rng.random((N, 8, 1, V)); w = np.where(u < a, SZ[0], np.where(u < 1 - b, SZ[1], np.where(u < 1 - 0.4 * b, SZ[2], SZ[3])))
    return fold(rng.integers(-127, 128, (N, 8, 16, 1)) + np.add.accumulate(rng.integers(-w, w + 1, (N, 8, 16, V)), axis=3))
def walk(rng, t):
    i = np.arange(16); m = t[..., None] // 16 + ((i + np.arange(V)[:, None]) % 16 < t[..., None] % 16)
    kind = rng.integers(0, 4, t.shape); s = (kind == 1) & (t > 259); one = kind == 2
    four = np.stack([i // 4 == h for h in range(4)] + [i % 4 == h for h in range(4)]); u = rng.integers(0, 8, np.count_nonzero(s))
    fin = np.add.accumulate(four.astype(np.int64), axis=1) - 1; fout = np.add.accumulate((~four).astype(np.int64), axis=1) - 1
    a = 257 + 2 * rng.integers(0, 2, (u.size, 1)); b = t[s][:, None] - a
    m[s] = np.where(four[u], a // 4 + (fin[u] < a % 4), b // 12 + (fout[u] < b % 12))
    y = np.zeros((N, 8, 16, V), np.int64); p = rng.integers(-127, 128, (N, 8, 16)); z = 2 * rng.integers(0, 2, (V, N, 8, 16)) - 1
    for k in range(V):
        y[..., k] = p; tk = t[:, :, k, None]; h = np.abs(p)
        big = np.minimum(tk, 127 + np.max(h, axis=2, keepdims=True)); w = tk - big; o = (i - np.argmax(h, axis=2)[..., None]) % 16
        mk = np.where(one[:, :, k, None], np.where(o == 0, big, w // 15 + (o <= w % 15)), m[:, :, k])
        p = p + mk * np.where(np.abs(p + z[k] * mk) <= 127, z[k], np.where(p > 0, -1, 1))
    return y
def lay(rng, y, n, m, mode, ok):
    x = np.zeros((N, 8, 16, V), np.int64); nx = np.full((N, 8, V), -1, np.int64); hd = np.zeros((N, 8, GH), np.int64)
    for q in range(N):
        for g in range(8):
            k, mm, o = int(n[q, g]), int(m[q, g]), rng.permutation(V)
            if mode[q, g] == 1: o = np.concatenate([V - k + rng.permutation(k), rng.permutation(V - k)])
            if mode[q, g] == 2: o = np.concatenate([rng.permutation(k), k + rng.permutation(V - k)])
            if mode[q, g] == 3:
                o = np.concatenate([rng.permutation(V - 1), np.full(1, V - 1)])
                o = np.concatenate([o[:k][o[:k] % 2 == 1], o[:k][o[:k] % 2 == 0], o[k:]])
            if mode[q, g] == 4:
                ev, od, w = 2 * rng.permutation(V // 2), 2 * rng.permutation(V // 2) + 1, k // 2
                o = np.concatenate([np.stack([ev[:w], od[:w]], axis=1).reshape(-1), rng.permutation(np.concatenate([ev[w:], od[w:]]))])
            if mode[q, g] == 5:
                z = rng.permutation(16)[np.arange(V) % 16]; fr = z == 15
                fr[np.flatnonzero((z > 1) & (z < 15))[-(V - k - V // 16):]] = True
                lv = rng.permutation(np.flatnonzero(~fr)); lv = lv[np.argsort(z[lv], kind="stable")]
                a = ~ok[q, g, :k]; a = a | np.concatenate([a[1:], np.zeros(1, bool)]); c = np.count_nonzero(a)
                o[:k][a] = rng.permutation(lv[:c]); o[:k][~a] = rng.permutation(lv[c:]); o[k:] = np.flatnonzero(fr)
            x[q, g][:, o] = y[q, g]
            u = o[:k]; c = np.sort(rng.permutation(k - 1)[:mm - 1]) + 1
            a = np.concatenate([np.zeros(1, np.int64), c]); b = np.concatenate([c, np.full(1, k)]) - 1
            e = min((mm + 1) // 2 + int(rng.integers(0, mm // 2 + 1)), GH)
            nx[q, g, u[:-1]] = u[1:]; nx[q, g, u[b]] = u[a]
            nx[q, g, u[b[rng.permutation(mm)[:e]]]] = V + rng.permutation(GH)[:e]
            h = u[(u % 2 == 0) & ok[q, g, :k]]; d = rng.permutation(h[nx[q, g, h] >= V])[:GH // 4]
            hd[q, g] = rng.permutation(np.resize(np.concatenate([d, rng.permutation(np.setdiff1d(h, d))]), GH))
    return x, nx, hd
def nears(rng, x, nx, hd):
    for q in range(N):
        for g in range(8):
            i = rng.permutation(np.flatnonzero(nx[q, g] >= V)); i = i[:(i.size + 1) // 2]
            if i.size == 0: continue
            t = nx[q, g, i] - V; src = (q + np.array(SHIFTS)[t // L]) % N
            w = SZ[rng.integers(0, 3, (i.size, 1))]
            x[q, g][:, i] = np.clip(x[src, g, :, hd[src, g, t]] + rng.integers(-w, w + 1, (i.size, 16)), -127, 127).T
def off(rng, p, t):
    m = t[:, None] // 16 + ((np.arange(16) + rng.integers(0, 16, (t.size, 1))) % 16 < t[:, None] % 16)
    z = 2 * rng.integers(0, 2, p.shape) - 1
    return p + m * np.where(np.abs(p + z * m) <= 127, z, np.where(p > 0, -1, 1))
def edge(rng, x, nx, hd):
    for q in range(N):
        for g in range(8):
            i = np.flatnonzero((nx[q, g] >= V) & ~np.isin(np.arange(V), hd[q, g]))
            if i.size == 0: continue
            t = nx[q, g, i] - V; src = (q + np.array(SHIFTS)[t // L]) % N
            x[q, g][:, i] = off(rng, x[src, g, :, hd[src, g, t]], rng.choice(np.array([LO - 1, LO, HI - 1, HI, HI, HI, HI + 1, HI + 1]), i.size)).T
            before = np.full(V, -1, np.int64); own = np.flatnonzero((nx[q, g] >= 0) & (nx[q, g] < V)); before[nx[q, g, own]] = own
            b = before[i]; s = (b >= 0) & ~np.isin(b, hd[q, g])
            x[q, g][:, b[s]] = off(rng, x[q, g][:, i[s]].T, rng.choice(np.array([0, 1, LO // 2, LO - 1, LO - 1, LO]), np.count_nonzero(s))).T
def pack(x, nx, hd):
    return {"x": np.ascontiguousarray(x.reshape(N, 128, V)).astype(np.float32).astype(BF), "nxt": np.stack([gtable(a) for a in nx]), "head": np.stack([gtable(a) for a in hd])}
def sizes(rng):
    return rng.integers(V // 2, V - RO * CAP + 1, (N, 8)), rng.integers(GH // 2, GH + 33, (N, 8))
ANY = np.ones((N, 8, V), bool); MIX = np.zeros((N, 8), np.int64)
def setup_inputs(rng):
    n, m = sizes(rng); a = rng.choice(np.array([0.25, 0.35, 0.5]), (N, 8, 1, 1)); b = rng.choice(np.array([0.02, 0.06, 0.12, 0.25]), (N, 8, 1, 1))
    x, nx, hd = lay(rng, steps(rng, a, b), n, m, MIX, ANY); nears(rng, x, nx, hd)
    return pack(x, nx, hd)
def setup_inputs_cap(rng):
    k = V - RO * CAP; kinds = (CAP, CAP + 1, CAP - 1, 0, 1, k - 4, CAP, 0); modes = (3, 0, 0, 4, 0, 3, 5, 0)
    far = np.zeros((N, 8, V), bool); mode = np.zeros((N, 8), np.int64); m = np.ones((N, 8), np.int64); R = np.full((N, 8, 1, 1), HI // 32)
    for q in range(N):
        for g in range(8):
            j = (g + q) % 8; far[q, g, 3 + 2 * rng.permutation((k - 4) // 2)[:kinds[j] // 2]] = True
            far[q, g, 0] = kinds[j] % 2 == 1; mode[q, g] = modes[j]
            if j == 3: R[q, g] = (LO - 1) // 32
            if j == 7: far[q, g, :k - 48] = True; m[q, g] = 2 * GH
    c = rng.integers(80, 101, (8, 16, 1)) * (2 * rng.integers(0, 2, (8, 16, 1)) - 1)
    y = np.where(far[:, :, None, :], -c, c) + rng.integers(-R, R + 1, (N, 8, 16, V))
    return pack(*lay(rng, y, np.full((N, 8), k), m, mode, ~far))
def setup_inputs_ties(rng):
    n, m = sizes(rng); t = rng.choice(np.array([0, 1, LO - 1, LO, LO + 1, HI - 1, HI, HI, HI + 1, HI + 1]), (N, 8, V))
    x, nx, hd = lay(rng, walk(rng, t), n, m, MIX, ANY); edge(rng, x, nx, hd)
    return pack(x, nx, hd)
def setup_inputs_loops(rng):
    n, m = sizes(rng); m = n // 3
    x, nx, hd = lay(rng, steps(rng, 0.6, 0.1), n, m, rng.integers(0, 3, (N, 8)), ANY)
    hd[:, ::2] = np.take_along_axis(hd[:, ::2], rng.integers(0, 3, (N, 4, GH)), 2)
    q, g, z = int(rng.integers(0, N)), int(rng.integers(0, 8)), V - 2
    nx[q, g] = -1; nx[q, g, z] = z; hd[q, g] = z
    nears(rng, x, nx, hd)
    return pack(x, nx, hd)
def setup_inputs_churn(rng):
    n, m = sizes(rng); n[:, ::2] = V - RO * CAP
    x, nx, hd = lay(rng, steps(rng, 0.55, 0.35), n, m, rng.integers(0, 3, (N, 8)), ANY); nears(rng, x, nx, hd)
    return pack(x, nx, hd)
def setup_inputs_spread(rng):
    n, m = sizes(rng); y = np.rint(127 * np.exp2(-7 * rng.random((N, 8, 1, V))) * (2 * rng.random((N, 8, 16, V)) - 1)).astype(np.int64)
    x, nx, hd = lay(rng, y, n, m, MIX, ANY)
    return pack(x, nx, hd)
def check_inputs(d):
    bad = []; xf = np.asarray(d["x"]).astype(np.float32)
    if not np.all(np.abs(xf) <= 127) or not np.all(np.rint(xf) == xf): bad.append("x: whole numbers from -127 to 127")
    nl = np.stack([gentries(a) for a in d["nxt"]]).astype(np.int64); hl = np.stack([gentries(a) for a in d["head"]]).astype(np.int64)
    if np.min(nl) < -1 or np.max(nl) > V + GH - 1: bad.append("range of nxt")
    if np.min(hl) < 0 or np.max(hl) > V - 1: bad.append("range of head")
    if "range of nxt" in bad or "range of head" in bad: return bad
    live = nl >= 0; own = live & (nl < V); s = np.sort(nl, axis=2)
    if np.any((s[:, :, 1:] == s[:, :, :-1]) & (s[:, :, 1:] >= 0)): bad.append("nxt: one predecessor a node")
    if np.any(own & ~np.take_along_axis(live, np.where(own, nl, 0), 2)): bad.append("nxt names live nodes only")
    if np.any(hl % 2 == 1): bad.append("heads are even")
    if not np.all(np.take_along_axis(live, hl, 2)): bad.append("heads are live")
    if np.min(np.count_nonzero(~live, axis=2)) < RO * CAP: bad.append("free nodes")
    return bad
def reference(x, nxt, head):
    X = x.astype(np.float32).astype(np.int64).reshape(N, 8, 16, V)
    nx = np.stack([gentries(a) for a in nxt]).astype(np.int64); hd = np.stack([gentries(a) for a in head]).astype(np.int64)
    even = np.arange(V) % 2 == 0
    for rnd in range(RO):
        ghost = np.stack([np.concatenate([np.take_along_axis(X[(r + s) % N], hd[(r + s) % N][:, None, b * L:(b + 1) * L], 2) for b, s in enumerate(SHIFTS)], axis=2) for r in range(N)])
        live = nx >= 0
        Xn = np.take_along_axis(np.concatenate([X, ghost], axis=3), np.where(live, nx, 0)[:, :, None, :], 3)
        ln = np.add.reduce(np.abs(X - Xn), axis=2)
        far = live & (ln > HI); split = far & (np.add.accumulate(far.astype(np.int64), axis=2) <= CAP)
        own = live & (nx < V); j = np.where(own, nx, 0)
        merge = own & even & (j % 2 == 1) & (ln < LO) & (np.take_along_axis(ln, j, 2) <= HI)
        new = np.where(merge, np.take_along_axis(nx, j, 2), nx)
        for r in range(N):
            for g in range(8):
                i = np.flatnonzero(split[r, g]); f = np.flatnonzero(~live[r, g])[:i.size]
                X[r, g][:, f] = (X[r, g][:, i] + Xn[r, g][:, i]) >> 1
                new[r, g, f] = nx[r, g, i]; new[r, g, i] = f
                new[r, g, j[r, g][merge[r, g]]] = -1
        nx = new; live = nx >= 0
        Xn = np.take_along_axis(np.concatenate([X, ghost], axis=3), np.where(live, nx, 0)[:, :, None, :], 3)
        X = X + np.where(live[:, :, None, :], np.clip(Xn - X, -1, 1), 0)
    X = np.where((nx >= 0)[:, :, None, :], X, 0)
    return {"yx": X.reshape(N, 128, V).astype(np.float32).astype(BF), "yn": np.stack([gtable(a) for a in nx]).astype(np.float32)}

@@ -1,0 +1,509 @@
+from concourse.bass import DstId, RemoteDMATransfer
+from concourse.mybir import AluOpType, ActivationFunctionType
+
+V, H, L, CAP, RO = 3072, 1536, 96, 320, 3
+SHIFTS = (1, 3)
+GO = 3712
+XW = GO + 2 * L
+ZW = GO + H
+KWW = 3168
+bf, f32, i32, u16 = "bfloat16", "float32", "int32", "uint16"
+
+SB = {
+    "xr": (V, bf), "X0": (XW, bf), "X1": (XW, bf), "X2": (XW, bf), "X3": (XW, bf), "Y": (V, bf), "XB": (V, bf), "thr": (192, f32),
+    "D": (ZW, bf), "NW": (ZW, bf), "DE": (H, bf), "A": (V, bf), "AJ": (H, bf), "C": (V, bf), "Q": (H, bf),
+    "DW": (GO, f32), "KI0": (KWW, f32), "KI1": (KWW, f32), "KF0": (KWW, f32), "KF1": (KWW, f32),
+    "kI": (640, bf), "kF": (640, bf), "WI": (192, f32), "WF": (192, f32), "SI": (208, bf), "SF": (208, bf),
+    "DI": (320, bf), "DF": (320, bf), "uI": (8, f32), "uF": (8, f32), "vI": (8, f32), "vF": (8, f32),
+    "cI": (8, u16), "cF": (8, u16), "PH": (40, f32), "J0": (40, f32), "J1": (40, f32), "PM": (40, f32), "ifo": (40, u16),
+    "tot": (8, f32), "far": (192, bf), "FR": (192, bf), "rk": (192, f32), "dd": (96, bf),
+    "sh": (96, f32), "okj": (96, f32), "m1": (96, f32), "m2": (96, f32), "m3": (96, f32), "moff": (96, u16),
+    "soff": (192, u16), "s": (192, f32), "ab": (96, f32), "cc": (96, bf), "dj": (96, f32),
+    "yy": (320, f32), "hh": (320, bf), "e1": (320, bf), "em": (320, bf), "si": (320, bf),
+    "XV": (640, bf), "NV": (640, bf), "S0": (192, bf), "S1": (192, bf), "S2": (192, bf),
+    "ni": (192, i32), "hi": (12, i32), "h0": (12, u16), "h1": (12, u16), "h2": (12, i32),
+    "t0": (192, i32), "t1": (192, i32), "t2": (192, f32), "t3": (192, f32), "t4": (192, f32), "t5": (192, f32),
+    "t6": (192, f32), "fn": (192, f32), "rh": (192, bf), "rl": (192, bf), "yo": (192, u16), "ynb": (192, f32),
+    "iu": (144, bf), "M0": (144, bf), "pi": (8, i32), "col": (24, f32), "E": (16, f32), "Tm": (144, bf), "Tf": (144, f32),
+    "U": (16 * 144, bf), "Bm": (128, bf), "Tri": (128, bf), "Im": (128, bf), "Ni": (128, bf), "N4": (128, bf), "I4": (128, bf),
+    "A0": (128, bf), "A1": (128, bf), "w0": (128, bf), "w1": (128, bf), "w2": (128, bf), "w3": (128, bf), "w4": (144, bf),
+    "w5": (128, bf), "Pt": (272, f32), "T3": (272, f32), "c16": (192, bf), "c128": (192, bf), "phi": (192, f32),
+    "base": (96, f32), "k2": (96, f32), "nn": (40, f32), "jn": (40, f32), "ca": (16, bf), "inc": (960, f32),
+}
+SCRATCH = {k: ("sbuf", [128, n], d) for k, (n, d) in SB.items()}
+for _b in range(8):
+    SCRATCH["P%d" % _b] = ("psum", [128, 512], f32)
+NDMA = 44
+SEMAPHORES = ["cv", "ca", "cp", "cg", "sent", "arr0", "arr1", "arr2"] + ["d%d" % i for i in range(NDMA)]
+ALU, ACT = AluOpType, ActivationFunctionType
+MAGIC = 12582912.0
+O = {"odd": 1, "nwv": 3, "co": "va", "ce": "vvv", "xc": "aaaaaa", "hd": "v", "ajc": 512, "dwc": 256}
+GA, SC, HOP, PE, TT = 1.55, 3.8, 110.0, 0.5, 2.0
+CUT = ((H, 2304), (2304, V), (0, 768), (768, 1280), (1280, H))
+ORDER = "240D030M0G0K000L0J0I020E25010F0N0O1C2N0P0Q1L0S0R150W1T1S0T042S1M1R16202W0H1N2U1V2T1E1W2X2V300Y1D2Z1Q050U102Y0X31112C2O1H090V0C0Z121732233637380B1F3C391A3D331828341Y1O0635263E1P3F0A145D1Z3O3S213P3Q3T3U1X3G1B4D4X3R4V3V4Y51442A3K454Z46534W4C27073H292F485513473L644E4F1I525056226B543B2E57632P583M1J5E5F4G3I5H5A4H5G5I2D2G493A4I1G594J5J5K1K4M4K3J2J6C195Y5B5C2H2I4A5L5N5M4P4N5O2M3N5P5Q6J4O4Q5Z5R5S604B4R405T611U4S3W5U4L6K4T5V5W62653X3Y4U41675X66426L7K3Z6D6M68696A436N6F6E6G6O6P6R6H6Q6S776I086V6W7578796T6U6X6Y9T74767A7B7L7C7071732K7R7D8F7M7N7O7P7Q7E7F8G9M6Z8D8E8H728J8N8I8K7S7T8L7V7U7H8V7G8O7I8M7W9L8P7J8W8Y9U8S7X7Y7Z8Z8R8X8Q9091808192849G829395948TA1859787868896988U9H999I9A898A9B9C9J9K839NA22L9O8B9D9E8CAO9PB29F9V9RA39WAP9QAQA49SA5ARA6A99XB9A7AA9Z9YA8A0ADABAMACAN2BAEAFB3AGAIB4B5B6ASATAHB7AVBVBWAKALAUAWAXAYBXBYAJB8BZC1C3C0BABBBDC2B0C5C6C8D3C9CBAZC4C7BCCACCBECFCYCDCECZD0D1BFD2BGBHCGCHD7BIBJBMD4E62RE7CICJBKBLD8DBBNCKCNCLBODFB1CMBPE8D5CPCOBQBRDJE9CQD6CRCSDDCTEDCUD9DADKDZBSBTCVCWEPEQERCXEABUDLE02QEBDMDNDOE1E2DYDXDGDPDQDEECDRE3DHDIDCDSDTEEE4DVEFDUDWESETF4EHE5EUEGEJEIEKELF7F5EMFDENFCEOEVF3F9FFFAEWFGF8FBF6FJFHF2FIEXEYFEF0EZF1"
+
+
+def R(n, lo=0, hi=None, st=1):
+    return (n, lo, SB[n][0] if hi is None else hi, st)
+
+
+def cnt(r):
+    return (r[2] - r[1] + r[3] - 1) // r[3]
+
+
+def two(r):
+    return r[0] in SB and SB[r[0]][1] in (bf, u16)
+
+
+def build(g, T, topo, core, rank):
+    ops = []
+
+    def ap(r):
+        if r[3] == 1:
+            return T[r[0]][:, r[1]:r[2]]
+        return T[r[0]][:, r[1]:r[2]:r[3]]
+
+    def add(q, cost, rd, wr, fn, kind="c", lat=0.0, after=()):
+        ops.append([q, float(cost), lat, list(rd), list(wr), fn, kind, list(after)])
+        return len(ops) - 1
+
+    def sc(x):
+        return ap(x) if isinstance(x, tuple) else x
+
+    def side(x):
+        return ap(x[0]).indirect(ap(x[1])) if isinstance(x, list) else ap(x)
+
+    def regs(*xs):
+        out = []
+        for x in xs:
+            if isinstance(x, list):
+                out += x
+            elif isinstance(x, tuple):
+                out.append(x)
+        return out
+
+    def vcost(o, a, f):
+        if isinstance(o, list):
+            return 60 + SC * 16 * cnt(o[1])
+        if isinstance(a, list):
+            return 60 + GA * 16 * cnt(a[1])
+        return 60 + max(64, f * cnt(o))
+
+    def wr(o):
+        return [o[0]] if isinstance(o, list) else [o]
+
+    def rd(o):
+        return [o[1]] if isinstance(o, list) else []
+
+    def ts(o, a, s1, op0, s2=None, op1=None):
+        def fn():
+            if op1 is None:
+                return g.vector.tensor_scalar(ap(o), ap(a), sc(s1), None, op0)
+            return g.vector.tensor_scalar(ap(o), ap(a), sc(s1), sc(s2), op0, op1)
+        return add("v", vcost(o, a, 0.5 if two(o) and two(a) else 1), regs(a, s1, s2), [o], fn)
+
+    def tt(o, a, b, op):
+        f = TT if isinstance(a, list) or (a[0] in SB and b[0] in SB) else 1
+        return add("v", vcost(o, a, f), regs(a, b), [o], lambda: g.vector.tensor_tensor(ap(o), side(a), ap(b), op))
+
+    def cp(o, a):
+        f = 0.5 if not isinstance(o, list) and not isinstance(a, list) and two(o) and two(a) else 1
+        return add("v", vcost(o, a, f), regs(a) + rd(o), wr(o), lambda: g.vector.tensor_copy(side(o), side(a)))
+
+    def ms(o, val):
+        return add("v", vcost(o, o, 0.5 if two(o) else 1), [], [o], lambda: g.vector.memset(ap(o), val))
+
+    def scan(o, a, b, op0, op1):
+        return add("v", vcost(o, a, 0.5 if two(o) and two(a) and two(b) else 1), [a, b], [o],
+                   lambda: g.vector.tensor_tensor_scan(ap(o), ap(a), ap(b), 0.0, op0, op1))
+
+    def act(o, a, func, bias=None, scale=None):
+        def fn():
+            kw = {}
+            if bias is not None:
+                kw["bias"] = sc(bias)
+            if scale is not None:
+                kw["scale"] = sc(scale)
+            return g.scalar.activation(side(o), side(a), func, **kw)
+        return add("a", 30 + vcost(o, a, 1), regs(a, bias, scale) + rd(o), wr(o), fn)
+
+    def copy(q, o, a):
+        return cp(o, a) if q == "v" else act(o, a, ACT.Copy)
+
+    def mm(lst):
+        def fn():
+            ins = None
+            for i, (o, l, r) in enumerate(lst):
+                ins = g.tensor.matmul(ap(o), ap(l), ap(r), i == 0, i == len(lst) - 1)
+            return ins
+        c = sum(max(64, cnt(r)) * (4 if SB[r[0]][1] == f32 else 1) for o, l, r in lst) * PE + 60
+        return add("p", c, [x[1] for x in lst] + [x[2] for x in lst], [lst[0][0]], fn)
+
+    def iota(o, pat, base, cm, after=()):
+        def fn():
+            if SB[o[0]][1] == i32:
+                return g.iota(ap(o), pat, base, cm)
+            return g.iota(ap(o), pat, base, cm, allow_small_or_imprecise_dtypes=True)
+        return add("g", 160 + 2 * cnt(o), [], [o], fn, after=after)
+
+    def dma(q, o, a, lat, acc=False, after=()):
+        def fn():
+            x, y = ap(o) if isinstance(o, tuple) else o(), ap(a) if isinstance(a, tuple) else a()
+            if acc:
+                return g.dma_start(x, y, accum_op=ALU.add)
+            return {"s": g.sync, "a": g.scalar}[q].dma_start(x, y)
+        return add(q, 1200 if q == "g" else 80, regs(a) + (regs(o) if acc else []), regs(o), fn, "dma", lat, after)
+
+    def P(b, lo, hi, st=1):
+        return ("P%d" % b, lo, hi, st)
+
+    def C(j):
+        return R("col", j, j + 1)
+
+    def sel(p, n="Tm"):
+        return R(n, 15 - p, 143 - p)
+
+    def send(r):
+        trs = []
+        for b, s in enumerate(SHIFTS):
+            dst = T.cores[(rank - s) % len(T.cores)]
+            rid, pid = topo.addr(dst, core)
+            en = topo.engines(core, dst)
+            k = len(en) // 2
+            trs.append((rid, pid, sum(1 << e for e in en[b * k:(b + 1) * k]), k))
+
+        def fn():
+            return g.remote_dma_fused(
+                [RemoteDMATransfer(dst_ids=[DstId(rid=t[0], pnc=t[1])], dma_engine_mask=t[2], remote_sem=T.sem["arr%d" % r],
+                                   src=ap(R("S%d" % r, b * L, (b + 1) * L)), dst=ap(R("X%d" % r, GO + b * L, GO + (b + 1) * L)))
+                 for b, t in enumerate(trs)], local_sem=T.sem.sent)
+        n = trs[0][3] + trs[1][3]
+        return add("g", 600, [R("S%d" % r)], [R("X%d" % r, GO, XW)], fn, ("arr%d" % r, n), 4500.0 if r == 0 else 3000.0)
+
+    dma("a", R("hi"), lambda: T.head[:], 2400.0)
+    for k in range(2):
+        dma("s", R("xr", k * H, (k + 1) * H), lambda k=k: T.x[:, k * H:(k + 1) * H], 3800.0 + 1200 * k)
+    dma("a", R("ni"), lambda: T.nxt[:], 2600.0)
+    cp(R("h0"), R("hi"))
+    cp(R("S0"), [R("xr"), R("h0")])
+    s0 = send(0)
+    ts(R("h2"), R("hi"), 1, ALU.arith_shift_right)
+    cp(R("h1"), R("h2"))
+    for k in range(2):
+        cp(R("X0", k * 768, (k + 1) * 768), R("xr", k * H, (k + 1) * H, 2))
+        act(R("X0", H + k * 768, H + (k + 1) * 768), R("xr", k * H + 1, (k + 1) * H, 2), ACT.Copy)
+
+    iota(R("pi", 0, 1), [[0, 1]], 0, 1)
+    iota(R("iu"), [[1, 144]], 0, 0)
+    iota(R("c16"), [[16, 192]], 0, 0)
+    iota(R("c128"), [[0, 2], [128, 96]], 128 * 129, 0)
+    iota(R("nn"), [[0, 2], [16, 20]], 0, 0)
+    for j, m in ((1, 112), (2, 15), (3, 7), (4, 1), (5, 14), (6, 8)):
+        ts(R("pi", j, j + 1), R("pi", 0, 1), m, ALU.bitwise_and)
+    cp(R("col", 0, 7), R("pi", 0, 7))
+    ts(R("M0"), R("iu"), C(1), ALU.subtract)
+    ts(R("E"), R("iu", 0, 16), C(2), ALU.is_equal)
+    ts(C(7), C(5), 0.5, ALU.mult, 8.0, ALU.add)
+    ts(C(8), C(4), -1.0, ALU.mult, 1.0, ALU.add)
+    ts(R("Pt", 0, 136), R("M0", 0, 136), C(7), ALU.is_equal, C(8), ALU.mult)
+    ts(R("Pt", 136, 272), R("M0", 0, 136), C(7), ALU.is_equal, C(4), ALU.mult)
+    ts(R("Tm"), R("M0"), 15.0, ALU.is_equal)
+    ts(R("Im"), R("M0", 0, 128), C(2), ALU.is_equal)
+    act(R("Ni"), R("Im"), ACT.Identity, scale=-1.0)
+    act(R("N4"), R("Im"), ACT.Identity, scale=-4096.0)
+    act(R("I4"), R("Im"), ACT.Identity, scale=4096.0)
+    ts(R("w0"), R("M0", 0, 128), 15.0, ALU.is_le)
+    ts(R("w1"), R("M0", 0, 128), 0.0, ALU.is_ge)
+    ts(R("w2"), R("M0", 0, 128), C(2), ALU.is_ge)
+    tt(R("Bm"), R("w0"), R("w1"), ALU.mult)
+    tt(R("Tri"), R("w0"), R("w2"), ALU.mult)
+    act(R("phi"), R("c16"), ACT.Identity, bias=C(2))
+    act(R("base"), R("phi", 0, 96), ACT.Identity, bias=float(GO - H))
+    act(R("k2"), R("phi", 0, 96), ACT.Identity, bias=float(GO))
+    act(R("nn"), R("nn"), ACT.Identity, bias=C(2))
+    act(R("jn"), R("phi", 0, 40), ACT.Identity, bias=float(V))
+    ms(R("ca"), 0.0)
+    ts(R("ca", 7, 13), R("c16", 0, 6), -1.0 / 4096, ALU.mult)
+    act(C(9), C(2), ACT.Identity, bias=float(V))
+    act(C(10), R("E", 1, 2), ACT.Identity, scale=-2048.0)
+    act(C(11), R("E", 15, 16), ACT.Identity, scale=16.0)
+    act(C(12), R("E", 15, 16), ACT.Identity, bias=1.0, scale=-16.0)
+    ts(R("A0"), R("M0", 0, 128), 0.0, ALU.is_equal, float(H), ALU.mult)
+    ts(R("w3"), R("M0", 0, 128), 1.0, ALU.is_equal, C(11), ALU.mult)
+    ts(R("w5"), R("M0", 0, 128), 2.0, ALU.is_equal, C(12), ALU.mult)
+    tt(R("w3"), R("w3"), R("w5"), ALU.add)
+    tt(R("A1"), R("w3"), R("A0"), ALU.subtract)
+    ts(R("w4"), R("M0"), 4.0, ALU.is_equal)
+    for p in range(16):
+        act(R("U", 144 * p, 144 * p + 129), R("w4", 0, 129), ACT.Identity, scale=R("E", p, p + 1))
+    ms(R("SI"), 0.0)
+    ms(R("SF"), 0.0)
+    ms(R("D", V, GO), 0.0)
+    for lo in range(GO, ZW, 512):
+        dma("s", R("D", lo, lo + 512), R("D", V, V + 512), 2500.0)
+    for k in range(4):
+        dma("s", R("X%d" % k, V, GO), R("D", V, GO), 2500.0)
+    dma("s", R("X3", GO, XW), R("D", V, V + 2 * L), 2500.0)
+    dma("s", R("NW", V, ZW), R("D", V, ZW), 3500.0)
+    ms(R("inc", 0, 320), 1.0 / 128)
+    ms(R("KF0", 0, 320), 0.0)
+    for n in ("KF1", "KI0", "KI1"):
+        dma("s", R(n, 0, 320), R("KF0", 0, 320), 2500.0)
+    iota(R("DW", 0, H), [[0, H]], 0, 0, after=[s0])
+    for r in range(1, RO):
+        act(R("inc", 320 * r, 320 * r + 320), R("inc", 0, 320), ACT.Identity, scale=2.0 ** r)
+    ts(R("Tf"), R("M0"), 15.0, ALU.is_equal)
+    act(C(13), C(3), ACT.Identity, bias=1.0, scale=2.0)
+    act(C(14), C(6), ACT.Identity, scale=0.125)
+    act(C(15), C(6), ACT.Identity, bias=1.0, scale=-0.125)
+    ts(R("T3", 0, 129), R("M0", 0, 129), C(13), ALU.is_equal, C(15), ALU.mult)
+    ts(R("T3", 136, 265), R("M0", 0, 129), C(13), ALU.is_equal, C(14), ALU.mult)
+
+    ts(R("t0"), R("ni"), float(V), ALU.min, 0.0, ALU.max)
+    ts(R("t1"), R("t0"), 1, ALU.bitwise_and)
+    ts(R("t2"), R("t0"), 0.5, ALU.mult)
+    ts(R("t3"), R("t1"), H - 0.5, ALU.mult)
+    ts(R("t4"), R("ni"), float(V), ALU.is_ge, float(GO - H), ALU.mult)
+    ts(R("t5"), R("ni"), float(V), ALU.subtract, 0.0, ALU.max)
+    ts(R("fn"), R("ni"), 0.0, ALU.is_lt)
+
+    def perm(bank, srcs):
+        for b in range(2):
+            mm([(P(bank, 96 * b, 96 * b + 96), R("Pt", 136 * b + 8 - 8 * h, 136 * b + 136 - 8 * h), R(s, h, 192, 2))
+                for s in srcs for h in range(2)])
+    tt(R("t2"), R("t2"), R("t3"), ALU.add)
+    tt(R("t4"), R("t4"), R("t5"), ALU.add)
+    perm(7, ["t2", "t4"])
+    perm(4, ["fn"])
+    cp(R("FR"), P(4, 0, 192))
+
+    def pointers(pl, n=96):
+        ts(R("soff", 96, 192), P(7 if n == 192 else 3, 96, 192), pl, ALU.add)
+        ts(R("soff", 0, 96), P(7, 0, 96), pl, ALU.add)
+        act(R("s", 0, n), P(7, 0, n), ACT.Identity, bias=pl)
+        act(R("ab"), R("s", 0, 96), ACT.Abs, bias=-(H + V - 1) / 2.0)
+        tt(R("dj"), R("s", 0, 96), R("k2"), ALU.subtract)
+        ts(R("cc"), R("ab"), 768.0, ALU.is_lt)
+    pointers(0.0, 192)
+    tt(R("t0"), R("s"), R("phi"), ALU.subtract)
+    ts(R("t1"), R("t0"), 31, ALU.bitwise_and)
+    cp(R("rl"), R("t1"))
+    tt(R("rh"), R("t0"), R("t1"), ALU.subtract)
+    for p in range(16):
+        bk, o = (0, 1, 2, 6)[(p // 2) % 4], 192 * (p % 2)
+        mm([(P(bk, o, o + 192), R("U", 144 * p + 1, 144 * p + 129), R("rh")), (P(bk, o, o + 192), R("U", 144 * p, 144 * p + 128), R("rl"))])
+        copy("v" if p < O["nwv"] else "a", R("NW", p, V, 16), P(bk, o, o + 192))
+
+    def nth(n, a, r):
+        S, z = "S" + n, float(2 ** r)
+        a0, a1, a2 = R(a, 0, 96), R(a, 96, 192), R(S, 112, 208)
+        scan(R(S, 1, 97), a0, a1, ALU.add, ALU.add)
+        tt(a2, a0, a1, ALU.add)
+        k, d, o = (5, 6, 0) if n == "I" else (2, 7, 192)
+        mm([(P(k, 384, 397), R("Im"), R("ca", 0, 13))] + [(P(k, 384, 397), sel(p), R(S, p, 208, 16)) for p in range(16)])
+        if n == "I":
+            mm([(P(k, 400, 401), R("Bm"), R(S, 96, 97))])
+        mm([(P(k, 0, 192), R("Ni"), R("c128")), (P(k, 0, 96), R("Tri"), a2), (P(k, 0, 96), R("Ni"), a1), (P(k, 96, 192), R("Tri"), a2)])
+        if n == "F":
+            mm([(P(k, 192, 288), R("Bm"), R(S, 0, 96)), (P(k, 192, 288), R("Tri"), a2), (P(k, 192, 288), R("Ni"), a1), (P(k, 192, 288), R("I4"), a0)])
+            mm([(P(k, 288, 384), R("Bm"), R(S, 0, 96)), (P(k, 288, 384), R("Tri"), a2), (P(k, 288, 384), R("I4"), a1)])
+        ts(R("u" + n, 0, 6), P(k, 391, 397), -4096.0, ALU.mult, C(9), ALU.add)
+        tt(R("v" + n, 0, 6), R("u" + n, 0, 6), P(k, 384, 390), ALU.max)
+        if n == "I":
+            ts(R("tot", 0, 1), P(k, 400, 401), float(CAP), ALU.min)
+        act(R("W" + n), P(k, 0, 192), ACT.Identity, bias=z * (0.5 / 128 - 0.5), scale=-z / 128)
+        if n == "F":
+            act(R("rk"), P(k, 192, 384), ACT.Copy)
+        cp(R("c" + n, 0, 6), R("v" + n, 0, 6))
+        for b in range(2):
+            K = "K%s%d" % (n, b)
+            act([R(K), R("c" + n, 0, 6)], R("W" + n, 96 * b, 96 * b + 96), ACT.Silu)
+            scan(R("k" + n, 320 * b, 320 * b + 320), R("inc", 320 * r, 320 * r + 320), R(K, 0, 320), ALU.add, ALU.max)
+        mm([(P(d, o, o + 320), R("A0"), R("k" + n, 0, 320)), (P(d, o, o + 320), R("A1"), R("k" + n, 320, 640))])
+        act(R("D" + n), P(d, o, o + 320), ACT.Identity, bias=C(10), scale=1 / z)
+        mm([(P(k, 420, 440), sel(p), R("D" + n, p, 320, 16)) for p in range(16)])
+        if n == "I":
+            ts(R("PH", 0, 20), P(k, 420, 440), float(V - 1), ALU.min)
+        else:
+            act(R("PH", 20, 40), P(k, 420, 440), ACT.Copy)
+
+    for r in range(RO):
+        X, Xn, last = "X%d" % r, "X%d" % (r + 1), r == RO - 1
+        nth("F", "FR", r)
+        for lo, hi in CUT:
+            own = R("XB", lo, hi) if r else R("xr", 2 * (lo % H) + lo // H, 2 * (lo % H + hi - lo), 2)
+            tt(R("D", lo, hi), [R(X), R("soff", lo // 16, hi // 16)], own, ALU.subtract)
+            act(R("A", lo, hi), R("D", lo, hi), ACT.Abs)
+        for lo, hi in ((96, 192), (0, 80), (80, 96)):
+            o = P(3, lo, hi)
+            mm([(o, sel(p), R("A", 16 * lo + p, 16 * hi, 16)) for p in range(16)])
+        for lo in range(0, H, O["ajc"]):
+            hi = lo + O["ajc"]
+            act(R("AJ", lo, hi), [R("D", 0, XW), R("soff", lo // 16, hi // 16)], ACT.Abs)
+        for lo, hi in ((0, 64), (64, 96)):
+            o = P(4, lo, hi)
+            mm([(o, R("N4"), R("cc", lo, hi))] + [(o, sel(p), R("AJ", 16 * lo + p, 16 * hi, 16)) for p in range(16)])
+        act(R("thr"), R("FR"), ACT.Identity, bias=440.5, scale=8192.0)
+        tt(R("far"), P(3, 0, 192), R("thr"), ALU.is_gt)
+        ts(R("sh"), P(3, 0, 96), 239.5, ALU.is_lt)
+        nth("I", "far", r)
+        tt(R("m1"), R("sh"), R("dj"), ALU.mult)
+        ts(R("okj"), P(4, 0, 96), 440.5 - 4096, ALU.is_lt)
+        tt(R("m2"), R("m1"), R("okj"), ALU.mult)
+        tt(R("m3"), R("m2"), R("base"), ALU.add)
+        cp(R("moff"), R("m3"))
+        for k, lo in enumerate((H, 2304)):
+            if O["co"][k] == "v":
+                ts(R("C", lo, lo + 768), R("D", lo, lo + 768), 1.0, ALU.min, -1.0, ALU.max)
+            else:
+                act(R("C", lo, lo + 768), R("D", lo, lo + 768), ACT.Sign)
+        for k in range(3):
+            lo, hi = 512 * k, 512 * k + 512
+            tt(R("DE", lo, hi), [R("D", H, ZW), R("moff", lo // 16, hi // 16)], R("D", lo, hi), ALU.add)
+            if O["ce"][k] == "v":
+                ts(R("C", lo, hi), R("DE", lo, hi), 1.0, ALU.min, -1.0, ALU.max)
+            else:
+                act(R("C", lo, hi), R("DE", lo, hi), ACT.Sign)
+        if O["odd"]:
+            dma("s", R(Xn, H, V), R(X, H, V), 4000.0)
+            dma("g", R(Xn, H, V), R("C", H, V), 5500.0, acc=True)
+        for i, k in enumerate((0, 1, 2) if O["odd"] else (3, 4, 5, 0, 1, 2)):
+            lo, hi = 512 * k, 512 * k + 512
+            mm([(P(i % 2, 0, 512), R("Im"), R(X, lo, hi)), (P(i % 2, 0, 512), R("Im"), R("C", lo, hi))])
+            copy(O["xc"][k], R(Xn, lo, hi), P(i % 2, 0, 512))
+        ts(R("J0"), R("nn"), R("tot", 0, 1), ALU.is_ge, 8192.0, ALU.mult)
+        tt(R("J1"), R("J0"), R("jn"), ALU.min)
+        tt(R("PM"), R("PH"), R("J1"), ALU.max)
+        cp(R("ifo"), R("PM"))
+        oi, of = R("ifo", 0, 20), R("ifo", 20, 40)
+        act(R("yy"), [R("D", 0, GO), oi], ACT.Identity, bias=-0.25, scale=0.5)
+        ts(R("hh"), R("yy"), MAGIC, ALU.add, MAGIC, ALU.subtract)
+        ts(R("si"), R("hh"), 1.0, ALU.min, -1.0, ALU.max)
+        tt(R("XV", 0, 320), [R(X, 0, GO), oi], R("si"), ALU.add)
+        act(R("em"), R("yy"), ACT.Abs, bias=0.25)
+        ts(R("e1"), R("em"), 0.5, ALU.is_equal)
+        mm([(P(6, 0, 320), R("Im"), R(n, 0, 320)) for n in ("XV", "hh", "e1")])
+        act(R("XV", 320, 640), P(6, 0, 320), ACT.Copy)
+        cp([R(Xn, 0, GO), oi], R("XV", 0, 320))
+        if not last:
+            copy(O["hd"], R("S%d" % (r + 1)), [R(Xn, 0, H), R("h1")])
+            send(r + 1)
+        cp([R(Xn, 0, GO), of], R("XV", 320, 640))
+        for k, (lo, hi) in enumerate(() if last else CUT):
+            dma("s", R("XB", lo, hi), R(Xn, lo, hi), 3000.0 + 700 * k)
+        for lo in (0, 512, 1024):
+            act(R("Q", lo, lo + 512), [R("NW", H, ZW), R("moff", lo // 16, lo // 16 + 32)], ACT.Copy)
+        mm([(P(5, 0, 320), R("Im"), R("DF")), (P(5, 0, 320), R("Ni"), R("DI"))])
+        act(R("NV", 0, 320), P(5, 0, 320), ACT.Copy)
+        tt(R("NV", 320, 640), [R("NW", 0, GO), oi], R("NV", 0, 320), ALU.subtract)
+        cp([R("NW", 0, GO), R("ifo")], R("NV"))
+        for b in (1, 0):
+            o = P(7 - 4 * b, 96 * b, 96 * b + 96)
+            mm([(o, R("Im"), R("c16", 96 * b, 96 * b + 96))] + [(o, sel(p), R("Q", p, H, 16)) for p in range(16) if b == 0]
+               + [(o, sel(p), R("NW", H * b + p, H * b + H, 16)) for p in range(16)])
+        if not last:
+            pointers(C(2))
+            dma("g", R("NW", 0, H), R("Q"), 5000.0, acc=True)
+        for lo in range(0, H, O["dwc"]):
+            act([R("DW"), R("moff", lo // 16, (lo + O["dwc"]) // 16)], R("inc", 320 * r, 320 * r + O["dwc"]), ACT.Silu)
+        mm([(P(4, 96, 192), sel(p, "Tf"), R("DW", p, H, 16)) for p in range(16)])
+        ts(R("FR"), R("rk"), 4096.0, ALU.subtract, R("tot", 0, 1), ALU.is_gt)
+        ts(R("dd"), P(4, 96, 192), 6.0 * 2 ** r / 128, ALU.is_gt)
+        tt(R("FR", 96, 192), R("FR", 96, 192), R("dd"), ALU.add)
+
+    act(R("s", 0, 96), P(7, 0, 96), ACT.Identity, bias=C(2))
+    act(R("s", 96, 192), P(3, 96, 192), ACT.Identity, bias=C(2))
+    ts(R("t2"), R("s"), float(H), ALU.is_ge, -(V - 1.0), ALU.mult)
+    act(R("t3"), R("s"), ACT.Identity, bias=1.0, scale=2.0)
+    ts(R("t4"), R("s"), float(GO), ALU.is_lt, 8192.0, ALU.mult)
+    act(R("t5"), R("s"), ACT.Identity, bias=float(V - GO + 1))
+    tt(R("t2"), R("t2"), R("t3"), ALU.add)
+    tt(R("t4"), R("t4"), R("t5"), ALU.add)
+    tt(R("t2"), R("t2"), R("t4"), ALU.min)
+    for b in range(2):
+        lo, hi = 96 * b, 96 * b + 96
+        act(R("t6", lo, hi), R("FR", lo, hi), ACT.Identity, scale=float(GO))
+        tt(R("fn", lo, hi), R("t6", lo, hi), R("phi", lo, hi), ALU.max)
+        cp(R("yo", lo, hi), R("fn", lo, hi))
+    act(R("t3"), R("FR"), ACT.Identity, bias=1.0, scale=-1.0)
+    tt(R("t5"), R("t2"), R("t3"), ALU.mult)
+    for h in range(2):
+        mm([(P(3, 96 * h, 96 * h + 96), R("T3", 136 * h + 1 - b, 136 * h + 129 - b), R("t5", 96 * b, 96 * b + 96)) for b in range(2)])
+    for h in range(2):
+        ts(R("ynb", h, 192, 2), P(3, 96 * h, 96 * h + 96), -1.0, ALU.add)
+    dma("s", lambda: T.yn[:], R("ynb"), 2500.0)
+    NQ = 6
+    w = V // NQ
+    for b in range(2):
+        for k in range(NQ):
+            copy("va"[k % 2], R("Y", w * k + b, w * k + w, 2), [R("X3"), R("yo", 96 * b + w // 32 * k, 96 * b + w // 32 * (k + 1))])
+    for k in range(NQ):
+        dma("s", lambda k=k: T.yx[:, w * k:w * k + w], R("Y", w * k, w * k + w), 2600.0)
+    return ops
+
+
+def depend(ops):
+    acc, deps, last = {}, [], {}
+    for i, op in enumerate(ops):
+        d = set(op[7])
+        for rs, w in ((op[3], False), (op[4], True)):
+            for r in rs:
+                for j, x, w2 in acc.get(r[0], ()):
+                    if r[0] not in SB:
+                        if (w or w2 or ops[j][0] != op[0]) and not (op[0] == "p" and ops[j][0] == "p"):
+                            d.add(j)
+                    elif (w or w2) and x[1] < r[2] and r[1] < x[2] and not (x[3] == r[3] and (x[1] - r[1]) % r[3]):
+                        d.add(j)
+        for rs, w in ((op[3], False), (op[4], True)):
+            for r in rs:
+                acc.setdefault(r[0], []).append((i, r, w))
+        if op[0] == "p":
+            if op[4][0][0] in last:
+                d.add(last[op[4][0][0]])
+            last[op[4][0][0]] = i
+        d.discard(i)
+        deps.append(d)
+    return deps
+
+
+def rank_program(g, core, T, topo):
+    rank = T.rank_of(core)
+    if rank is None:
+        return
+    ops = build(g, T, topo, core, rank)
+    deps = depend(ops)
+    order = [int(ORDER[k:k + 2], 36) for k in range(0, len(ORDER), 2)] or list(range(len(ops)))
+    assert sorted(order) == list(range(len(ops)))
+    Q = {"v": g.vector, "a": g.scalar, "p": g.tensor, "g": g, "s": g.sync}
+    mark, total, seen, nd = {}, {}, {q: {} for q in Q}, 0
+    for i in order:
+        op = ops[i]
+        q, need = op[0], {}
+        for j in deps[i]:
+            if ops[j][0] == q and (q == "p" or j in op[7]):
+                continue
+            s, v = mark[j]
+            need[s] = max(need.get(s, 0), v)
+        for s in sorted(need):
+            if seen[q].get(s, 0) < need[s]:
+                Q[q].wait_ge(T.sem[s], need[s])
+                seen[q][s] = need[s]
+        ins = op[5]()
+        if op[6] == "c":
+            s = "c" + q
+            total[s] = total.get(s, 0) + 1
+            ins.then_inc(T.sem[s], 1)
+            mark[i] = (s, total[s])
+        elif op[6] == "dma":
+            s = "d%d" % nd
+            nd += 1
+            total[s] = 16
+            ins.then_inc(T.sem[s], 16)
+            mark[i] = (s, 16)
+        else:
+            mark[i] = op[6]
+            total[op[6][0]] = op[6][1]
+            total["sent"] = total.get("sent", 0) + op[6][1]
+    for s in sorted(total):
+        if seen["g"].get(s, 0) < total[s]:
+            g.wait_ge(T.sem[s], total[s])

@@ -10,37 +10,37 @@ KWW = 3168
 bf, f32, i32, u16 = "bfloat16", "float32", "int32", "uint16"
 
 SB = {
-    "xr": (V, bf), "X0": (XW, bf), "X1": (XW, bf), "X2": (XW, bf), "X3": (XW, bf), "Y": (V, bf), "XB": (V, bf), "thr": (192, f32),
-    "D": (ZW, bf), "NW": (ZW, bf), "DE": (H, bf), "A": (V, bf), "AJ": (H, bf), "C": (V, bf), "Q": (H, bf),
+    "xr": (V, bf), "X0": (XW, bf), "X1": (XW, bf), "X2": (XW, bf), "X3": (XW, bf), "Y": (V, bf), "XB": (V, bf), "DB": (H, bf),
+    "D": (ZW, bf), "NW": (ZW, bf), "DE": (H, bf), "A": (V, bf), "AJ": (H, bf), "C": (V, bf), "Q": (H, bf), "thr": (192, f32),
     "DW": (GO, f32), "KI0": (KWW, f32), "KI1": (KWW, f32), "KF0": (KWW, f32), "KF1": (KWW, f32),
     "kI": (640, bf), "kF": (640, bf), "WI": (192, f32), "WF": (192, f32), "SI": (208, bf), "SF": (208, bf),
-    "DI": (320, bf), "DF": (320, bf), "uI": (8, f32), "uF": (8, f32), "vI": (8, f32), "vF": (8, f32),
-    "cI": (8, u16), "cF": (8, u16), "PH": (40, f32), "J0": (40, f32), "J1": (40, f32), "PM": (40, f32), "ifo": (40, u16),
-    "tot": (8, f32), "far": (192, bf), "FR": (192, bf), "rk": (192, f32), "dd": (96, bf),
-    "sh": (96, f32), "okj": (96, f32), "m1": (96, f32), "m2": (96, f32), "m3": (96, f32), "moff": (96, u16),
+    "DD": (640, bf), "uI": (8, f32), "uF": (8, f32), "vI": (8, f32), "vF": (8, f32),
+    "cI": (8, u16), "cF": (8, u16), "J0": (40, bf), "PM": (40, f32), "ifo": (40, u16),
+    "tot": (8, f32), "far": (192, bf), "FR": (192, bf), "dd": (96, bf),
+    "sh": (96, bf), "okj": (96, f32), "m2": (96, f32), "m3": (96, f32), "moff": (96, u16),
     "soff": (192, u16), "s": (192, f32), "ab": (96, f32), "cc": (96, bf), "dj": (96, f32),
     "yy": (320, f32), "hh": (320, bf), "e1": (320, bf), "em": (320, bf), "si": (320, bf),
     "XV": (640, bf), "NV": (640, bf), "S0": (192, bf), "S1": (192, bf), "S2": (192, bf),
     "ni": (192, i32), "hi": (12, i32), "h0": (12, u16), "h1": (12, u16), "h2": (12, i32),
     "t0": (192, i32), "t1": (192, i32), "t2": (192, f32), "t3": (192, f32), "t4": (192, f32), "t5": (192, f32),
     "t6": (192, f32), "fn": (192, f32), "rh": (192, bf), "rl": (192, bf), "yo": (192, u16), "ynb": (192, f32),
-    "iu": (144, bf), "M0": (144, bf), "pi": (8, i32), "col": (24, f32), "E": (16, f32), "Tm": (144, bf), "Tf": (144, f32),
+    "iu": (144, bf), "M0": (144, bf), "pi": (8, i32), "col": (24, f32), "E": (16, f32), "Tm": (144, bf),
     "U": (16 * 144, bf), "Bm": (128, bf), "Tri": (128, bf), "Im": (128, bf), "Ni": (128, bf), "N4": (128, bf), "I4": (128, bf),
-    "A0": (128, bf), "A1": (128, bf), "w0": (128, bf), "w1": (128, bf), "w2": (128, bf), "w3": (128, bf), "w4": (144, bf),
+    "A0": (128, bf), "A1": (128, bf), "w0": (128, bf), "w1": (128, bf), "w3": (128, bf), "w4": (144, bf),
     "w5": (128, bf), "Pt": (272, f32), "T3": (272, f32), "c16": (192, bf), "c128": (192, bf), "phi": (192, f32),
-    "base": (96, f32), "k2": (96, f32), "nn": (40, f32), "jn": (40, f32), "ca": (16, bf), "inc": (960, f32),
+    "base": (96, f32), "nn": (40, f32), "jn": (40, f32), "ca": (16, bf), "inc": (960, f32),
 }
 SCRATCH = {k: ("sbuf", [128, n], d) for k, (n, d) in SB.items()}
 for _b in range(8):
     SCRATCH["P%d" % _b] = ("psum", [128, 512], f32)
-NDMA = 44
+NDMA = 48
 SEMAPHORES = ["cv", "ca", "cp", "cg", "sent", "arr0", "arr1", "arr2"] + ["d%d" % i for i in range(NDMA)]
 ALU, ACT = AluOpType, ActivationFunctionType
 MAGIC = 12582912.0
-O = {"odd": 1, "nwv": 3, "co": "va", "ce": "vvv", "xc": "aaaaaa", "hd": "v", "ajc": 512, "dwc": 256}
 GA, SC, HOP, PE, TT = 1.55, 3.8, 110.0, 0.5, 2.0
 CUT = ((H, 2304), (2304, V), (0, 768), (768, 1280), (1280, H))
-ORDER = "240D030M0G0K000L0J0I020E25010F0N0O1C2N0P0Q1L0S0R150W1T1S0T042S1M1R16202W0H1N2U1V2T1E1W2X2V300Y1D2Z1Q050U102Y0X31112C2O1H090V0C0Z121732233637380B1F3C391A3D331828341Y1O0635263E1P3F0A145D1Z3O3S213P3Q3T3U1X3G1B4D4X3R4V3V4Y51442A3K454Z46534W4C27073H292F485513473L644E4F1I525056226B543B2E57632P583M1J5E5F4G3I5H5A4H5G5I2D2G493A4I1G594J5J5K1K4M4K3J2J6C195Y5B5C2H2I4A5L5N5M4P4N5O2M3N5P5Q6J4O4Q5Z5R5S604B4R405T611U4S3W5U4L6K4T5V5W62653X3Y4U41675X66426L7K3Z6D6M68696A436N6F6E6G6O6P6R6H6Q6S776I086V6W7578796T6U6X6Y9T74767A7B7L7C7071732K7R7D8F7M7N7O7P7Q7E7F8G9M6Z8D8E8H728J8N8I8K7S7T8L7V7U7H8V7G8O7I8M7W9L8P7J8W8Y9U8S7X7Y7Z8Z8R8X8Q9091808192849G829395948TA1859787868896988U9H999I9A898A9B9C9J9K839NA22L9O8B9D9E8CAO9PB29F9V9RA39WAP9QAQA49SA5ARA6A99XB9A7AA9Z9YA8A0ADABAMACAN2BAEAFB3AGAIB4B5B6ASATAHB7AVBVBWAKALAUAWAXAYBXBYAJB8BZC1C3C0BABBBDC2B0C5C6C8D3C9CBAZC4C7BCCACCBECFCYCDCECZD0D1BFD2BGBHCGCHD7BIBJBMD4E62RE7CICJBKBLD8DBBNCKCNCLBODFB1CMBPE8D5CPCOBQBRDJE9CQD6CRCSDDCTEDCUD9DADKDZBSBTCVCWEPEQERCXEABUDLE02QEBDMDNDOE1E2DYDXDGDPDQDEECDRE3DHDIDCDSDTEEE4DVEFDUDWESETF4EHE5EUEGEJEIEKELF7F5EMFDENFCEOEVF3F9FFFAEWFGF8FBF6FJFHF2FIEXEYFEF0EZF1"
+ONV = ",33,47,115,117,152,154,163,212,213,217,219,223,225,239,241,261,283,310,332,333,335,337,339,345,354,361,381,410,430,440,442,444,447,452,453,455,457,472,474,511,521,522,527,528,529,534,"
+ORDER = "0D0N0I0M02030K0J0L0O0E180P000R0F1J0S0Q0H160T14041R1N2N2R2V2S2T1W1M2U2W2M2Y2Z0U1P2O1A1930311D0W2X1E320V222P201K1G3515010905061C360Y331S113710251V1Q0B3B0G2K3C0X3D261O17213E0C12344B4C2L0A5A3N0Z3O243F3G3P3J382C4R3R1Z1L1X4T3Q3K3S43443H134V4X4Z233T3A3I453U462H3V4S5X1F4U5W1U3L4D4E1Y4F2G39274W4Y2E504748512F3M4G541H52535B4H3Z5C5D282I4I07494J4K55574A561I085E5F5G5H2D4L58595J5I4N4M5L4O1T5K3W5S1B40415T6C5U5M4P5N5V5O2B5P645Y423X3Y4Q7C622J5Q5R606D5Z6E616F636X66676G706H6869716K6I6L6A6J656B6M7D6Y7E726O6N6P6R6S6Z737K7476756T7F7G7H6Q838485868D6V6W7I7J6U77788789888A8E8B8C8F7L9G7M797B7N7O8I8M7A2Q8G8N8O8J7P7Q997R8P7S8H7T7U7V7W8Q7Z7X988R8S8T8V8U8K8L808X9O7Y818W9094918Y958Z92829396979CAA9PAO9A9Q9B9R9I9S9DAC9E9J9T9KAB9F9U9W9M9N9L9V9XADA99HA0A19Y9ZAEA329APAQA4AFAGAWAIA2A5ARASAHATA6BFBGBHA7BIBPAJA8BJBLAKBKBMAUAVBQBNBOCKALBRAXAYBSAZB0B1BTB2B3AMBYBZBVC0BWCLB4BUBXC1C2C3B5B6ANCSB8CGB7B9BBCHCICJBAC4C5C7C6BCC9C8DVCCCACDBDBEDNDOCBCQCED0CFDPDQDRDSD1CMCODGDED2CND3DHDIE7D4D8E8D5CUCTDFCPD6DTCRE9CWD7D9DJDKCVDACXCYCZDUDMDB2ADWDCDXEADDEBDLDYDZE0ECE2E1E4E3ELE5E6EQEDEEEVESEMEYEKEPF1ENETEWEOEUF0EREZEFEGEXEHEIEJ"
 
 
 def R(n, lo=0, hi=None, st=1):
@@ -98,9 +98,9 @@ def build(g, T, topo, core, rank):
     def ts(o, a, s1, op0, s2=None, op1=None):
         def fn():
             if op1 is None:
-                return g.vector.tensor_scalar(ap(o), ap(a), sc(s1), None, op0)
-            return g.vector.tensor_scalar(ap(o), ap(a), sc(s1), sc(s2), op0, op1)
-        return add("v", vcost(o, a, 0.5 if two(o) and two(a) else 1), regs(a, s1, s2), [o], fn)
+                return g.vector.tensor_scalar(ap(o), side(a), sc(s1), None, op0)
+            return g.vector.tensor_scalar(ap(o), side(a), sc(s1), sc(s2), op0, op1)
+        return add("v", vcost(o, a, 0.5 if two(o) and isinstance(a, tuple) and two(a) else 1), regs(a, s1, s2), [o], fn)
 
     def tt(o, a, b, op):
         f = TT if isinstance(a, list) or (a[0] in SB and b[0] in SB) else 1
@@ -127,8 +127,17 @@ def build(g, T, topo, core, rank):
             return g.scalar.activation(side(o), side(a), func, **kw)
         return add("a", 30 + vcost(o, a, 1), regs(a, bias, scale) + rd(o), wr(o), fn)
 
-    def copy(q, o, a):
-        return cp(o, a) if q == "v" else act(o, a, ACT.Copy)
+    def either():
+        return "v" if ",%d," % len(ops) in ONV else "a"
+
+    def copy(o, a, func=ACT.Copy):
+        return cp(o, a) if either() == "v" else act(o, a, func)
+
+    def lin(o, a, bias=0.0, scale=1.0):
+        return ts(o, a, scale, ALU.mult, bias, ALU.add) if either() == "v" else act(o, a, ACT.Identity, bias=bias, scale=scale)
+
+    def clip(o, a):
+        return ts(o, a, 1.0, ALU.min, -1.0, ALU.max) if either() == "v" else act(o, a, ACT.Sign)
 
     def mm(lst):
         def fn():
@@ -146,12 +155,15 @@ def build(g, T, topo, core, rank):
             return g.iota(ap(o), pat, base, cm, allow_small_or_imprecise_dtypes=True)
         return add("g", 160 + 2 * cnt(o), [], [o], fn, after=after)
 
+    def pick(o, a, base, op):
+        return add("g", 205 + 2 * cnt(o), [a], [o], lambda: g.affine_select(ap(o), ap(a), [[-1, cnt(o)]], op, 0.0, base, 1))
+
     def dma(q, o, a, lat, acc=False, after=()):
         def fn():
             x, y = ap(o) if isinstance(o, tuple) else o(), ap(a) if isinstance(a, tuple) else a()
             if acc:
                 return g.dma_start(x, y, accum_op=ALU.add)
-            return {"s": g.sync, "a": g.scalar}[q].dma_start(x, y)
+            return {"s": g.sync, "a": g.scalar, "g": g}[q].dma_start(x, y)
         return add(q, 1200 if q == "g" else 80, regs(a) + (regs(o) if acc else []), regs(o), fn, "dma", lat, after)
 
     def P(b, lo, hi, st=1):
@@ -185,13 +197,13 @@ def build(g, T, topo, core, rank):
         dma("s", R("xr", k * H, (k + 1) * H), lambda k=k: T.x[:, k * H:(k + 1) * H], 3800.0 + 1200 * k)
     dma("a", R("ni"), lambda: T.nxt[:], 2600.0)
     cp(R("h0"), R("hi"))
-    cp(R("S0"), [R("xr"), R("h0")])
+    g0 = [copy(R("S0"), [R("xr"), R("h0")])]
     s0 = send(0)
     ts(R("h2"), R("hi"), 1, ALU.arith_shift_right)
     cp(R("h1"), R("h2"))
     for k in range(2):
-        cp(R("X0", k * 768, (k + 1) * 768), R("xr", k * H, (k + 1) * H, 2))
-        act(R("X0", H + k * 768, H + (k + 1) * 768), R("xr", k * H + 1, (k + 1) * H, 2), ACT.Copy)
+        copy(R("X0", k * 768, (k + 1) * 768), R("xr", k * H, (k + 1) * H, 2))
+        copy(R("X0", H + k * 768, H + (k + 1) * 768), R("xr", k * H + 1, (k + 1) * H, 2))
 
     iota(R("pi", 0, 1), [[0, 1]], 0, 1)
     iota(R("iu"), [[1, 144]], 0, 0)
@@ -209,25 +221,23 @@ def build(g, T, topo, core, rank):
     ts(R("Pt", 136, 272), R("M0", 0, 136), C(7), ALU.is_equal, C(4), ALU.mult)
     ts(R("Tm"), R("M0"), 15.0, ALU.is_equal)
     ts(R("Im"), R("M0", 0, 128), C(2), ALU.is_equal)
-    act(R("Ni"), R("Im"), ACT.Identity, scale=-1.0)
-    act(R("N4"), R("Im"), ACT.Identity, scale=-4096.0)
-    act(R("I4"), R("Im"), ACT.Identity, scale=4096.0)
+    lin(R("Ni"), R("Im"), scale=-1.0)
+    lin(R("N4"), R("Im"), scale=-4096.0)
+    lin(R("I4"), R("Im"), scale=4096.0)
     ts(R("w0"), R("M0", 0, 128), 15.0, ALU.is_le)
     ts(R("w1"), R("M0", 0, 128), 0.0, ALU.is_ge)
-    ts(R("w2"), R("M0", 0, 128), C(2), ALU.is_ge)
     tt(R("Bm"), R("w0"), R("w1"), ALU.mult)
-    tt(R("Tri"), R("w0"), R("w2"), ALU.mult)
-    act(R("phi"), R("c16"), ACT.Identity, bias=C(2))
-    act(R("base"), R("phi", 0, 96), ACT.Identity, bias=float(GO - H))
-    act(R("k2"), R("phi", 0, 96), ACT.Identity, bias=float(GO))
-    act(R("nn"), R("nn"), ACT.Identity, bias=C(2))
-    act(R("jn"), R("phi", 0, 40), ACT.Identity, bias=float(V))
+    add("g", 461, [R("Bm")], [R("Tri")], lambda: g.affine_select(ap(R("Tri")), ap(R("Bm")), [[1, 128]], ALU.is_ge, 0.0, 0, -1))
+    lin(R("phi"), R("c16"), bias=C(2))
+    lin(R("base"), R("phi", 0, 96), bias=float(GO - H))
+    lin(R("nn"), R("nn"), bias=C(2))
+    lin(R("jn"), R("phi", 0, 40), bias=float(V))
     ms(R("ca"), 0.0)
     ts(R("ca", 7, 13), R("c16", 0, 6), -1.0 / 4096, ALU.mult)
-    act(C(9), C(2), ACT.Identity, bias=float(V))
-    act(C(10), R("E", 1, 2), ACT.Identity, scale=-2048.0)
-    act(C(11), R("E", 15, 16), ACT.Identity, scale=16.0)
-    act(C(12), R("E", 15, 16), ACT.Identity, bias=1.0, scale=-16.0)
+    lin(C(9), C(2), bias=float(V))
+    lin(C(10), R("E", 1, 2), scale=-2048.0)
+    lin(C(11), R("E", 15, 16), scale=16.0)
+    lin(C(12), R("E", 15, 16), bias=1.0, scale=-16.0)
     ts(R("A0"), R("M0", 0, 128), 0.0, ALU.is_equal, float(H), ALU.mult)
     ts(R("w3"), R("M0", 0, 128), 1.0, ALU.is_equal, C(11), ALU.mult)
     ts(R("w5"), R("M0", 0, 128), 2.0, ALU.is_equal, C(12), ALU.mult)
@@ -235,27 +245,27 @@ def build(g, T, topo, core, rank):
     tt(R("A1"), R("w3"), R("A0"), ALU.subtract)
     ts(R("w4"), R("M0"), 4.0, ALU.is_equal)
     for p in range(16):
-        act(R("U", 144 * p, 144 * p + 129), R("w4", 0, 129), ACT.Identity, scale=R("E", p, p + 1))
-    ms(R("SI"), 0.0)
-    ms(R("SF"), 0.0)
+        pick(R("U", 144 * p, 144 * p + 129), R("w4", 0, 129), 4 - p, ALU.is_equal)
+    iota(R("SF"), [[0, 208]], 0, 0)
+    dma("s", R("SI"), R("SF"), 2500.0, after=g0)
     ms(R("D", V, GO), 0.0)
     for lo in range(GO, ZW, 512):
-        dma("s", R("D", lo, lo + 512), R("D", V, V + 512), 2500.0)
+        dma("s", R("D", lo, lo + 512), R("D", V, V + 512), 3000.0, after=g0)
     for k in range(4):
-        dma("s", R("X%d" % k, V, GO), R("D", V, GO), 2500.0)
-    dma("s", R("X3", GO, XW), R("D", V, V + 2 * L), 2500.0)
-    dma("s", R("NW", V, ZW), R("D", V, ZW), 3500.0)
-    ms(R("inc", 0, 320), 1.0 / 128)
-    ms(R("KF0", 0, 320), 0.0)
+        dma("s", R("X%d" % k, V, GO), R("D", V, GO), 3000.0, after=g0 if k == 0 else [s0])
+    dma("s", R("X3", GO, XW), R("D", V, V + 2 * L), 2500.0, after=[s0])
+    dma("s", R("NW", V, ZW), R("D", V, ZW), 3500.0, after=[s0])
+    iota(R("KF0", 0, 320), [[0, 320]], 0, 0)
     for n in ("KF1", "KI0", "KI1"):
-        dma("s", R(n, 0, 320), R("KF0", 0, 320), 2500.0)
+        dma("s", R(n, 0, 320), R("KF0", 0, 320), 3000.0, after=g0)
     iota(R("DW", 0, H), [[0, H]], 0, 0, after=[s0])
-    for r in range(1, RO):
-        act(R("inc", 320 * r, 320 * r + 320), R("inc", 0, 320), ACT.Identity, scale=2.0 ** r)
-    ts(R("Tf"), R("M0"), 15.0, ALU.is_equal)
-    act(C(13), C(3), ACT.Identity, bias=1.0, scale=2.0)
-    act(C(14), C(6), ACT.Identity, scale=0.125)
-    act(C(15), C(6), ACT.Identity, bias=1.0, scale=-0.125)
+    for r in range(RO):
+        iota(R("inc", 320 * r, 320 * r + 320), [[0, 320]], 2 ** r, 0)
+    lin(C(16), C(2), bias=-(H + V - 1) / 2.0)
+    lin(C(17), C(2), bias=-float(H))
+    lin(C(13), C(3), bias=1.0, scale=2.0)
+    lin(C(14), C(6), scale=0.125)
+    lin(C(15), C(6), bias=1.0, scale=-0.125)
     ts(R("T3", 0, 129), R("M0", 0, 129), C(13), ALU.is_equal, C(15), ALU.mult)
     ts(R("T3", 136, 265), R("M0", 0, 129), C(13), ALU.is_equal, C(14), ALU.mult)
 
@@ -275,14 +285,15 @@ def build(g, T, topo, core, rank):
     tt(R("t4"), R("t4"), R("t5"), ALU.add)
     perm(7, ["t2", "t4"])
     perm(4, ["fn"])
-    cp(R("FR"), P(4, 0, 192))
+    copy(R("FR"), P(4, 0, 192))
 
     def pointers(pl, n=96):
         ts(R("soff", 96, 192), P(7 if n == 192 else 3, 96, 192), pl, ALU.add)
         ts(R("soff", 0, 96), P(7, 0, 96), pl, ALU.add)
-        act(R("s", 0, n), P(7, 0, n), ACT.Identity, bias=pl)
-        act(R("ab"), R("s", 0, 96), ACT.Abs, bias=-(H + V - 1) / 2.0)
-        tt(R("dj"), R("s", 0, 96), R("k2"), ALU.subtract)
+        if n == 192:
+            lin(R("s", 0, n), P(7, 0, n), bias=pl)
+        act(R("ab"), P(7, 0, 96), ACT.Abs, bias=-(H + V - 1) / 2.0 if n == 192 else C(16))
+        lin(R("dj"), P(7, 0, 96), bias=-float(H) if n == 192 else C(17))
         ts(R("cc"), R("ab"), 768.0, ALU.is_lt)
     pointers(0.0, 192)
     tt(R("t0"), R("s"), R("phi"), ALU.subtract)
@@ -292,7 +303,7 @@ def build(g, T, topo, core, rank):
     for p in range(16):
         bk, o = (0, 1, 2, 6)[(p // 2) % 4], 192 * (p % 2)
         mm([(P(bk, o, o + 192), R("U", 144 * p + 1, 144 * p + 129), R("rh")), (P(bk, o, o + 192), R("U", 144 * p, 144 * p + 128), R("rl"))])
-        copy("v" if p < O["nwv"] else "a", R("NW", p, V, 16), P(bk, o, o + 192))
+        copy(R("NW", p, V, 16), P(bk, o, o + 192))
 
     def nth(n, a, r):
         S, z = "S" + n, float(2 ** r)
@@ -311,21 +322,14 @@ def build(g, T, topo, core, rank):
         tt(R("v" + n, 0, 6), R("u" + n, 0, 6), P(k, 384, 390), ALU.max)
         if n == "I":
             ts(R("tot", 0, 1), P(k, 400, 401), float(CAP), ALU.min)
-        act(R("W" + n), P(k, 0, 192), ACT.Identity, bias=z * (0.5 / 128 - 0.5), scale=-z / 128)
-        if n == "F":
-            act(R("rk"), P(k, 192, 384), ACT.Copy)
+        lin(R("W" + n), P(k, 0, 192), bias=z * (0.5 - 64), scale=-z)
         cp(R("c" + n, 0, 6), R("v" + n, 0, 6))
         for b in range(2):
             K = "K%s%d" % (n, b)
-            act([R(K), R("c" + n, 0, 6)], R("W" + n, 96 * b, 96 * b + 96), ACT.Silu)
+            copy([R(K), R("c" + n, 0, 6)], R("W" + n, 96 * b, 96 * b + 96), ACT.Silu)
             scan(R("k" + n, 320 * b, 320 * b + 320), R("inc", 320 * r, 320 * r + 320), R(K, 0, 320), ALU.add, ALU.max)
         mm([(P(d, o, o + 320), R("A0"), R("k" + n, 0, 320)), (P(d, o, o + 320), R("A1"), R("k" + n, 320, 640))])
-        act(R("D" + n), P(d, o, o + 320), ACT.Identity, bias=C(10), scale=1 / z)
-        mm([(P(k, 420, 440), sel(p), R("D" + n, p, 320, 16)) for p in range(16)])
-        if n == "I":
-            ts(R("PH", 0, 20), P(k, 420, 440), float(V - 1), ALU.min)
-        else:
-            act(R("PH", 20, 40), P(k, 420, 440), ACT.Copy)
+        lin(R("DD", 320 * (n == "F"), 320 * (n == "F") + 320), P(d, o, o + 320), bias=C(10), scale=1 / (128 * z))
 
     for r in range(RO):
         X, Xn, last = "X%d" % r, "X%d" % (r + 1), r == RO - 1
@@ -337,64 +341,55 @@ def build(g, T, topo, core, rank):
         for lo, hi in ((96, 192), (0, 80), (80, 96)):
             o = P(3, lo, hi)
             mm([(o, sel(p), R("A", 16 * lo + p, 16 * hi, 16)) for p in range(16)])
-        for lo in range(0, H, O["ajc"]):
-            hi = lo + O["ajc"]
-            act(R("AJ", lo, hi), [R("D", 0, XW), R("soff", lo // 16, hi // 16)], ACT.Abs)
+        for lo in range(0, H, 512):
+            act(R("AJ", lo, lo + 512), [R("D", 0, XW), R("soff", lo // 16, lo // 16 + 32)], ACT.Abs)
+        ts(R("sh"), P(3, 0, 96), 239.5, ALU.is_gt)
         for lo, hi in ((0, 64), (64, 96)):
             o = P(4, lo, hi)
-            mm([(o, R("N4"), R("cc", lo, hi))] + [(o, sel(p), R("AJ", 16 * lo + p, 16 * hi, 16)) for p in range(16)])
-        act(R("thr"), R("FR"), ACT.Identity, bias=440.5, scale=8192.0)
+            mm([(o, R("N4"), R("cc", lo, hi)), (o, R("I4"), R("sh", lo, hi))] + [(o, sel(p), R("AJ", 16 * lo + p, 16 * hi, 16)) for p in range(16)])
+        lin(R("thr"), R("FR"), bias=440.5, scale=8192.0)
         tt(R("far"), P(3, 0, 192), R("thr"), ALU.is_gt)
-        ts(R("sh"), P(3, 0, 96), 239.5, ALU.is_lt)
         nth("I", "far", r)
-        tt(R("m1"), R("sh"), R("dj"), ALU.mult)
-        ts(R("okj"), P(4, 0, 96), 440.5 - 4096, ALU.is_lt)
-        tt(R("m2"), R("m1"), R("okj"), ALU.mult)
-        tt(R("m3"), R("m2"), R("base"), ALU.add)
+        ts(R("okj"), P(4, 0, 96), 440.5 - 4096, ALU.is_gt, 8192.0, ALU.mult)
+        tt(R("m2"), R("okj"), R("dj"), ALU.add)
+        tt(R("m3"), R("m2"), R("base"), ALU.min)
         cp(R("moff"), R("m3"))
-        for k, lo in enumerate((H, 2304)):
-            if O["co"][k] == "v":
-                ts(R("C", lo, lo + 768), R("D", lo, lo + 768), 1.0, ALU.min, -1.0, ALU.max)
-            else:
-                act(R("C", lo, lo + 768), R("D", lo, lo + 768), ACT.Sign)
+        for lo in (H, 2304):
+            clip(R("C", lo, lo + 768), R("D", lo, lo + 768))
         for k in range(3):
             lo, hi = 512 * k, 512 * k + 512
             tt(R("DE", lo, hi), [R("D", H, ZW), R("moff", lo // 16, hi // 16)], R("D", lo, hi), ALU.add)
-            if O["ce"][k] == "v":
-                ts(R("C", lo, hi), R("DE", lo, hi), 1.0, ALU.min, -1.0, ALU.max)
-            else:
-                act(R("C", lo, hi), R("DE", lo, hi), ACT.Sign)
-        if O["odd"]:
-            dma("s", R(Xn, H, V), R(X, H, V), 4000.0)
-            dma("g", R(Xn, H, V), R("C", H, V), 5500.0, acc=True)
-        for i, k in enumerate((0, 1, 2) if O["odd"] else (3, 4, 5, 0, 1, 2)):
+            clip(R("C", lo, hi), R("DE", lo, hi))
+        dma("s", R(Xn, H, V), R(X, H, V), 4000.0)
+        dma("g", R(Xn, H, V), R("C", H, V), 5500.0, acc=True)
+        for k in range(3):
             lo, hi = 512 * k, 512 * k + 512
-            mm([(P(i % 2, 0, 512), R("Im"), R(X, lo, hi)), (P(i % 2, 0, 512), R("Im"), R("C", lo, hi))])
-            copy(O["xc"][k], R(Xn, lo, hi), P(i % 2, 0, 512))
-        ts(R("J0"), R("nn"), R("tot", 0, 1), ALU.is_ge, 8192.0, ALU.mult)
-        tt(R("J1"), R("J0"), R("jn"), ALU.min)
-        tt(R("PM"), R("PH"), R("J1"), ALU.max)
+            mm([(P(k % 2, 0, 512), R("Im"), R(X, lo, hi)), (P(k % 2, 0, 512), R("Im"), R("C", lo, hi))])
+            copy(R(Xn, lo, hi), P(k % 2, 0, 512))
+        ts(R("J0"), R("nn"), R("tot", 0, 1), ALU.is_ge, 65536.0, ALU.mult)
+        mm([(P(5, 420, 460), R("Im"), R("J0"))] + [(P(5, 420, 460), sel(p), R("DD", p, 640, 16)) for p in range(16)])
+        tt(R("PM"), P(5, 420, 460), R("jn"), ALU.min)
         cp(R("ifo"), R("PM"))
         oi, of = R("ifo", 0, 20), R("ifo", 20, 40)
-        act(R("yy"), [R("D", 0, GO), oi], ACT.Identity, bias=-0.25, scale=0.5)
+        lin(R("yy"), [R("D", 0, GO), oi], bias=-0.25, scale=0.5)
         ts(R("hh"), R("yy"), MAGIC, ALU.add, MAGIC, ALU.subtract)
-        ts(R("si"), R("hh"), 1.0, ALU.min, -1.0, ALU.max)
+        clip(R("si"), R("hh"))
         tt(R("XV", 0, 320), [R(X, 0, GO), oi], R("si"), ALU.add)
         act(R("em"), R("yy"), ACT.Abs, bias=0.25)
         ts(R("e1"), R("em"), 0.5, ALU.is_equal)
         mm([(P(6, 0, 320), R("Im"), R(n, 0, 320)) for n in ("XV", "hh", "e1")])
-        act(R("XV", 320, 640), P(6, 0, 320), ACT.Copy)
+        copy(R("XV", 320, 640), P(6, 0, 320))
         cp([R(Xn, 0, GO), oi], R("XV", 0, 320))
         if not last:
-            copy(O["hd"], R("S%d" % (r + 1)), [R(Xn, 0, H), R("h1")])
+            copy(R("S%d" % (r + 1)), [R(Xn, 0, H), R("h1")])
             send(r + 1)
         cp([R(Xn, 0, GO), of], R("XV", 320, 640))
         for k, (lo, hi) in enumerate(() if last else CUT):
             dma("s", R("XB", lo, hi), R(Xn, lo, hi), 3000.0 + 700 * k)
         for lo in (0, 512, 1024):
-            act(R("Q", lo, lo + 512), [R("NW", H, ZW), R("moff", lo // 16, lo // 16 + 32)], ACT.Copy)
-        mm([(P(5, 0, 320), R("Im"), R("DF")), (P(5, 0, 320), R("Ni"), R("DI"))])
-        act(R("NV", 0, 320), P(5, 0, 320), ACT.Copy)
+            copy(R("Q", lo, lo + 512), [R("NW", H, ZW), R("moff", lo // 16, lo // 16 + 32)])
+        mm([(P(5, 0, 320), R("Im"), R("DD", 320, 640)), (P(5, 0, 320), R("Ni"), R("DD", 0, 320))])
+        copy(R("NV", 0, 320), P(5, 0, 320))
         tt(R("NV", 320, 640), [R("NW", 0, GO), oi], R("NV", 0, 320), ALU.subtract)
         cp([R("NW", 0, GO), R("ifo")], R("NV"))
         for b in (1, 0):
@@ -404,39 +399,40 @@ def build(g, T, topo, core, rank):
         if not last:
             pointers(C(2))
             dma("g", R("NW", 0, H), R("Q"), 5000.0, acc=True)
-        for lo in range(0, H, O["dwc"]):
-            act([R("DW"), R("moff", lo // 16, (lo + O["dwc"]) // 16)], R("inc", 320 * r, 320 * r + O["dwc"]), ACT.Silu)
-        mm([(P(4, 96, 192), sel(p, "Tf"), R("DW", p, H, 16)) for p in range(16)])
-        ts(R("FR"), R("rk"), 4096.0, ALU.subtract, R("tot", 0, 1), ALU.is_gt)
-        ts(R("dd"), P(4, 96, 192), 6.0 * 2 ** r / 128, ALU.is_gt)
+        for lo in range(0, H, 256):
+            act([R("DW"), R("moff", lo // 16, lo // 16 + 16)], R("inc", 320 * r, 320 * r + 256), ACT.Silu)
+        dma("g", R("DB"), R("DW", 0, H), 3500.0)
+        mm([(P(4, 96, 192), sel(p), R("DB", p, H, 16)) for p in range(16)])
+        ts(R("FR"), P(2, 192, 384), 4096.0, ALU.subtract, R("tot", 0, 1), ALU.is_gt)
+        ts(R("dd"), P(4, 96, 192), (8.0, 20.0, 45.0)[r], ALU.is_gt)
         tt(R("FR", 96, 192), R("FR", 96, 192), R("dd"), ALU.add)
 
-    act(R("s", 0, 96), P(7, 0, 96), ACT.Identity, bias=C(2))
-    act(R("s", 96, 192), P(3, 96, 192), ACT.Identity, bias=C(2))
+    lin(R("s", 0, 96), P(7, 0, 96), bias=C(2))
+    lin(R("s", 96, 192), P(3, 96, 192), bias=C(2))
     ts(R("t2"), R("s"), float(H), ALU.is_ge, -(V - 1.0), ALU.mult)
-    act(R("t3"), R("s"), ACT.Identity, bias=1.0, scale=2.0)
+    lin(R("t3"), R("s"), bias=1.0, scale=2.0)
     ts(R("t4"), R("s"), float(GO), ALU.is_lt, 8192.0, ALU.mult)
-    act(R("t5"), R("s"), ACT.Identity, bias=float(V - GO + 1))
+    lin(R("t5"), R("s"), bias=float(V - GO + 1))
     tt(R("t2"), R("t2"), R("t3"), ALU.add)
     tt(R("t4"), R("t4"), R("t5"), ALU.add)
     tt(R("t2"), R("t2"), R("t4"), ALU.min)
     for b in range(2):
         lo, hi = 96 * b, 96 * b + 96
-        act(R("t6", lo, hi), R("FR", lo, hi), ACT.Identity, scale=float(GO))
+        lin(R("t6", lo, hi), R("FR", lo, hi), scale=float(GO))
         tt(R("fn", lo, hi), R("t6", lo, hi), R("phi", lo, hi), ALU.max)
         cp(R("yo", lo, hi), R("fn", lo, hi))
-    act(R("t3"), R("FR"), ACT.Identity, bias=1.0, scale=-1.0)
+    lin(R("t3"), R("FR"), bias=1.0, scale=-1.0)
     tt(R("t5"), R("t2"), R("t3"), ALU.mult)
     for h in range(2):
         mm([(P(3, 96 * h, 96 * h + 96), R("T3", 136 * h + 1 - b, 136 * h + 129 - b), R("t5", 96 * b, 96 * b + 96)) for b in range(2)])
     for h in range(2):
-        ts(R("ynb", h, 192, 2), P(3, 96 * h, 96 * h + 96), -1.0, ALU.add)
+        lin(R("ynb", h, 192, 2), P(3, 96 * h, 96 * h + 96), bias=-1.0)
     dma("s", lambda: T.yn[:], R("ynb"), 2500.0)
     NQ = 6
     w = V // NQ
     for b in range(2):
         for k in range(NQ):
-            copy("va"[k % 2], R("Y", w * k + b, w * k + w, 2), [R("X3"), R("yo", 96 * b + w // 32 * k, 96 * b + w // 32 * (k + 1))])
+            copy(R("Y", w * k + b, w * k + w, 2), [R("X3"), R("yo", 96 * b + w // 32 * k, 96 * b + w // 32 * (k + 1))])
     for k in range(NQ):
         dma("s", lambda k=k: T.yx[:, w * k:w * k + w], R("Y", w * k, w * k + w), 2600.0)
     return ops
@@ -476,18 +472,18 @@ def rank_program(g, core, T, topo):
     assert sorted(order) == list(range(len(ops)))
     Q = {"v": g.vector, "a": g.scalar, "p": g.tensor, "g": g, "s": g.sync}
     mark, total, seen, nd = {}, {}, {q: {} for q in Q}, 0
+    at, knew, by = {i: k for k, i in enumerate(order)}, {}, {}
     for i in order:
         op = ops[i]
-        q, need = op[0], {}
-        for j in deps[i]:
-            if ops[j][0] == q and (q == "p" or j in op[7]):
-                continue
+        q = op[0]
+        for j in sorted(deps[i], key=lambda j: -at[j]):
             s, v = mark[j]
-            need[s] = max(need.get(s, 0), v)
-        for s in sorted(need):
-            if seen[q].get(s, 0) < need[s]:
-                Q[q].wait_ge(T.sem[s], need[s])
-                seen[q][s] = need[s]
+            if seen[q].get(s, 0) >= v or (ops[j][0] == q and (q == "p" or j in op[7])):
+                continue
+            Q[q].wait_ge(T.sem[s], v)
+            for x, y in list(knew[by[s, v]].items()) + [(s, v)]:
+                seen[q][x] = max(seen[q].get(x, 0), y)
+        knew[i] = dict(seen[q]) if op[6] in ("c", "dma") else {}
         ins = op[5]()
         if op[6] == "c":
             s = "c" + q
@@ -504,6 +500,7 @@ def rank_program(g, core, T, topo):
             mark[i] = op[6]
             total[op[6][0]] = op[6][1]
             total["sent"] = total.get("sent", 0) + op[6][1]
+        by[mark[i]] = i
     for s in sorted(total):
         if seen["g"].get(s, 0) < total[s]:
             g.wait_ge(T.sem[s], total[s])

@@ -3,44 +3,115 @@ from concourse.mybir import AluOpType, ActivationFunctionType
 
 V, H, L, CAP, RO = 3072, 1536, 96, 320, 3
 SHIFTS = (1, 3)
-GO = 3712
+OD = H + 16
+JK = OD + H
+GO = JK + 2 * CAP
 XW = GO + 2 * L
-ZW = GO + H
+WW = OD + 16
 KWW = 3168
+BIG = float(2 ** 20)
 bf, f32, i32, u16 = "bfloat16", "float32", "int32", "uint16"
 
 SB = {
-    "xr": (V, bf), "X0": (XW, bf), "X1": (XW, bf), "X2": (XW, bf), "X3": (XW, bf), "Y": (V, bf), "XB": (V, bf), "DB": (H, bf),
-    "D": (ZW, bf), "NW": (ZW, bf), "DE": (H, bf), "A": (V, bf), "AJ": (H, bf), "C": (V, bf), "Q": (H, bf), "thr": (192, f32),
-    "DW": (GO, f32), "KI0": (KWW, f32), "KI1": (KWW, f32), "KF0": (KWW, f32), "KF1": (KWW, f32),
+    "xr": (V + 16, bf), "X0": (XW, bf), "X1": (XW, bf), "X2": (XW, bf), "X3": (XW, bf), "Y": (V + 2 * CAP, bf), "XB": (JK, bf),
+    "D": (XW, bf), "NW": (GO, bf), "A": (JK, bf), "AJ": (H, bf), "C": (JK, bf), "Q": (H, bf), "W": (WW, bf), "Ut": (H, bf),
+    "KI0": (KWW, f32), "KI1": (KWW, f32), "KF0": (KWW, f32), "KF1": (KWW, f32),
     "kI": (640, bf), "kF": (640, bf), "WI": (192, f32), "WF": (192, f32), "SI": (208, bf), "SF": (208, bf),
     "DD": (640, bf), "uI": (8, f32), "uF": (8, f32), "vI": (8, f32), "vF": (8, f32),
-    "cI": (8, u16), "cF": (8, u16), "J0": (40, bf), "PM": (40, f32), "ifo": (40, u16),
-    "tot": (8, f32), "far": (192, bf), "FR": (192, bf), "dd": (96, bf),
-    "sh": (96, bf), "okj": (96, f32), "m2": (96, f32), "m3": (96, f32), "moff": (96, u16),
-    "soff": (192, u16), "s": (192, f32), "ab": (96, f32), "cc": (96, bf), "dj": (96, f32),
-    "yy": (320, f32), "hh": (320, bf), "e1": (320, bf), "em": (320, bf), "si": (320, bf),
+    "cI": (8, u16), "cF": (8, u16), "J0": (40, bf), "PM": (80, f32), "ifo": (80, u16),
+    "tot": (8, f32), "far": (192, bf), "FR": (192, bf), "dd": (96, bf), "sh": (96, bf), "m2": (96, f32), "moff": (96, u16),
+    "soff": (192, u16), "aoff": (96, u16), "dj": (96, f32), "HH": (272, f32), "rn": (96, f32), "df": (96, f32), "qa": (96, f32),
+    "zc": (96, f32), "c1": (192, bf), "c2": (192, bf), "e2": (320, bf), "yy": (320, f32), "hh": (320, bf), "e1": (320, bf), "em": (320, bf), "si": (320, bf), "G": (320, bf),
     "XV": (640, bf), "NV": (640, bf), "S0": (192, bf), "S1": (192, bf), "S2": (192, bf),
-    "ni": (192, i32), "hi": (12, i32), "h0": (12, u16), "h1": (12, u16), "h2": (12, i32),
-    "t0": (192, i32), "t1": (192, i32), "t2": (192, f32), "t3": (192, f32), "t4": (192, f32), "t5": (192, f32),
-    "t6": (192, f32), "fn": (192, f32), "rh": (192, bf), "rl": (192, bf), "yo": (192, u16), "ynb": (192, f32),
-    "iu": (144, bf), "M0": (144, bf), "pi": (8, i32), "col": (24, f32), "E": (16, f32), "Tm": (144, bf),
-    "U": (16 * 144, bf), "Bm": (128, bf), "Tri": (128, bf), "Im": (128, bf), "Ni": (128, bf), "N4": (128, bf), "I4": (128, bf),
-    "A0": (128, bf), "A1": (128, bf), "w0": (128, bf), "w1": (128, bf), "w3": (128, bf), "w4": (144, bf),
-    "w5": (128, bf), "Pt": (272, f32), "T3": (272, f32), "c16": (192, bf), "c128": (192, bf), "phi": (192, f32),
-    "base": (96, f32), "nn": (40, f32), "jn": (40, f32), "ca": (16, bf), "inc": (960, f32),
+    "ni": (192, i32), "hi": (12, i32), "h0": (12, u16), "h1": (12, u16),
+    "ti": (4 * 192, i32), "dg": (8 * 192, bf), "Z": (2 * 192, bf),
+    "t2": (192, f32), "t3": (192, f32), "t4": (192, f32), "t5": (192, f32), "yo": (96, u16), "ynb": (192, f32),
+    "iu": (144, bf), "M0": (144, bf), "pi": (8, i32), "col": (40, f32), "E": (16, f32), "Tm": (144, bf), "T2": (144, bf), "T5": (144, bf),
+    "Bm": (128, bf), "Tri": (128, bf), "Im": (144, bf), "Ni": (128, bf), "N4": (128, bf), "IB": (128, bf), "I32": (128, f32),
+    "A0": (128, bf), "ab": (128, bf), "w0": (128, bf), "w1": (128, bf), "w2": (3 * 128, bf), "on": (144, bf),
+    "Pb": (272, bf), "T3": (272, bf), "T4": (272, bf), "c16": (192, bf), "c128": (192, bf), "phn": (192, f32),
+    "nn": (40, f32), "jn": (80, f32), "ca": (16, bf), "inc": (960, f32),
+    "O6": (144, bf), "O7": (144, bf), "O8": (144, bf), "BP": (128, bf),
+    "M1": (128, bf), "M2": (128, bf), "pw": (96, f32), "bas": (192, bf), "RR": (96, f32),
 }
 SCRATCH = {k: ("sbuf", [128, n], d) for k, (n, d) in SB.items()}
-for _b in range(8):
+for _b in (0, 1, 2, 3, 4, 5, 7):
     SCRATCH["P%d" % _b] = ("psum", [128, 512], f32)
-NDMA = 48
+SCRATCH["P6"] = ("psum", [128, 1024], bf)
+NDMA = 56
 SEMAPHORES = ["cv", "ca", "cp", "cg", "sent", "arr0", "arr1", "arr2"] + ["d%d" % i for i in range(NDMA)]
 ALU, ACT = AluOpType, ActivationFunctionType
 MAGIC = 12582912.0
-GA, SC, HOP, PE, TT = 1.55, 3.8, 110.0, 0.5, 2.0
-CUT = ((H, 2304), (2304, V), (0, 768), (768, 1280), (1280, H))
-ONV = ",33,47,115,117,152,154,163,212,213,217,219,223,225,239,241,261,283,310,332,333,335,337,339,345,354,361,381,410,430,440,442,444,447,452,453,455,457,472,474,511,521,522,527,528,529,534,"
-ORDER = "0D0N0I0M02030K0J0L0O0E180P000R0F1J0S0Q0H160T14041R1N2N2R2V2S2T1W1M2U2W2M2Y2Z0U1P2O1A1930311D0W2X1E320V222P201K1G3515010905061C360Y331S113710251V1Q0B3B0G2K3C0X3D261O17213E0C12344B4C2L0A5A3N0Z3O243F3G3P3J382C4R3R1Z1L1X4T3Q3K3S43443H134V4X4Z233T3A3I453U462H3V4S5X1F4U5W1U3L4D4E1Y4F2G39274W4Y2E504748512F3M4G541H52535B4H3Z5C5D282I4I07494J4K55574A561I085E5F5G5H2D4L58595J5I4N4M5L4O1T5K3W5S1B40415T6C5U5M4P5N5V5O2B5P645Y423X3Y4Q7C622J5Q5R606D5Z6E616F636X66676G706H6869716K6I6L6A6J656B6M7D6Y7E726O6N6P6R6S6Z737K7476756T7F7G7H6Q838485868D6V6W7I7J6U77788789888A8E8B8C8F7L9G7M797B7N7O8I8M7A2Q8G8N8O8J7P7Q997R8P7S8H7T7U7V7W8Q7Z7X988R8S8T8V8U8K8L808X9O7Y818W9094918Y958Z92829396979CAA9PAO9A9Q9B9R9I9S9DAC9E9J9T9KAB9F9U9W9M9N9L9V9XADA99HA0A19Y9ZAEA329APAQA4AFAGAWAIA2A5ARASAHATA6BFBGBHA7BIBPAJA8BJBLAKBKBMAUAVBQBNBOCKALBRAXAYBSAZB0B1BTB2B3AMBYBZBVC0BWCLB4BUBXC1C2C3B5B6ANCSB8CGB7B9BBCHCICJBAC4C5C7C6BCC9C8DVCCCACDBDBEDNDOCBCQCED0CFDPDQDRDSD1CMCODGDED2CND3DHDIE7D4D8E8D5CUCTDFCPD6DTCRE9CWD7D9DJDKCVDACXCYCZDUDMDB2ADWDCDXEADDEBDLDYDZE0ECE2E1E4E3ELE5E6EQEDEEEVESEMEYEKEPF1ENETEWEOEUF0EREZEFEGEXEHEIEJ"
+MT = 440.5 * 4096 - BIG
+CUT = ((OD, OD + 768, "t"), (OD + 768, JK, "t"), (0, 768, "d"), (768, H, "d"))
+LEN = ((OD, JK), (0, 768), (768, H))
+NVA = False
+NQ = 4
+PLAN = {
+    "v": "sD.0 spw.0 spi.2 spi.4 spi.5 sxr.2 spi.3 spi.1 spi.6 sSI.0 scol.0 spw.2 scol.1 sti.0 sE.0 scol.18 sSF.0 sh0.0 sbas.6 sM0.0 sti.3 "
+         "sbas.4 sti.1 sdg.2 sPb.0 sIm.0 sdg.7 sti.2 sdg.4 sPb.1 sdg.6 sdg.3 sdg.5 scol.4 syo.0 spw.1 sbas.7 sD.1 sbas.2 sT3.1 sFR.0 sBm.0 "
+         "scol.19 sT3.0 sBP.0 sw0.0 sh1.0 sI32.0 sbas.5 sD.3 ssoff.1 spw.3 ssoff.0 sTm.0 0SF.0 saoff.0 0SF.1 scol.20 0D.4 0D.1 0D.0 snn.1 "
+         "sZ.0 scol.9 sjn.0 0uF.0 sN4.0 0WF.0 sA0.0 0vF.0 sNW.2 0cF.0 0C.1 sW.4 0C.0 0KF1.0 0far.0 sw1.0 0SI.1 0SI.0 0kF.1 sNW.3 0uI.0 "
+         "scol.22 0vI.0 0WI.0 0cI.0 0KF0.0 0KI0.0 0kF.0 0zc.0 0kI.0 0m2.0 0tot.0 0m2.1 0FR.0 0moff.0 0kI.1 0J0.0 0D.7 0D.6 0D.8 0C.3 0PM.0 "
+         "0C.4 0ifo.0 0C.2 0yy.0 0NV.1 0hh.0 0e2.0 0S1.0 0e1.0 0NW.0 0XV.0 0NW.1 0X1.6 0X1.7 0soff.1 0Ut.1 sw2.1 0soff.0 1D.0 1D.1 0HH.0 "
+         "0HH.1 0aoff.0 0rn.0 sT4.0 0df.0 scol.11 0dd.0 0FR.1 0dj.0 1SF.0 1SF.1 1far.0 sjn.1 1SI.0 1uF.0 1SI.1 1vF.0 1WF.0 1cF.0 sw2.2 "
+         "1KF0.0 1KF1.0 1uI.0 1kF.0 1vI.0 1zc.0 1kF.1 1cI.0 1m2.0 1tot.0 1m2.1 1J0.0 1moff.0 1kI.1 1kI.0 1D.7 1D.6 1FR.0 1D.8 1C.2 1PM.0 "
+         "1NV.0 1ifo.0 1C.4 1NV.1 1S2.0 1hh.0 1NW.0 1e1.0 1XV.0 1e2.0 1NW.1 1X2.6 1X2.7 1soff.1 2D.2 1soff.0 1aoff.0 2D.0 2D.1 1HH.0 1HH.1 "
+         "1rn.0 1df.0 1dj.0 2C.1 1dd.0 1FR.1 2C.0 2SF.0 2SF.1 2far.0 2SI.0 2uF.0 2SI.1 2vF.0 2cF.0 2KF0.0 2KF1.0 2kF.0 2vI.0 2kF.1 2cI.0 "
+         "2m2.0 2moff.0 2tot.0 2kI.1 2kI.0 2D.6 2Ut.0 2FR.0 2J0.0 2D.7 2Ut.1 2D.8 2PM.0 2ifo.0 2Ut.2 2NV.1 2NW.0 2HH.0 2HH.1 2NW.1 2rn.0 "
+         "2df.0 2hh.0 2dd.0 2PM.1 2FR.1 2e1.0 2XV.0 2yo.0 2ifo.1 2Y.6 2Y.4 2t3.0 2t4.0 2t5.0 2t2.0 2Y.7 2ynb.0 2ynb.1",
+    "a": "sni.0 shi.0 scol.13 scol.14 scol.2 scol.3 scol.16 scol.15 scol.12 scol.21 sbas.1 sS0.0 sX0.1 scol.5 sbas.3 scol.8 sNi.0 sab.0 "
+         "scol.6 sX0.2 sX0.6 sX0.5 sbas.0 sca.1 0D.2 sdj.0 sW.2 sW.3 0A.1 0A.0 sIB.0 0A.2 0A.3 sNW.4 0AJ.0 sNW.6 0sh.0 0AJ.1 0AJ.2 0KI1.0 "
+         "scol.7 sNW.5 0Q.0 0DD.0 0DD.1 0Q.1 sRR.3 sNW.7 0c1.0 0NV.0 0c2.0 0em.0 0X1.2 0si.0 0Q.2 0X1.3 0X1.4 scol.10 0XV.1 0Ut.0 sRR.2 "
+         "sRR.0 scol.17 sRR.1 sphn.1 1D.2 1D.4 0Ut.2 1A.0 1A.1 1A.2 0qa.0 1A.3 1AJ.1 1AJ.0 1sh.0 1AJ.2 1WI.0 1C.1 1C.0 1KI1.0 1KI0.0 1DD.0 "
+         "1Q.1 1Q.2 1DD.1 1Q.0 1C.3 1c1.0 1c2.0 1yy.0 1X2.2 1em.0 1si.0 1X2.4 1X2.3 1XV.1 1Ut.0 2D.4 1Ut.1 1Ut.2 2A.0 2A.1 2A.2 1qa.0 2A.3 "
+         "2AJ.0 2AJ.1 2WF.0 2AJ.2 2uI.0 2WI.0 2sh.0 2KI1.0 2KI0.0 2Q.0 2DD.0 2Q.1 2DD.1 2Q.2 2C.2 2NV.0 2C.4 2Y.0 2yy.0 2C.3 2qa.0 2em.0 "
+         "2si.0 2Y.1 2Y.2 2Y.3 2Y.5 2XV.1 2out.2",
+    "p": "sP4.0 sP4.1 sP4.2 sP7.0 sP5.0 sP3.0 sP0.0 sP1.0 sP3.1 0P2.0 0P7.0 sP0.1 sP1.1 0P3.0 sP1.2 0P3.1 0P3.2 sP1.3 sP0.2 0P5.0 0P1.0 "
+         "sP0.3 0P4.0 0P1.1 0P4.1 0P5.1 0P4.2 0P2.1 0P2.2 0P7.1 sP0.4 0P3.3 0P5.2 0P2.3 0P0.0 0P6.0 0P1.2 0P0.1 0P3.4 0P7.2 0P7.3 0P6.1 "
+         "0P4.3 0P5.3 0P6.2 0P4.4 0P4.5 0P4.6 1P3.0 1P3.1 1P3.2 1P7.0 1P2.0 1P1.0 1P5.0 1P4.0 1P1.1 1P4.1 1P4.2 1P5.1 1P7.1 1P2.1 1P3.3 "
+         "1P2.2 1P5.2 1P2.3 1P0.0 1P6.0 1P1.2 1P0.1 1P7.2 1P3.4 1P7.3 1P4.3 1P6.1 1P5.3 1P6.2 1P4.4 1P4.5 1P4.6 2P3.0 2P3.1 2P3.2 2P7.0 "
+         "2P2.0 2P1.0 2P5.0 2P4.0 2P4.1 2P4.2 2P2.1 2P5.1 2P2.2 2P7.1 2P6.0 2P3.3 2P6.1 2P4.3 2P5.2 2P2.3 2P6.2 2P4.4 2P0.0 2P4.5 2P5.3 "
+         "2P0.1 2P4.6 2P1.1 2P7.2 2P5.4 2P7.3 2P3.4 2P3.5 2P3.6",
+    "g": "spi.0 siu.0 sdg.0 sca.0 sdg.1 son.0 sc16.0 sW.0 sO8.0 sX0.0 sD.2 sc128.0 sO6.0 sX0.3 sTri.0 sO7.0 sW.1 sM2.0 snn.0 sM2.1 sKF0.0 "
+         "0D.3 0D.5 sinc.0 sNW.0 sM1.0 sT5.0 sM1.1 sM2.2 sw2.0 sM1.2 sM2.3 sM2.4 sM1.3 sM2.5 sT2.0 sM2.6 sM1.4 sM2.7 sM1.5 sM1.6 sM1.7 "
+         "sHH.0 sM1.8 sphn.0 sM1.9 sinc.1 sM1.10 0X1.1 0X1.5 sinc.2 sM2.8 sM2.9 sM1.11 sT5.1 sM2.10 sM2.11 1D.3 1D.5 0NW.2 1X2.1 1X2.5 "
+         "2D.3 2D.5 1NW.2 2X3.1",
+    "s": "sxr.0 sxr.1 sX0.4 sKI1.0 sNW.1 sKF1.0 sX1.0 0X1.0 sKI0.0 sW.5 sX3.0 0W.0 0XB.0 sX2.0 0XB.1 1X2.0 sX3.1 1XB.0 1XB.1 1W.0 2X3.0 "
+         "2out.1 2out.0",
+}
+OLD1 = {
+    "v": "sD.0 son.0 spi.6 spi.5 spi.2 spi.4 spi.1 spi.3 scol.0 spw.0 scol.5 sh0.0 sM0.0 sdg.4 scol.3 sti.0 sti.3 sti.2 sdg.7 sE.0 sPb.0 "
+         "sdg.2 sdg.6 sti.1 sdg.3 sIm.0 scol.19 sPb.1 sdg.5 sSI.0 sTm.0 sT3.1 sT3.0 spw.2 syo.0 sBm.0 sFR.0 sbas.4 sW.0 sX0.5 0SF.0 sBP.0 "
+         "ssoff.0 ssoff.1 0D.0 0D.1 0D.4 scol.9 sA0.0 sIB.0 0SF.1 sca.1 sNW.2 saoff.0 sdj.0 sw0.0 0C.1 0D.2 0WF.0 0D.3 sW.4 0uF.0 0C.0 "
+         "0vF.0 0cF.0 sNW.4 sw1.0 sW.1 spw.1 scol.20 sjn.0 0far.0 0SI.1 0SI.0 scol.6 sNW.3 0kF.1 0kF.0 0m2.0 0vI.0 0moff.0 0cI.0 0DE.2 "
+         "0kI.1 0tot.0 0kI.0 0FR.0 0J0.0 0DE.0 0DE.1 scol.22 spw.3 0PM.0 0C.4 0C.2 0ifo.0 sNW.7 0C.3 0NV.1 0hh.0 sh1.0 0NW.0 0e1.0 0XV.0 "
+         "0NW.1 0X1.5 0S1.0 0X1.7 0soff.0 sRR.2 0soff.1 sw2.1 sRR.1 0aoff.0 0HH.0 0HH.1 1D.0 1D.1 0rn.0 1D.4 0df.0 1D.2 1D.3 0dd.0 0FR.1 "
+         "1C.0 sjn.1 1SF.1 1SF.0 1far.0 1SI.0 1WF.0 1SI.1 scol.11 1uF.0 1vF.0 1cF.0 1KF1.0 1vI.0 1cI.0 1kF.1 1kF.0 1kI.0 1m2.0 1tot.0 "
+         "1moff.0 1kI.1 1J0.0 1DE.2 1DE.0 1DE.1 1PM.0 1C.2 1ifo.0 1C.3 1FR.0 1yy.0 1C.4 1hh.0 sw2.2 1si.0 1e1.0 1XV.0 1NV.1 1X2.5 1NW.0 "
+         "1X2.7 1NW.1 1Ut.2 1soff.0 1HH.0 1HH.1 2D.1 1soff.1 1rn.0 2D.0 1df.0 2D.2 2D.3 2D.4 1dd.0 1aoff.0 1FR.1 2SF.0 1dj.0 2SF.1 2far.0 "
+         "2WF.0 2SI.0 2uF.0 2SI.1 2vF.0 2cF.0 2uI.0 2vI.0 2kF.0 2cI.0 2tot.0 2kF.1 2kI.0 2m2.0 2kI.1 2moff.0 2FR.0 2J0.0 2DE.0 2DD.1 2DE.1 "
+         "2Ut.0 2DE.2 2PM.0 2ifo.0 2C.0 2NV.1 2C.2 2NW.0 2HH.0 2HH.1 2NW.1 2rn.0 2df.0 2hh.0 2PM.1 2dd.0 2FR.1 2yo.0 2e1.0 2Y.2 2XV.0 2Y.4 "
+         "2t3.0 2t4.0 2ifo.1 2t5.0 2Y.7 2ynb.0 2ynb.1",
+    "a": "sni.0 shi.0 scol.1 scol.15 scol.2 scol.16 sS0.0 scol.4 scol.12 sX0.1 sab.0 scol.8 sX0.2 sbas.7 scol.18 sNi.0 sbas.6 sX0.6 sbas.1 "
+         "scol.13 sN4.0 sbas.0 sbas.2 sbas.3 sbas.5 snn.1 sZ.0 scol.14 0A.0 sW.3 0A.1 0A.4 sW.2 0AJ.0 0AJ.1 0A.2 scol.21 0AJ.2 scol.10 "
+         "0A.3 0KF0.0 0KF1.0 0sh.0 sNW.6 scol.7 0uI.0 0WI.0 0KI1.0 0KI0.0 sNW.5 0DD.0 0Q.0 0DD.1 0Q.1 0Q.2 0NV.0 0yy.0 sT4.0 0em.0 0X1.2 "
+         "0si.0 0X1.3 0X1.4 sRR.0 sRR.3 0XV.1 0Ut.0 0Ut.1 0Ut.2 sI32.0 1A.0 0dj.0 1A.1 scol.17 1A.4 0qa.0 1A.2 1A.3 1AJ.1 1AJ.0 1AJ.2 "
+         "1WI.0 1uI.0 1sh.0 1KF0.0 1KI0.0 1KI1.0 1C.1 1DD.0 1Q.0 1DD.1 1Q.2 1Ut.0 1Q.1 sphn.1 1X2.2 1em.0 1NV.0 1X2.3 1X2.4 1XV.1 1S2.0 "
+         "1Ut.1 2A.1 2C.1 1qa.0 2A.0 2A.2 2A.3 2A.4 2AJ.0 2AJ.2 2AJ.1 2KF0.0 2KF1.0 2WI.0 2KI0.0 2sh.0 2KI1.0 2Q.0 2DD.0 2Q.1 2Q.2 2Ut.1 "
+         "2NV.0 2Ut.2 2C.3 2yy.0 2C.4 2Y.0 2qa.0 2em.0 2si.0 2Y.1 2Y.5 2Y.6 2Y.3 2XV.1 2t2.0 2out.2",
+    "p": "sP4.0 sP4.1 sP4.2 sP5.0 sP7.0 sP3.0 sP3.1 sP1.0 sP0.0 sP1.1 0P3.0 0P2.0 sP0.1 0P7.0 sP1.2 0P3.1 0P4.0 0P2.1 0P3.2 sP0.2 0P4.1 "
+         "sP1.3 0P5.0 0P4.2 0P1.0 0P2.2 sP0.3 0P5.1 0P7.1 0P3.3 sP0.4 0P5.2 0P2.3 0P6.0 0P7.2 0P0.0 0P1.1 0P0.1 0P3.4 0P5.3 0P6.1 0P7.3 "
+         "0P6.2 0P4.3 0P4.4 0P4.5 0P4.6 1P3.0 1P3.1 1P3.2 1P2.0 1P7.0 1P1.0 1P5.0 1P4.0 1P5.1 1P4.1 1P4.2 1P7.1 1P3.3 1P2.1 1P6.0 1P2.2 "
+         "1P5.2 1P0.0 1P2.3 1P1.1 1P4.3 1P0.1 1P3.4 1P6.1 1P7.2 1P4.4 1P6.2 1P5.3 1P4.5 1P7.3 1P4.6 2P3.0 2P3.1 2P3.2 2P2.0 2P7.0 2P2.1 "
+         "2P5.0 2P2.2 2P1.0 2P5.1 2P4.0 2P4.1 2P4.2 2P7.1 2P3.3 2P6.0 2P5.2 2P2.3 2P6.1 2P4.3 2P6.2 2P4.4 2P5.3 2P4.5 2P0.0 2P4.6 2P1.1 "
+         "2P7.2 2P5.4 2P0.1 2P7.3 2P3.4 2P3.5 2P3.6",
+    "g": "spi.0 snn.0 sSF.0 siu.0 sc16.0 sdg.1 sdg.0 sKF0.0 sX0.0 sca.0 sxr.2 sT5.0 sO6.0 sD.2 sO7.0 sX0.3 sO8.0 sD.1 sM1.0 sM1.1 sphn.0 "
+         "sTri.0 sM1.2 sc128.0 sT2.0 sM1.3 sM2.0 sNW.0 sinc.0 sM2.1 sM2.2 sM2.3 sinc.2 sM2.4 sM2.5 sM1.4 sM2.6 sM1.5 sM2.7 sinc.1 sT5.1 "
+         "sM1.6 sM2.8 sM1.7 0X1.1 sM1.8 sM1.9 sM2.9 sw2.0 sM1.10 sM1.11 0X1.6 sM2.10 sM2.11 sHH.0 0NW.2 1X2.1 1X2.6 1NW.2 2X3.1",
+    "s": "sxr.1 sxr.0 sX0.4 sKI1.0 sX2.0 sX3.1 sXB.2 sKF1.0 sKI0.0 sNW.1 sX1.0 sXB.0 sXB.1 0X1.0 sW.5 0XB.0 0XB.1 0XB.2 1X2.0 0XB.4 0XB.3 "
+         "0W.0 1XB.1 sX3.0 1XB.3 1W.0 1XB.4 1XB.0 2X3.0 1XB.2 2out.1 2out.0",
+}
 
 
 def R(n, lo=0, hi=None, st=1):
@@ -51,20 +122,23 @@ def cnt(r):
     return (r[2] - r[1] + r[3] - 1) // r[3]
 
 
-def two(r):
-    return r[0] in SB and SB[r[0]][1] in (bf, u16)
+def lcol(s):
+    return s // 16 if s < OD else 96 + (s - OD) // 16
 
 
 def build(g, T, topo, core, rank):
     ops = []
+    now = ["s", {}]
 
     def ap(r):
         if r[3] == 1:
             return T[r[0]][:, r[1]:r[2]]
         return T[r[0]][:, r[1]:r[2]:r[3]]
 
-    def add(q, cost, rd, wr, fn, kind="c", lat=0.0, after=()):
-        ops.append([q, float(cost), lat, list(rd), list(wr), fn, kind, list(after)])
+    def add(alt, rd, wr, kind="c", after=()):
+        w = wr[0][0] if wr else "out"
+        now[1][w] = now[1].get(w, -1) + 1
+        ops.append([alt, list(rd), list(wr), kind, list(after), "%s%s.%d" % (now[0], w, now[1][w])])
         return len(ops) - 1
 
     def sc(x):
@@ -82,42 +156,20 @@ def build(g, T, topo, core, rank):
                 out.append(x)
         return out
 
-    def vcost(o, a, f):
-        if isinstance(o, list):
-            return 60 + SC * 16 * cnt(o[1])
-        if isinstance(a, list):
-            return 60 + GA * 16 * cnt(a[1])
-        return 60 + max(64, f * cnt(o))
+    def put(alt, o, *ins):
+        return add(alt, regs(*ins) + ([o[1]] if isinstance(o, list) else []), [o[0]] if isinstance(o, list) else [o])
 
-    def wr(o):
-        return [o[0]] if isinstance(o, list) else [o]
-
-    def rd(o):
-        return [o[1]] if isinstance(o, list) else []
-
-    def ts(o, a, s1, op0, s2=None, op1=None):
+    def ts_(o, a, s1, op0, s2=None, op1=None):
         def fn():
             if op1 is None:
                 return g.vector.tensor_scalar(ap(o), side(a), sc(s1), None, op0)
             return g.vector.tensor_scalar(ap(o), side(a), sc(s1), sc(s2), op0, op1)
-        return add("v", vcost(o, a, 0.5 if two(o) and isinstance(a, tuple) and two(a) else 1), regs(a, s1, s2), [o], fn)
+        return {"v": fn}
 
-    def tt(o, a, b, op):
-        f = TT if isinstance(a, list) or (a[0] in SB and b[0] in SB) else 1
-        return add("v", vcost(o, a, f), regs(a, b), [o], lambda: g.vector.tensor_tensor(ap(o), side(a), ap(b), op))
+    def cp_(o, a):
+        return {"v": lambda: g.vector.tensor_copy(side(o), side(a))}
 
-    def cp(o, a):
-        f = 0.5 if not isinstance(o, list) and not isinstance(a, list) and two(o) and two(a) else 1
-        return add("v", vcost(o, a, f), regs(a) + rd(o), wr(o), lambda: g.vector.tensor_copy(side(o), side(a)))
-
-    def ms(o, val):
-        return add("v", vcost(o, o, 0.5 if two(o) else 1), [], [o], lambda: g.vector.memset(ap(o), val))
-
-    def scan(o, a, b, op0, op1):
-        return add("v", vcost(o, a, 0.5 if two(o) and two(a) and two(b) else 1), [a, b], [o],
-                   lambda: g.vector.tensor_tensor_scan(ap(o), ap(a), ap(b), 0.0, op0, op1))
-
-    def act(o, a, func, bias=None, scale=None):
+    def act_(o, a, func, bias=None, scale=None):
         def fn():
             kw = {}
             if bias is not None:
@@ -125,52 +177,82 @@ def build(g, T, topo, core, rank):
             if scale is not None:
                 kw["scale"] = sc(scale)
             return g.scalar.activation(side(o), side(a), func, **kw)
-        return add("a", 30 + vcost(o, a, 1), regs(a, bias, scale) + rd(o), wr(o), fn)
+        return {"a": fn}
 
-    def either():
-        return "v" if ",%d," % len(ops) in ONV else "a"
+    def ts(o, a, s1, op0, s2=None, op1=None):
+        return put(ts_(o, a, s1, op0, s2, op1), o, a, s1, s2)
+
+    def tt(o, a, b, op):
+        return put({"v": lambda: g.vector.tensor_tensor(ap(o), side(a), ap(b), op)}, o, a, b)
+
+    def cp(o, a):
+        return put(cp_(o, a), o, a)
+
+    def scan(o, a, b, op0, op1, init=0.0):
+        return put({"v": lambda: g.vector.tensor_tensor_scan(ap(o), ap(a), ap(b), init, op0, op1)}, o, a, b)
+
+    def act(o, a, func, bias=None, scale=None):
+        return put(act_(o, a, func, bias, scale), o, a, bias, scale)
 
     def copy(o, a, func=ACT.Copy):
-        return cp(o, a) if either() == "v" else act(o, a, func)
+        return put({**cp_(o, a), **act_(o, a, func)}, o, a)
 
     def lin(o, a, bias=0.0, scale=1.0):
-        return ts(o, a, scale, ALU.mult, bias, ALU.add) if either() == "v" else act(o, a, ACT.Identity, bias=bias, scale=scale)
+        return put({**ts_(o, a, scale, ALU.mult, bias, ALU.add), **act_(o, a, ACT.Identity, bias, scale)}, o, a, bias, scale)
 
     def clip(o, a):
-        return ts(o, a, 1.0, ALU.min, -1.0, ALU.max) if either() == "v" else act(o, a, ACT.Sign)
+        return put({**ts_(o, a, 1.0, ALU.min, -1.0, ALU.max), **act_(o, a, ACT.Sign)}, o, a)
 
-    def mm(lst):
+    def mm(lst, start=True, stop=True, each=None):
+        def fn():
+            ins, n = None, each or len(lst)
+            for i, (o, l, r) in enumerate(lst):
+                ins = g.tensor.matmul(ap(o), ap(l), ap(r), start and i % n == 0, stop and i % n == n - 1)
+            return ins
+        return add({"p": fn}, [x[1] for x in lst] + [x[2] for x in lst], [lst[0][0]])
+
+    def turn(o, a):
         def fn():
             ins = None
-            for i, (o, l, r) in enumerate(lst):
-                ins = g.tensor.matmul(ap(o), ap(l), ap(r), i == 0, i == len(lst) - 1)
+            for k in range(0, cnt(a), 128):
+                ins = g.tensor.transpose(ap(P(6, o[1] + k, o[1] + k + 128)), ap(R(a[0], a[1] + k, a[1] + k + 128)), ap(Im))
             return ins
-        c = sum(max(64, cnt(r)) * (4 if SB[r[0]][1] == f32 else 1) for o, l, r in lst) * PE + 60
-        return add("p", c, [x[1] for x in lst] + [x[2] for x in lst], [lst[0][0]], fn)
+        return add({"p": fn}, [a, Im], [o])
 
-    def iota(o, pat, base, cm, after=()):
+    def iota_(o, pat, base, cm):
         def fn():
             if SB[o[0]][1] == i32:
                 return g.iota(ap(o), pat, base, cm)
             return g.iota(ap(o), pat, base, cm, allow_small_or_imprecise_dtypes=True)
-        return add("g", 160 + 2 * cnt(o), [], [o], fn, after=after)
+        return {"g": fn}
 
-    def pick(o, a, base, op):
-        return add("g", 205 + 2 * cnt(o), [a], [o], lambda: g.affine_select(ap(o), ap(a), [[-1, cnt(o)]], op, 0.0, base, 1))
+    def iota(o, pat, base=0, cm=0):
+        return put(iota_(o, pat, base, cm), o)
 
-    def dma(q, o, a, lat, acc=False, after=()):
+    def fill(o, val):
+        return put({"v": lambda: g.vector.memset(ap(o), float(val)), **(iota_(o, [[0, cnt(o)]], val, 0) if val == int(val) else {})}, o)
+
+    def keep(o, a, op, base, cp_, ci, cj, other=0.0):
+        return put({"g": lambda: g.affine_select(ap(o), ap(a), [[ci, cnt(o) // 16], [cj, 16]], op, other, base, cp_)}, o, a)
+
+    def dma(q, o, a, acc=False, after=(), parts=None):
         def fn():
+            if parts:
+                return [g.sync.dma_start(T[o[0]][p:p + parts, o[1]:o[2]], T[a[0]][p:p + parts, a[1]:a[2]]) for p in range(0, 128, 16)]
             x, y = ap(o) if isinstance(o, tuple) else o(), ap(a) if isinstance(a, tuple) else a()
             if acc:
-                return g.dma_start(x, y, accum_op=ALU.add)
-            return {"s": g.sync, "a": g.scalar, "g": g}[q].dma_start(x, y)
-        return add(q, 1200 if q == "g" else 80, regs(a) + (regs(o) if acc else []), regs(o), fn, "dma", lat, after)
+                return [g.dma_start(x, y, accum_op=ALU.add)]
+            return [{"s": g.sync, "a": g.scalar}[q].dma_start(x, y)]
+        return add({q: fn}, regs(a) + (regs(o) if acc else []), regs(o), "dma", after)
 
     def P(b, lo, hi, st=1):
         return ("P%d" % b, lo, hi, st)
 
-    def C(j):
-        return R("col", j, j + 1)
+    def C(j, n=1):
+        return R("col", j, j + n)
+
+    def E(j, n=1):
+        return R("E", j, j + n)
 
     def sel(p, n="Tm"):
         return R(n, 15 - p, 143 - p)
@@ -189,277 +271,367 @@ def build(g, T, topo, core, rank):
                 [RemoteDMATransfer(dst_ids=[DstId(rid=t[0], pnc=t[1])], dma_engine_mask=t[2], remote_sem=T.sem["arr%d" % r],
                                    src=ap(R("S%d" % r, b * L, (b + 1) * L)), dst=ap(R("X%d" % r, GO + b * L, GO + (b + 1) * L)))
                  for b, t in enumerate(trs)], local_sem=T.sem.sent)
-        n = trs[0][3] + trs[1][3]
-        return add("g", 600, [R("S%d" % r)], [R("X%d" % r, GO, XW)], fn, ("arr%d" % r, n), 4500.0 if r == 0 else 3000.0)
+        return add({"g": fn}, [R("S%d" % r)], [R("X%d" % r, GO, XW)], ("arr%d" % r, trs[0][3] + trs[1][3]))
 
-    dma("a", R("hi"), lambda: T.head[:], 2400.0)
+    Im, Ni = R("Im", 0, 128), R("Ni")
+    dma("a", R("hi"), lambda: T.head[:])
+    dma("a", R("ni"), lambda: T.nxt[:])
     for k in range(2):
-        dma("s", R("xr", k * H, (k + 1) * H), lambda k=k: T.x[:, k * H:(k + 1) * H], 3800.0 + 1200 * k)
-    dma("a", R("ni"), lambda: T.nxt[:], 2600.0)
+        dma("s", R("xr", k * H, (k + 1) * H), lambda k=k: T.x[:, k * H:(k + 1) * H])
     cp(R("h0"), R("hi"))
-    g0 = [copy(R("S0"), [R("xr"), R("h0")])]
+    g0 = [copy(R("S0"), [R("xr", 0, V), R("h0")])]
     s0 = send(0)
-    ts(R("h2"), R("hi"), 1, ALU.arith_shift_right)
-    cp(R("h1"), R("h2"))
+    ts(R("h1"), R("hi"), 0.5, ALU.mult)
     for k in range(2):
-        copy(R("X0", k * 768, (k + 1) * 768), R("xr", k * H, (k + 1) * H, 2))
-        copy(R("X0", H + k * 768, H + (k + 1) * 768), R("xr", k * H + 1, (k + 1) * H, 2))
+        copy(R("X0", OD + k * 768, OD + (k + 1) * 768), R("xr", k * H + 1, (k + 1) * H, 2))
 
     iota(R("pi", 0, 1), [[0, 1]], 0, 1)
-    iota(R("iu"), [[1, 144]], 0, 0)
-    iota(R("c16"), [[16, 192]], 0, 0)
-    iota(R("c128"), [[0, 2], [128, 96]], 128 * 129, 0)
-    iota(R("nn"), [[0, 2], [16, 20]], 0, 0)
-    for j, m in ((1, 112), (2, 15), (3, 7), (4, 1), (5, 14), (6, 8)):
-        ts(R("pi", j, j + 1), R("pi", 0, 1), m, ALU.bitwise_and)
-    cp(R("col", 0, 7), R("pi", 0, 7))
+    iota(R("iu"), [[1, 144]])
+    iota(R("c16"), [[OD, 2], [16, 96]])
+    iota(R("c128"), [[0, 2], [128, 96]], 128 * 129)
+    iota(R("nn"), [[0, 2], [16, 20]])
+    fill(R("on"), 1)
+    iota(R("dg", 960, 1152), [[-16, 96], [0, 2]])
+    iota(R("dg", 1152, 1344), [[0, 96], [-8, 2]])
+    for j, m in enumerate((112, 15, 1, 14, 8, 7)):
+        ts(R("pi", j + 1, j + 2), R("pi", 0, 1), m, ALU.bitwise_and)
+    cp(C(0, 7), R("pi", 0, 7))
+    row = C(2)
     ts(R("M0"), R("iu"), C(1), ALU.subtract)
-    ts(R("E"), R("iu", 0, 16), C(2), ALU.is_equal)
-    ts(C(7), C(5), 0.5, ALU.mult, 8.0, ALU.add)
-    ts(C(8), C(4), -1.0, ALU.mult, 1.0, ALU.add)
-    ts(R("Pt", 0, 136), R("M0", 0, 136), C(7), ALU.is_equal, C(8), ALU.mult)
-    ts(R("Pt", 136, 272), R("M0", 0, 136), C(7), ALU.is_equal, C(4), ALU.mult)
+    ts(R("E"), R("iu", 0, 16), row, ALU.is_equal)
+    ts(R("Im"), R("iu"), C(0), ALU.is_equal)
+    lin(C(7), C(4), bias=8.0, scale=0.5)
+    lin(C(8), C(3), bias=1.0, scale=-1.0)
+    ts(R("Pb", 0, 136), R("M0", 0, 136), C(7), ALU.is_equal, C(8), ALU.mult)
+    ts(R("Pb", 136, 272), R("M0", 0, 136), C(7), ALU.is_equal, C(3), ALU.mult)
+    lin(C(9), C(6), bias=1.0, scale=2.0)
+    lin(C(10), C(5), scale=0.125)
+    lin(C(11), C(5), bias=1.0, scale=-0.125)
+    ts(R("T3", 0, 136), R("M0", 0, 136), C(9), ALU.is_equal, C(11), ALU.mult)
+    ts(R("T3", 136, 272), R("M0", 0, 136), C(9), ALU.is_equal, C(10), ALU.mult)
+    lin(R("T4"), R("T3"), scale=-BIG)
     ts(R("Tm"), R("M0"), 15.0, ALU.is_equal)
-    ts(R("Im"), R("M0", 0, 128), C(2), ALU.is_equal)
-    lin(R("Ni"), R("Im"), scale=-1.0)
-    lin(R("N4"), R("Im"), scale=-4096.0)
-    lin(R("I4"), R("Im"), scale=4096.0)
-    ts(R("w0"), R("M0", 0, 128), 15.0, ALU.is_le)
-    ts(R("w1"), R("M0", 0, 128), 0.0, ALU.is_ge)
-    tt(R("Bm"), R("w0"), R("w1"), ALU.mult)
-    add("g", 461, [R("Bm")], [R("Tri")], lambda: g.affine_select(ap(R("Tri")), ap(R("Bm")), [[1, 128]], ALU.is_ge, 0.0, 0, -1))
-    lin(R("phi"), R("c16"), bias=C(2))
-    lin(R("base"), R("phi", 0, 96), bias=float(GO - H))
-    lin(R("nn"), R("nn"), bias=C(2))
-    lin(R("jn"), R("phi", 0, 40), bias=float(V))
-    ms(R("ca"), 0.0)
-    ts(R("ca", 7, 13), R("c16", 0, 6), -1.0 / 4096, ALU.mult)
-    lin(C(9), C(2), bias=float(V))
-    lin(C(10), R("E", 1, 2), scale=-2048.0)
-    lin(C(11), R("E", 15, 16), scale=16.0)
-    lin(C(12), R("E", 15, 16), bias=1.0, scale=-16.0)
-    ts(R("A0"), R("M0", 0, 128), 0.0, ALU.is_equal, float(H), ALU.mult)
-    ts(R("w3"), R("M0", 0, 128), 1.0, ALU.is_equal, C(11), ALU.mult)
-    ts(R("w5"), R("M0", 0, 128), 2.0, ALU.is_equal, C(12), ALU.mult)
-    tt(R("w3"), R("w3"), R("w5"), ALU.add)
-    tt(R("A1"), R("w3"), R("A0"), ALU.subtract)
-    ts(R("w4"), R("M0"), 4.0, ALU.is_equal)
-    for p in range(16):
-        pick(R("U", 144 * p, 144 * p + 129), R("w4", 0, 129), 4 - p, ALU.is_equal)
-    iota(R("SF"), [[0, 208]], 0, 0)
-    dma("s", R("SI"), R("SF"), 2500.0, after=g0)
-    ms(R("D", V, GO), 0.0)
-    for lo in range(GO, ZW, 512):
-        dma("s", R("D", lo, lo + 512), R("D", V, V + 512), 3000.0, after=g0)
+    keep(R("T2"), R("Tm"), ALU.is_ge, 1, -1, 16, 0)
+    keep(R("T5"), R("Tm"), ALU.is_ge, 3, -1, 16, 0)
+    keep(R("T5"), R("T5"), ALU.is_ge, -2, 1, -16, 0)
+    lin(Ni, Im, scale=-1.0)
+    lin(R("N4"), Im, scale=-4096.0)
+    lin(R("IB"), Im, scale=BIG)
+    lin(R("I32"), Im)
+    act(R("ab"), R("M0", 0, 128), ACT.Abs, bias=-7.5)
+    ts(R("Bm"), R("ab"), 8.0, ALU.is_lt)
+    keep(R("Tri"), R("Bm"), ALU.is_ge, 0, -1, 16, 1)
+    lin(R("nn"), R("nn"), bias=row)
+    ts(R("jn", 0, 40), R("c16", 0, 40), row, ALU.add, float(JK), ALU.add)
+    ts(R("jn", 40, 80), R("c16", 0, 40), row, ALU.add, float(V), ALU.add)
+    fill(R("ca"), 0)
+    lin(R("ca", 7, 13), R("c16", 0, 6), bias=-V / 4096, scale=-1.0 / 4096)
+    lin(C(12), E(0), scale=-2048.0)
+    lin(C(13), E(2), bias=C(12), scale=-4096.0)
+    lin(C(14), E(15), bias=-float(OD), scale=16.0)
+    lin(C(15), E(15), bias=1.0, scale=-16.0)
+    lin(C(16), E(15), scale=32.0)
+    lin(C(17), E(15), bias=1.0, scale=-32.0)
+    ts(R("A0"), R("M0", 0, 128), 0.0, ALU.is_equal, float(OD), ALU.mult)
+    ts(R("w0"), R("M0", 0, 128), 0.0, ALU.is_equal, C(14), ALU.mult)
+    ts(R("w1"), R("M0", 0, 128), 1.0, ALU.is_equal, C(15), ALU.mult)
+    keep(R("w2", 0, 128), R("Bm"), ALU.is_equal, -3, 0, 0, 1)
+    ts(R("w2", 128, 256), R("M0", 0, 128), 2.0, ALU.is_equal, C(16), ALU.mult)
+    ts(R("w2", 256, 384), R("M0", 0, 128), 3.0, ALU.is_equal, C(17), ALU.mult)
+    lin(C(18), row, scale=2.0)
+    lin(C(19), row, bias=-float(H))
+    lin(C(20), row, bias=MT - H)
+    lin(C(21), C(3), scale=-float(OD))
+    lin(C(22), C(4), scale=0.5)
+    lin(C(23), C(3), bias=C(22), scale=float(OD))
+    iota(R("phn"), [[8, 2], [16, 96]])
+    lin(R("phn"), R("phn"), bias=C(23))
+    for o in (R("SF"), R("SI"), R("D", JK, GO), R("xr", V, V + 16), R("X0", H, OD), R("NW", H, OD), R("W", 0, 16), R("W", OD, WW),
+              R("HH", 128, 136), R("KF0", 0, 320)):
+        fill(o, 0)
+    fill(R("D", JK + 1, JK + 2), -0.25)
+    fill(R("D", H, OD), 100)
+    fill(R("D", GO, XW), 100)
     for k in range(4):
-        dma("s", R("X%d" % k, V, GO), R("D", V, GO), 3000.0, after=g0 if k == 0 else [s0])
-    dma("s", R("X3", GO, XW), R("D", V, V + 2 * L), 2500.0, after=[s0])
-    dma("s", R("NW", V, ZW), R("D", V, ZW), 3500.0, after=[s0])
-    iota(R("KF0", 0, 320), [[0, 320]], 0, 0)
+        dma("s", R("X%d" % k, JK, GO), R("D", JK, GO), after=g0 if k == 0 else [s0])
+    dma("s", R("X3", GO, XW), R("D", JK, JK + 2 * L), after=[s0])
+    dma("s", R("NW", JK, GO), R("D", JK, GO), after=[s0])
     for n in ("KF1", "KI0", "KI1"):
-        dma("s", R(n, 0, 320), R("KF0", 0, 320), 3000.0, after=g0)
-    iota(R("DW", 0, H), [[0, H]], 0, 0, after=[s0])
+        dma("s", R(n, 0, 320), R("KF0", 0, 320), after=g0)
     for r in range(RO):
-        iota(R("inc", 320 * r, 320 * r + 320), [[0, 320]], 2 ** r, 0)
-    lin(C(16), C(2), bias=-(H + V - 1) / 2.0)
-    lin(C(17), C(2), bias=-float(H))
-    lin(C(13), C(3), bias=1.0, scale=2.0)
-    lin(C(14), C(6), scale=0.125)
-    lin(C(15), C(6), bias=1.0, scale=-0.125)
-    ts(R("T3", 0, 129), R("M0", 0, 129), C(13), ALU.is_equal, C(15), ALU.mult)
-    ts(R("T3", 136, 265), R("M0", 0, 129), C(13), ALU.is_equal, C(14), ALU.mult)
+        fill(R("inc", 320 * r, 320 * r + 320), 2 ** r)
+    for j in (6, 7, 8):
+        keep(R("O%d" % j), R("on"), ALU.is_equal, 16 - j - 256, 1, -16, 256)
+    lin(C(24), row, bias=10.0)
+    ts(C(25), row, 6.0, ALU.is_lt)
+    ts(R("BP"), R("M0", 0, 128), C(24), ALU.is_equal, C(25), ALU.mult)
+    fill(R("pw", 0, 24), 2)
+    fill(R("pw", 24, 48), 0.5)
+    scan(R("pw", 48, 72), R("pw", 0, 24), R("SI", 100, 124), ALU.mult, ALU.add, 0.5)
+    scan(R("pw", 72, 96), R("pw", 24, 48), R("SF", 100, 124), ALU.mult, ALU.add, 1.0)
+    for k in range(4):
+        for h in range(2):
+            lin(R("bas", 2 * k + h, 192, 8), R("pw", 48, 72), bias=E(8), scale=E(k + 3 * h if k < 3 else 6 + h))
+    for t in range(3):
+        mm([(P(t % 2, a, 512, 8), m, R("bas", 64 * t, 64 * t + 64)) for a in range(8)
+            for m in (R("BP"), sel(a, "O8"), sel((a + 1) % 8, "O6"), sel((a + 2) % 8, "O7"))], each=4)
+        copy(R("W", 16 + 512 * t, 528 + 512 * t), P(t % 2, 0, 512))
+    tt(C(26, 3), E(10, 3), E(13, 3), ALU.add)
+    act(C(30), row, ACT.Abs, bias=-5.5)
+    ts(C(29), C(30), 4.0, ALU.is_lt)
+    for k in range(4):
+        lin(R("RR", k, 96, 4), R("pw", 72, 96), scale=C(26 + k))
+    for h in range(2):
+        M = R("M%d" % (h + 1))
+        keep(M, R("Bm"), ALU.is_ge, -10 - 3 * h, 1, -16, 0)
+        keep(M, M, ALU.is_ge, 12 + 3 * h, -1, 16, 0)
+        keep(M, M, ALU.is_ge, -2, 0, 0, 1)
+        keep(M, M, ALU.is_ge, 9, 0, 0, -1)
+        for a in range(8):
+            keep(M, M, ALU.not_equal, -2 - (a + 1 + h) % 8 - 256 * (2 + a), 1, -16, 256, 1.0)
 
-    ts(R("t0"), R("ni"), float(V), ALU.min, 0.0, ALU.max)
-    ts(R("t1"), R("t0"), 1, ALU.bitwise_and)
-    ts(R("t2"), R("t0"), 0.5, ALU.mult)
-    ts(R("t3"), R("t1"), H - 0.5, ALU.mult)
-    ts(R("t4"), R("ni"), float(V), ALU.is_ge, float(GO - H), ALU.mult)
-    ts(R("t5"), R("ni"), float(V), ALU.subtract, 0.0, ALU.max)
-    ts(R("fn"), R("ni"), 0.0, ALU.is_lt)
+    def ti(k):
+        return R("ti", 192 * k, 192 * k + 192)
 
-    def perm(bank, srcs):
-        for b in range(2):
-            mm([(P(bank, 96 * b, 96 * b + 96), R("Pt", 136 * b + 8 - 8 * h, 136 * b + 136 - 8 * h), R(s, h, 192, 2))
-                for s in srcs for h in range(2)])
-    tt(R("t2"), R("t2"), R("t3"), ALU.add)
-    tt(R("t4"), R("t4"), R("t5"), ALU.add)
-    perm(7, ["t2", "t4"])
-    perm(4, ["fn"])
-    copy(R("FR"), P(4, 0, 192))
+    def dg(k, h=None):
+        return R("dg", 192 * k, 192 * k + 192) if h is None else R("dg", 192 * k + h, 192 * k + 192, 2)
 
-    def pointers(pl, n=96):
-        ts(R("soff", 96, 192), P(7 if n == 192 else 3, 96, 192), pl, ALU.add)
-        ts(R("soff", 0, 96), P(7, 0, 96), pl, ALU.add)
-        if n == 192:
-            lin(R("s", 0, n), P(7, 0, n), bias=pl)
-        act(R("ab"), P(7, 0, 96), ACT.Abs, bias=-(H + V - 1) / 2.0 if n == 192 else C(16))
-        lin(R("dj"), P(7, 0, 96), bias=-float(H) if n == 192 else C(17))
-        ts(R("cc"), R("ab"), 768.0, ALU.is_lt)
-    pointers(0.0, 192)
-    tt(R("t0"), R("s"), R("phi"), ALU.subtract)
-    ts(R("t1"), R("t0"), 31, ALU.bitwise_and)
-    cp(R("rl"), R("t1"))
-    tt(R("rh"), R("t0"), R("t1"), ALU.subtract)
-    for p in range(16):
-        bk, o = (0, 1, 2, 6)[(p // 2) % 4], 192 * (p % 2)
-        mm([(P(bk, o, o + 192), R("U", 144 * p + 1, 144 * p + 129), R("rh")), (P(bk, o, o + 192), R("U", 144 * p, 144 * p + 128), R("rl"))])
-        copy(R("NW", p, V, 16), P(bk, o, o + 192))
+    def rows(b, h):
+        return R("Pb", 136 * b + 8 - 8 * h, 136 * b + 136 - 8 * h)
+    ts(ti(0), R("ni"), float(V), ALU.min, 0.0, ALU.max)
+    ts(dg(7), R("ni"), 0.0, ALU.is_lt, float(H), ALU.mult)
+    ts(dg(2), R("ni"), float(V), ALU.is_ge, float(GO - H), ALU.mult)
+    ts(dg(4), R("ni"), float(V), ALU.subtract, 0.0, ALU.max)
+    ts(ti(1), ti(0), 1, ALU.arith_shift_right, 4080, ALU.bitwise_and)
+    ts(ti(2), ti(0), 1, ALU.bitwise_and)
+    ts(ti(3), ti(0), 1, ALU.arith_shift_right, 15, ALU.bitwise_and)
+    cp(dg(0), ti(1))
+    ts(dg(1), ti(2), float(OD), ALU.mult, C(21), ALU.add)
+    ts(dg(3), ti(3), C(22), ALU.subtract)
+    for b in range(2):
+        mm([(P(4, 96 * b, 96 * b + 96), rows(b, h), dg(7, h)) for h in range(2)])
+    mm([(P(4, 192, 288), rows(0, h), dg(7, h)) for h in (0, 1, 0, 1)] + [(P(4, 192, 288), Im, R("c16", 0, 96))] * 2)
+    ts(R("yo"), P(4, 192, 288), C(18), ALU.add, float(V), ALU.min)
+    lin(R("FR"), P(4, 0, 192), scale=1.0 / H)
+    for k in range(2):
+        copy(R("X0", k * 768, (k + 1) * 768), [R("xr"), R("yo", 48 * k, 48 * k + 48)])
+    for lo, hi, way in CUT:
+        if way == "t" and lo < H:
+            dma("s", R("XB", lo, hi), R("X0", lo, hi))
+    for b in (1, 0):
+        o = P(7 - 2 * b, 0, 96)
+        mm([(o, Im, R("c16", 96 * b, 96 * b + 96))] + [(o, rows(b, h), dg(k, h)) for k in range(8) for h in range(2)])
+
+    def pointers():
+        ts(R("soff", 96, 192), P(5, 0, 96), row, ALU.add)
+        ts(R("soff", 0, 96), P(7, 0, 96), row, ALU.add)
+        ts(R("aoff"), P(7, 0, 96), C(19), ALU.add, 0.0, ALU.max)
+        lin(R("dj"), P(7, 0, 96), bias=C(20))
+    pointers()
+    for h in range(2):
+        o = P(3, 192 * h, 192 * h + 192)
+        mm([(o, R("T3", 136 * h + 1 - b, 136 * h + 129 - b), dg(k)) for b, ks in enumerate(((0, 1, 2, 5, 7), (3, 4, 6))) for k in ks])
+    copy(R("Z"), P(3, 0, 384))
+    for t in range(6):
+        b, c = 1 - t // 3, 64 * (t % 3)
+        mm([(P((t + 1) % 2, p // 2, 512, 8), R("Im", 2 * (p % 8), 2 * (p % 8) + 128), R("Z", 192 * (p // 8) + c, 192 * (p // 8) + c + 64))
+            for p in range(b, 16, 2)], each=1)
+        copy(R("NW", OD * b + 8 * c, OD * b + 8 * c + 512), P((t + 1) % 2, 0, 512))
+    dma("s", R("W", 16, OD), R("NW", OD, JK), parts=2)
 
     def nth(n, a, r):
         S, z = "S" + n, float(2 ** r)
         a0, a1, a2 = R(a, 0, 96), R(a, 96, 192), R(S, 112, 208)
-        scan(R(S, 1, 97), a0, a1, ALU.add, ALU.add)
         tt(a2, a0, a1, ALU.add)
-        k, d, o = (5, 6, 0) if n == "I" else (2, 7, 192)
-        mm([(P(k, 384, 397), R("Im"), R("ca", 0, 13))] + [(P(k, 384, 397), sel(p), R(S, p, 208, 16)) for p in range(16)])
-        if n == "I":
-            mm([(P(k, 400, 401), R("Bm"), R(S, 96, 97))])
-        mm([(P(k, 0, 192), R("Ni"), R("c128")), (P(k, 0, 96), R("Tri"), a2), (P(k, 0, 96), R("Ni"), a1), (P(k, 96, 192), R("Tri"), a2)])
-        if n == "F":
-            mm([(P(k, 192, 288), R("Bm"), R(S, 0, 96)), (P(k, 192, 288), R("Tri"), a2), (P(k, 192, 288), R("Ni"), a1), (P(k, 192, 288), R("I4"), a0)])
-            mm([(P(k, 288, 384), R("Bm"), R(S, 0, 96)), (P(k, 288, 384), R("Tri"), a2), (P(k, 288, 384), R("I4"), a1)])
-        ts(R("u" + n, 0, 6), P(k, 391, 397), -4096.0, ALU.mult, C(9), ALU.add)
+        scan(R(S, 1, 97), a0, a1, ALU.add, ALU.add)
+        d, k, w = (3, 5, 1) if n == "I" else (7, 7, 2)
+        mm([(P(w, 0, 192), Ni, R("c128")), (P(w, 0, 96), R("Tri"), a2), (P(w, 0, 96), Ni, a1), (P(w, 96, 192), R("Tri"), a2)])
+        lin(R("W" + n), P(w, 0, 192), bias=z * (0.5 - 64), scale=-z)
+        mm([(P(k, 384, 397), Im, R("ca", 0, 13))] + [(P(k, 384, 397), sel(p), R(S, p, 208, 16)) for p in range(16)])
+        lin(R("u" + n, 0, 6), P(k, 391, 397), bias=row, scale=-4096.0)
         tt(R("v" + n, 0, 6), R("u" + n, 0, 6), P(k, 384, 390), ALU.max)
-        if n == "I":
-            ts(R("tot", 0, 1), P(k, 400, 401), float(CAP), ALU.min)
-        lin(R("W" + n), P(k, 0, 192), bias=z * (0.5 - 64), scale=-z)
         cp(R("c" + n, 0, 6), R("v" + n, 0, 6))
+        if n == "F":
+            mm([(P(2, 192, 288), R("Bm"), R(S, 0, 96)), (P(2, 192, 288), R("Tri"), a2), (P(2, 192, 288), Ni, a1), (P(2, 192, 288), R("IB"), a0)])
+            mm([(P(2, 288, 384), R("Bm"), R(S, 0, 96)), (P(2, 288, 384), R("Tri"), a2), (P(2, 288, 384), R("IB"), a1)])
+        else:
+            if r < RO - 1:
+                mm([(P(1, 192, 288), R("Bm"), R(S, 0, 96)), (P(1, 192, 288), R("Tri"), a2), (P(1, 192, 288), Ni, a1), (P(1, 192, 288), R("N4"), a0)])
+                ts(R("zc"), P(1, 192, 288), CAP + 0.5 - 4096, ALU.is_lt, OD + MT, ALU.add)
+            mm([(P(5, 400, 401), R("Bm"), R(S, 96, 97))])
+            ts(R("tot", 0, 1), P(5, 400, 401), float(CAP), ALU.min)
+            ts(R("FR"), P(2, 192, 384), BIG, ALU.subtract, R("tot", 0, 1), ALU.is_gt)
         for b in range(2):
             K = "K%s%d" % (n, b)
             copy([R(K), R("c" + n, 0, 6)], R("W" + n, 96 * b, 96 * b + 96), ACT.Silu)
             scan(R("k" + n, 320 * b, 320 * b + 320), R("inc", 320 * r, 320 * r + 320), R(K, 0, 320), ALU.add, ALU.max)
-        mm([(P(d, o, o + 320), R("A0"), R("k" + n, 0, 320)), (P(d, o, o + 320), R("A1"), R("k" + n, 320, 640))])
-        lin(R("DD", 320 * (n == "F"), 320 * (n == "F") + 320), P(d, o, o + 320), bias=C(10), scale=1 / (128 * z))
+        k0, k1 = R("k" + n, 0, 320), R("k" + n, 320, 640)
+        num = [(R("w2", 0, 128), k0), (R("w2", 128, 256), k1), (R("w2", 256, 384), k1)] * (r == RO - 1)
+        mm([(P(d, 192, 512), m, x) for m, x in [(R("A0"), k0), (R("w0"), k1), (R("w1"), k1)] + num])
+        lin(R("DD", 320 * (n == "F"), 320 * (n == "F") + 320), P(d, 192, 512), bias=C(13), scale=1 / (128 * z))
 
     for r in range(RO):
         X, Xn, last = "X%d" % r, "X%d" % (r + 1), r == RO - 1
+        now[:] = [str(r), {}]
         nth("F", "FR", r)
-        for lo, hi in CUT:
-            own = R("XB", lo, hi) if r else R("xr", 2 * (lo % H) + lo // H, 2 * (lo % H + hi - lo), 2)
-            tt(R("D", lo, hi), [R(X), R("soff", lo // 16, hi // 16)], own, ALU.subtract)
+        for lo, hi, way in CUT:
+            nx = [R(X), R("soff", lcol(lo), lcol(lo) + (hi - lo) // 16)]
+            if way == "t":
+                tt(R("D", lo, hi), nx, R("XB", lo, hi) if r or lo < H else R("xr", 2 * (lo - OD) + 1, 2 * (hi - OD), 2), ALU.subtract)
+            else:
+                put({**ts_(R("D", lo, hi), nx, -1.0, ALU.mult), **act_(R("D", lo, hi), nx, ACT.Identity, scale=-1.0)}, R("D", lo, hi), nx)
+                dma("g", R("D", lo, hi), R(X, lo, hi), acc=True)
             act(R("A", lo, hi), R("D", lo, hi), ACT.Abs)
-        for lo, hi in ((96, 192), (0, 80), (80, 96)):
-            o = P(3, lo, hi)
-            mm([(o, sel(p), R("A", 16 * lo + p, 16 * hi, 16)) for p in range(16)])
+        for lo, hi in LEN:
+            o = P(3, lcol(lo), lcol(lo) + (hi - lo) // 16)
+            mm([(P(3, 0, 192), Im, R("D", GO - 192, GO))] * (lo == OD) + [(o, sel(p), R("A", lo + p, hi, 16)) for p in range(16)]
+               + [(P(3, 0, 192), R("N4"), R("FR"))] * (hi == H), lo == OD, hi == H)
         for lo in range(0, H, 512):
-            act(R("AJ", lo, lo + 512), [R("D", 0, XW), R("soff", lo // 16, lo // 16 + 32)], ACT.Abs)
-        ts(R("sh"), P(3, 0, 96), 239.5, ALU.is_gt)
-        for lo, hi in ((0, 64), (64, 96)):
-            o = P(4, lo, hi)
-            mm([(o, R("N4"), R("cc", lo, hi)), (o, R("I4"), R("sh", lo, hi))] + [(o, sel(p), R("AJ", 16 * lo + p, 16 * hi, 16)) for p in range(16)])
-        lin(R("thr"), R("FR"), bias=440.5, scale=8192.0)
-        tt(R("far"), P(3, 0, 192), R("thr"), ALU.is_gt)
+            act(R("AJ", lo, lo + 512), [R("D", H, XW), R("aoff", lo // 16, lo // 16 + 32)], ACT.Abs, scale=4096.0)
+        ts(R("far"), P(3, 0, 192), 440.5, ALU.is_gt)
+        act(R("sh"), P(3, 0, 96), ACT.Sign, bias=-239.5)
+        mm([(P(4, 0, 96), Im, R("D", GO - 96, GO))] + [(P(4, 0, 64), sel(p), R("AJ", p, 1024, 16)) for p in range(16)], stop=False)
+        mm([(P(4, 64, 96), sel(p), R("AJ", 1024 + p, H, 16)) for p in range(16)], False, False)
+        mm([(P(4, 0, 96), R("IB"), R("sh"))], start=False)
         nth("I", "far", r)
-        ts(R("okj"), P(4, 0, 96), 440.5 - 4096, ALU.is_gt, 8192.0, ALU.mult)
-        tt(R("m2"), R("okj"), R("dj"), ALU.add)
-        tt(R("m3"), R("m2"), R("base"), ALU.min)
-        cp(R("moff"), R("m3"))
-        for lo in (H, 2304):
+        tt(R("m2"), P(4, 0, 96), R("dj"), ALU.max)
+        if last:
+            ts(R("moff"), R("m2"), MT, ALU.subtract, float(OD), ALU.min)
+        else:
+            tt(R("m2"), R("m2"), R("zc"), ALU.min)
+            ts(R("moff"), R("m2"), MT, ALU.subtract)
+        for lo in (OD, OD + 768):
             clip(R("C", lo, lo + 768), R("D", lo, lo + 768))
+        dma("s", R(Xn, H, JK), R(X, H, JK))
+        dma("g", R(Xn, OD, JK), R("C", OD, JK), acc=True)
         for k in range(3):
-            lo, hi = 512 * k, 512 * k + 512
-            tt(R("DE", lo, hi), [R("D", H, ZW), R("moff", lo // 16, hi // 16)], R("D", lo, hi), ALU.add)
-            clip(R("C", lo, hi), R("DE", lo, hi))
-        dma("s", R(Xn, H, V), R(X, H, V), 4000.0)
-        dma("g", R(Xn, H, V), R("C", H, V), 5500.0, acc=True)
-        for k in range(3):
-            lo, hi = 512 * k, 512 * k + 512
-            mm([(P(k % 2, 0, 512), R("Im"), R(X, lo, hi)), (P(k % 2, 0, 512), R("Im"), R("C", lo, hi))])
-            copy(R(Xn, lo, hi), P(k % 2, 0, 512))
-        ts(R("J0"), R("nn"), R("tot", 0, 1), ALU.is_ge, 65536.0, ALU.mult)
-        mm([(P(5, 420, 460), R("Im"), R("J0"))] + [(P(5, 420, 460), sel(p), R("DD", p, 640, 16)) for p in range(16)])
-        tt(R("PM"), P(5, 420, 460), R("jn"), ALU.min)
-        cp(R("ifo"), R("PM"))
+            lo, hi, o = 512 * k, 512 * k + 512, P(k % 2, 0, 512)
+            neg = any(c[0] <= lo < c[1] and c[2] == "d" for c in CUT)
+            de = R("D", lo, hi)
+            tt(de, [R("D", H, XW), R("moff", lo // 16, hi // 16)], de, ALU.subtract if neg else ALU.add)
+            clip(R("C", lo, hi), de)
+            mm([(o, Im, R(X, lo, hi)), (o, Im, R("C", lo, hi))])
+            copy(R("Y", 2 * lo, 2 * hi, 2) if last else R(Xn, lo, hi), o)
+        if not last:
+            lin(R("c1"), [R("D", 0, H), R("h1")], bias=192.0, scale=0.55)
+            act(R("c2"), R("c1"), ACT.Sign, bias=-192.0)
+            tt(R("S%d" % (r + 1)), [R(X, 0, H), R("h1")], R("c2"), ALU.add)
+            send(r + 1)
+        ts(R("J0"), R("nn"), R("tot", 0, 1), ALU.is_ge, BIG, ALU.mult)
+        for k in range(1 + last):
+            o = P(5, 420 + 40 * k, 460 + 40 * k)
+            mm([(o, Im, R("J0"))] + [(o, sel(p, ("T2", "T5")[k]), R("DD", p, 640, 16)) for p in range(16)])
+            tt(R("PM", 40 * k, 40 * k + 40), o, R("jn", 40 * k, 40 * k + 40), ALU.min)
+            cp(R("ifo", 40 * k, 40 * k + 40), R("PM", 40 * k, 40 * k + 40))
         oi, of = R("ifo", 0, 20), R("ifo", 20, 40)
         lin(R("yy"), [R("D", 0, GO), oi], bias=-0.25, scale=0.5)
         ts(R("hh"), R("yy"), MAGIC, ALU.add, MAGIC, ALU.subtract)
         clip(R("si"), R("hh"))
         tt(R("XV", 0, 320), [R(X, 0, GO), oi], R("si"), ALU.add)
         act(R("em"), R("yy"), ACT.Abs, bias=0.25)
-        ts(R("e1"), R("em"), 0.5, ALU.is_equal)
-        mm([(P(6, 0, 320), R("Im"), R(n, 0, 320)) for n in ("XV", "hh", "e1")])
-        copy(R("XV", 320, 640), P(6, 0, 320))
-        cp([R(Xn, 0, GO), oi], R("XV", 0, 320))
+        if last:
+            ts(R("e1"), R("em"), 0.5, ALU.is_equal)
+        else:
+            ts(R("e1"), R("em"), 0.3, ALU.is_gt)
+            ts(R("e2"), R("em"), 0.7, ALU.is_gt, -1.0, ALU.mult)
+        mm([(P(3, 192, 512), Im, R(n, 0, 320)) for n in ("XV", "hh", "e1") + ("e2",) * (not last)])
+        copy(R("XV", 320, 640), P(3, 192, 512))
         if not last:
-            copy(R("S%d" % (r + 1)), [R(Xn, 0, H), R("h1")])
-            send(r + 1)
-        cp([R(Xn, 0, GO), of], R("XV", 320, 640))
-        for k, (lo, hi) in enumerate(() if last else CUT):
-            dma("s", R("XB", lo, hi), R(Xn, lo, hi), 3000.0 + 700 * k)
-        for lo in (0, 512, 1024):
-            copy(R("Q", lo, lo + 512), [R("NW", H, ZW), R("moff", lo // 16, lo // 16 + 32)])
-        mm([(P(5, 0, 320), R("Im"), R("DD", 320, 640)), (P(5, 0, 320), R("Ni"), R("DD", 0, 320))])
-        copy(R("NV", 0, 320), P(5, 0, 320))
-        tt(R("NV", 320, 640), [R("NW", 0, GO), oi], R("NV", 0, 320), ALU.subtract)
-        cp([R("NW", 0, GO), R("ifo")], R("NV"))
-        for b in (1, 0):
-            o = P(7 - 4 * b, 96 * b, 96 * b + 96)
-            mm([(o, R("Im"), R("c16", 96 * b, 96 * b + 96))] + [(o, sel(p), R("Q", p, H, 16)) for p in range(16) if b == 0]
-               + [(o, sel(p), R("NW", H * b + p, H * b + H, 16)) for p in range(16)])
+            cp([R(Xn, 0, GO), oi], R("XV", 0, 320))
+            cp([R(Xn, 0, GO), of], R("XV", 320, 640))
+            for lo, hi, way in CUT:
+                if way == "t":
+                    dma("s", R("XB", lo, hi), R(Xn, lo, hi))
+        for k in range(3):
+            lo, hi, o = 512 * k, 512 * k + 512, P(6, 512 * (k % 2), 512 * (k % 2) + 512)
+            copy(R("Q", lo, hi), [R("W"), R("moff", lo // 16, hi // 16)])
+            turn(o, R("Q", lo, hi))
+            copy(R("Ut", lo, hi), o)
+            mm([(P(4, 128, 256), R("Ut", j, j + 128), R("Ut", j, j + 128)) for j in range(lo, hi, 128)], k == 0, k == 2)
+        mm([(P(2, 0, 320), Im, R("DD", 320, 640)), (P(2, 0, 320), Ni, R("DD", 0, 320))])
+        copy(R("NV", 0, 320), P(2, 0, 320))
+        if NVA:
+            copy(R("G"), [R("NW"), oi])
+            mm([(P(2, 0, 320), Im, R("G")), (P(2, 0, 320), Ni, R("DD", 320, 640)), (P(2, 0, 320), Im, R("DD", 0, 320))])
+            copy(R("NV", 320, 640), P(2, 0, 320))
+        else:
+            tt(R("NV", 320, 640), [R("NW"), oi], R("NV", 0, 320), ALU.subtract)
+        cp([R("NW"), oi], R("NV", 0, 320))
+        cp([R("NW"), of], R("NV", 320, 640))
         if not last:
-            pointers(C(2))
-            dma("g", R("NW", 0, H), R("Q"), 5000.0, acc=True)
-        for lo in range(0, H, 256):
-            act([R("DW"), R("moff", lo // 16, lo // 16 + 16)], R("inc", 320 * r, 320 * r + 256), ACT.Silu)
-        dma("g", R("DB"), R("DW", 0, H), 3500.0)
-        mm([(P(4, 96, 192), sel(p), R("DB", p, H, 16)) for p in range(16)])
-        ts(R("FR"), P(2, 192, 384), 4096.0, ALU.subtract, R("tot", 0, 1), ALU.is_gt)
-        ts(R("dd"), P(4, 96, 192), (8.0, 20.0, 45.0)[r], ALU.is_gt)
+            ev, od = P(7, 0, 96), P(5, 0, 96)
+            mm([(ev, Im, R("c16", 0, 96))] + [(ev, sel(p, "T2"), R("Q", p, H, 16)) for p in range(16)], stop=False)
+            mm([(od, Im, R("c16", 96, 192))] + [(od, sel(p, "T2"), R("NW", OD + p, JK, 16)) for p in range(16)])
+            mm([(ev, sel(p, "T2"), R("NW", p, H, 16)) for p in range(16)], start=False)
+            pointers()
+            dma("g", R("NW", 0, H), R("Q"), acc=True)
+            dma("s", R("W", 16, OD), R("NW", OD, JK), parts=2)
+        tt(R("HH", 0, 128), P(4, 128, 256), R("M1"), ALU.mult)
+        tt(R("HH", 136, 264), P(4, 128, 256), R("M2"), ALU.mult)
+        mm([(P(4, 256, 352), R("HH", 2, 130), R("RR")), (P(4, 256, 352), R("HH", 130, 258), R("RR"))])
+        ts(R("rn"), P(4, 256, 352), 2.0 ** 23, ALU.add, 2.0 ** 23, ALU.subtract)
+        tt(R("df"), P(4, 256, 352), R("rn"), ALU.subtract)
+        act(R("qa"), R("df"), ACT.Abs, bias=2.0 ** -25 - 0.25)
+        ts(R("dd"), R("qa"), 0.25, ALU.is_gt)
         tt(R("FR", 96, 192), R("FR", 96, 192), R("dd"), ALU.add)
 
-    lin(R("s", 0, 96), P(7, 0, 96), bias=C(2))
-    lin(R("s", 96, 192), P(3, 96, 192), bias=C(2))
-    ts(R("t2"), R("s"), float(H), ALU.is_ge, -(V - 1.0), ALU.mult)
-    lin(R("t3"), R("s"), bias=1.0, scale=2.0)
-    ts(R("t4"), R("s"), float(GO), ALU.is_lt, 8192.0, ALU.mult)
-    lin(R("t5"), R("s"), bias=float(V - GO + 1))
-    tt(R("t2"), R("t2"), R("t3"), ALU.add)
-    tt(R("t4"), R("t4"), R("t5"), ALU.add)
-    tt(R("t2"), R("t2"), R("t4"), ALU.min)
-    for b in range(2):
-        lo, hi = 96 * b, 96 * b + 96
-        lin(R("t6", lo, hi), R("FR", lo, hi), scale=float(GO))
-        tt(R("fn", lo, hi), R("t6", lo, hi), R("phi", lo, hi), ALU.max)
-        cp(R("yo", lo, hi), R("fn", lo, hi))
-    lin(R("t3"), R("FR"), bias=1.0, scale=-1.0)
-    tt(R("t5"), R("t2"), R("t3"), ALU.mult)
+    mm([(P(5, 96, 192), Im, R("c16", 96, 192)), (P(5, 96, 192), R("IB"), R("FR", 96, 192))])
+    ts(R("yo"), P(5, 96, 192), C(19), ALU.add, float(GO - H), ALU.min)
     for h in range(2):
-        mm([(P(3, 96 * h, 96 * h + 96), R("T3", 136 * h + 1 - b, 136 * h + 129 - b), R("t5", 96 * b, 96 * b + 96)) for b in range(2)])
+        o = P(7, 96 * h, 96 * h + 96)
+        mm([(o, R("I32"), R("phn", 96 * h, 96 * h + 96))] + [(o, sel(p, "T2"), R("Q", 8 * h + p // 2, H, 16)) for p in range(0, 16, 2)]
+           + [(o, sel(p, "T2"), R("NW", OD * (p % 2) + 8 * h + p // 2, OD * (p % 2) + H, 16)) for p in range(16)])
+    ts(R("t3"), P(7, 0, 192), float(OD), ALU.is_ge, 1.0 - 2 * OD, ALU.mult)
+    ts(R("t4"), P(7, 0, 192), float(GO), ALU.is_ge, float(V + 2 * OD - 1 - 2 * GO), ALU.mult)
+    ts(R("t5"), P(7, 0, 192), float(GO), ALU.max, -1.0, ALU.mult)
+    lin(R("t2"), P(7, 0, 192), bias=float(GO), scale=2.0)
+    mm([(P(3, 0, 192), R("I32"), R(n)) for n in ("t3", "t4", "t5", "t2")], stop=False)
+    mm([(P(3, 96 * h, 96 * h + 96), R("T4", 136 * h + 1 - b, 136 * h + 129 - b), R("FR", 96 * b, 96 * b + 96)) for h in range(2) for b in range(2)], start=False)
     for h in range(2):
-        lin(R("ynb", h, 192, 2), P(3, 96 * h, 96 * h + 96), bias=-1.0)
-    dma("s", lambda: T.yn[:], R("ynb"), 2500.0)
-    NQ = 6
-    w = V // NQ
-    for b in range(2):
-        for k in range(NQ):
-            copy(R("Y", w * k + b, w * k + w, 2), [R("X3"), R("yo", 96 * b + w // 32 * k, 96 * b + w // 32 * (k + 1))])
+        ts(R("ynb", h, 192, 2), P(3, 96 * h, 96 * h + 96), -1.0, ALU.max)
+    dma("s", lambda: T.yn[:], R("ynb"))
     for k in range(NQ):
-        dma("s", lambda k=k: T.yx[:, w * k:w * k + w], R("Y", w * k, w * k + w), 2600.0)
+        w = V // NQ
+        copy(R("Y", w * k + 1, w * k + w, 2), [R("X3", H, XW), R("yo", w // 32 * k, w // 32 * (k + 1))])
+    cp([R("Y"), R("ifo", 40, 80)], R("XV"))
+    for k in range(2):
+        dma("sa"[k], lambda k=k: T.yx[:, H * k:H * k + H], R("Y", H * k, H * k + H))
     return ops
 
 
 def depend(ops):
     acc, deps, last = {}, [], {}
     for i, op in enumerate(ops):
-        d = set(op[7])
-        for rs, w in ((op[3], False), (op[4], True)):
+        d = {j: "order" for j in op[4]}
+        for rs, w in ((op[1], False), (op[2], True)):
             for r in rs:
                 for j, x, w2 in acc.get(r[0], ()):
                     if r[0] not in SB:
-                        if (w or w2 or ops[j][0] != op[0]) and not (op[0] == "p" and ops[j][0] == "p"):
-                            d.add(j)
+                        if not ("p" in op[0] and "p" in ops[j][0]):
+                            d[j] = "data" if w or w2 else d.get(j, "bank")
                     elif (w or w2) and x[1] < r[2] and r[1] < x[2] and not (x[3] == r[3] and (x[1] - r[1]) % r[3]):
-                        d.add(j)
-        for rs, w in ((op[3], False), (op[4], True)):
+                        d[j] = "data"
+        for rs, w in ((op[1], False), (op[2], True)):
             for r in rs:
                 acc.setdefault(r[0], []).append((i, r, w))
-        if op[0] == "p":
-            if op[4][0][0] in last:
-                d.add(last[op[4][0][0]])
-            last[op[4][0][0]] = i
-        d.discard(i)
+        if "p" in op[0]:
+            if op[2][0][0] in last:
+                d.setdefault(last[op[2][0][0]], "order")
+            last[op[2][0][0]] = i
+        d.pop(i, None)
         deps.append(d)
     return deps
+
+
+def arrange(ops, deps):
+    at = {op[5]: i for i, op in enumerate(ops)}
+    todo = {q: [at[w] for w in s.split()][::-1] for q, s in PLAN.items()}
+    order, on = [], {}
+    while len(order) < len(ops):
+        q = next(q for q in todo if todo[q] and all(j in on for j in deps[todo[q][-1]]))
+        order.append(todo[q].pop())
+        on[order[-1]] = q
+    return order, on
 
 
 def rank_program(g, core, T, topo):
@@ -468,38 +640,37 @@ def rank_program(g, core, T, topo):
         return
     ops = build(g, T, topo, core, rank)
     deps = depend(ops)
-    order = [int(ORDER[k:k + 2], 36) for k in range(0, len(ORDER), 2)] or list(range(len(ops)))
-    assert sorted(order) == list(range(len(ops)))
+    order, on = arrange(ops, deps)
     Q = {"v": g.vector, "a": g.scalar, "p": g.tensor, "g": g, "s": g.sync}
     mark, total, seen, nd = {}, {}, {q: {} for q in Q}, 0
     at, knew, by = {i: k for k, i in enumerate(order)}, {}, {}
     for i in order:
-        op = ops[i]
-        q = op[0]
+        op, q = ops[i], on[i]
         for j in sorted(deps[i], key=lambda j: -at[j]):
             s, v = mark[j]
-            if seen[q].get(s, 0) >= v or (ops[j][0] == q and (q == "p" or j in op[7])):
+            if seen[q].get(s, 0) >= v or (on[j] == q and (q == "p" or deps[i][j] != "data")):
                 continue
             Q[q].wait_ge(T.sem[s], v)
             for x, y in list(knew[by[s, v]].items()) + [(s, v)]:
                 seen[q][x] = max(seen[q].get(x, 0), y)
-        knew[i] = dict(seen[q]) if op[6] in ("c", "dma") else {}
-        ins = op[5]()
-        if op[6] == "c":
+        knew[i] = dict(seen[q]) if op[3] in ("c", "dma") else {}
+        ins = op[0][q]()
+        if op[3] == "c":
             s = "c" + q
             total[s] = total.get(s, 0) + 1
             ins.then_inc(T.sem[s], 1)
             mark[i] = (s, total[s])
-        elif op[6] == "dma":
+        elif op[3] == "dma":
             s = "d%d" % nd
             nd += 1
-            total[s] = 16
-            ins.then_inc(T.sem[s], 16)
-            mark[i] = (s, 16)
+            total[s] = 16 * len(ins)
+            for x in ins:
+                x.then_inc(T.sem[s], 16)
+            mark[i] = (s, total[s])
         else:
-            mark[i] = op[6]
-            total[op[6][0]] = op[6][1]
-            total["sent"] = total.get("sent", 0) + op[6][1]
+            mark[i] = op[3]
+            total[op[3][0]] = op[3][1]
+            total["sent"] = total.get("sent", 0) + op[3][1]
         by[mark[i]] = i
     for s in sorted(total):
         if seen["g"].get(s, 0) < total[s]:

@@ -13,104 +13,71 @@ BIG = float(2 ** 20)
 bf, f32, i32, u16 = "bfloat16", "float32", "int32", "uint16"
 
 SB = {
-    "xr": (V + 16, bf), "X0": (XW, bf), "X1": (XW, bf), "X2": (XW, bf), "X3": (XW, bf), "Y": (V + 2 * CAP, bf), "XB": (JK, bf),
+    "xr": (V + 16, bf), "X0": (XW, bf), "X1": (XW, bf), "X2": (XW, bf), "X3": (XW, bf), "Y": (V + 2 * CAP, bf), "XB": (H, bf),
     "D": (XW, bf), "NW": (GO, bf), "A": (JK, bf), "AJ": (H, bf), "C": (JK, bf), "Q": (H, bf), "W": (WW, bf), "Ut": (H, bf),
     "KI0": (KWW, f32), "KI1": (KWW, f32), "KF0": (KWW, f32), "KF1": (KWW, f32),
     "kI": (640, bf), "kF": (640, bf), "WI": (192, f32), "WF": (192, f32), "SI": (208, bf), "SF": (208, bf),
     "DD": (640, bf), "uI": (8, f32), "uF": (8, f32), "vI": (8, f32), "vF": (8, f32),
     "cI": (8, u16), "cF": (8, u16), "J0": (40, bf), "PM": (80, f32), "ifo": (80, u16),
-    "tot": (8, f32), "far": (192, bf), "FR": (192, bf), "dd": (96, bf), "sh": (96, bf), "m2": (96, f32), "moff": (96, u16),
-    "soff": (192, u16), "aoff": (96, u16), "dj": (96, f32), "HH": (272, f32), "rn": (96, f32), "df": (96, f32), "qa": (96, f32),
-    "zc": (96, f32), "c1": (192, bf), "c2": (192, bf), "e2": (320, bf), "yy": (320, f32), "hh": (320, bf), "e1": (320, bf), "em": (320, bf), "si": (320, bf), "G": (320, bf),
-    "XV": (640, bf), "NV": (640, bf), "S0": (192, bf), "S1": (192, bf), "S2": (192, bf),
-    "ni": (192, i32), "hi": (12, i32), "h0": (12, u16), "h1": (12, u16),
-    "ti": (4 * 192, i32), "dg": (8 * 192, bf), "Z": (2 * 192, bf),
-    "t2": (192, f32), "t3": (192, f32), "t4": (192, f32), "t5": (192, f32), "yo": (96, u16), "ynb": (192, f32),
-    "iu": (144, bf), "M0": (144, bf), "pi": (8, i32), "col": (40, f32), "E": (16, f32), "Tm": (144, bf), "T2": (144, bf), "T5": (144, bf),
-    "Bm": (128, bf), "Tri": (128, bf), "Im": (144, bf), "Ni": (128, bf), "N4": (128, bf), "IB": (128, bf), "I32": (128, f32),
-    "A0": (128, bf), "ab": (128, bf), "w0": (128, bf), "w1": (128, bf), "w2": (3 * 128, bf), "on": (144, bf),
-    "Pb": (272, bf), "T3": (272, bf), "T4": (272, bf), "c16": (192, bf), "c128": (192, bf), "phn": (192, f32),
-    "nn": (40, f32), "jn": (80, f32), "ca": (16, bf), "inc": (960, f32),
-    "O6": (144, bf), "O7": (144, bf), "O8": (144, bf), "BP": (128, bf),
-    "M1": (128, bf), "M2": (128, bf), "pw": (96, f32), "bas": (192, bf), "RR": (96, f32),
+    "tot": (8, f32), "far": (192, bf), "FR": (192, bf), "dd": (96, i32), "sh": (96, bf), "m2": (96, f32), "moff": (96, u16),
+    "soff": (192, u16), "aoff": (96, u16), "dj": (96, f32), "HH": (272, f32), "rn": (96, i32), "zc": (96, f32),
+    "c1": (192, bf), "c2": (192, bf), "yy": (320, f32), "hh": (320, bf), "e1": (320, f32), "em": (320, bf), "si": (320, bf),
+    "G": (320, bf), "XV": (640, bf), "NV": (640, bf), "S0": (192, bf), "S1": (192, bf), "S2": (192, bf),
+    "ni": (192, i32), "hi": (12, i32), "h0": (12, u16), "h1": (12, u16), "ti": (4 * 192, i32), "dg": (8 * 192, bf), "Z": (2 * 192, bf),
+    "t2": (192, f32), "t3": (192, bf), "t4": (192, bf), "t5": (192, bf), "yo": (96, u16), "ynb": (192, f32),
+    "iu": (144, bf), "M0": (144, bf), "pi": (8, i32), "col": (40, f32), "E": (16, f32), "on": (144, bf),
+    "Tm": (144, bf), "Tn": (144, bf), "T2": (144, bf), "T5": (144, bf), "Pb": (272, bf), "T3": (272, bf), "T4": (272, bf),
+    "Bm": (128, bf), "Bh": (128, bf), "Tri": (128, bf), "Im": (144, bf), "Ni": (128, bf), "N4": (128, bf), "IB": (128, bf),
+    "Na": (128, bf), "Nb": (128, bf), "I32": (128, f32), "A0": (128, bf), "ab": (128, bf), "w0": (128, bf), "w1": (128, bf),
+    "w2": (3 * 128, bf), "c16": (192, bf), "c128": (192, bf), "phn": (192, f32), "nn": (40, f32), "jn": (80, f32), "ca": (16, bf),
+    "inc": (960, f32), "O6": (144, bf), "O7": (144, bf), "O8": (144, bf), "BP": (128, bf), "M1": (128, bf), "M2": (128, bf),
+    "pw": (96, f32), "bas": (192, bf), "RR": (96, f32),
 }
 SCRATCH = {k: ("sbuf", [128, n], d) for k, (n, d) in SB.items()}
 for _b in (0, 1, 2, 3, 4, 5, 7):
     SCRATCH["P%d" % _b] = ("psum", [128, 512], f32)
 SCRATCH["P6"] = ("psum", [128, 1024], bf)
-NDMA = 56
+NDMA = 48
 SEMAPHORES = ["cv", "ca", "cp", "cg", "sent", "arr0", "arr1", "arr2"] + ["d%d" % i for i in range(NDMA)]
 ALU, ACT = AluOpType, ActivationFunctionType
 MAGIC = 12582912.0
 MT = 440.5 * 4096 - BIG
-CUT = ((OD, OD + 768, "t"), (OD + 768, JK, "t"), (0, 768, "d"), (768, H, "d"))
-LEN = ((OD, JK), (0, 768), (768, H))
-NVA = False
+EVEN = ((0, 768), (768, 1280), (1280, H))
+LEN0 = ((OD, JK, 0), (0, 768, 0), (768, H, 0))
+LEN1 = ((OD, JK, 1), (0, 768, 0), (768, H, 1))
 NQ = 4
 PLAN = {
-    "v": "sD.0 spw.0 spi.2 spi.4 spi.5 sxr.2 spi.3 spi.1 spi.6 sSI.0 scol.0 spw.2 scol.1 sti.0 sE.0 scol.18 sSF.0 sh0.0 sbas.6 sM0.0 sti.3 "
-         "sbas.4 sti.1 sdg.2 sPb.0 sIm.0 sdg.7 sti.2 sdg.4 sPb.1 sdg.6 sdg.3 sdg.5 scol.4 syo.0 spw.1 sbas.7 sD.1 sbas.2 sT3.1 sFR.0 sBm.0 "
-         "scol.19 sT3.0 sBP.0 sw0.0 sh1.0 sI32.0 sbas.5 sD.3 ssoff.1 spw.3 ssoff.0 sTm.0 0SF.0 saoff.0 0SF.1 scol.20 0D.4 0D.1 0D.0 snn.1 "
-         "sZ.0 scol.9 sjn.0 0uF.0 sN4.0 0WF.0 sA0.0 0vF.0 sNW.2 0cF.0 0C.1 sW.4 0C.0 0KF1.0 0far.0 sw1.0 0SI.1 0SI.0 0kF.1 sNW.3 0uI.0 "
-         "scol.22 0vI.0 0WI.0 0cI.0 0KF0.0 0KI0.0 0kF.0 0zc.0 0kI.0 0m2.0 0tot.0 0m2.1 0FR.0 0moff.0 0kI.1 0J0.0 0D.7 0D.6 0D.8 0C.3 0PM.0 "
-         "0C.4 0ifo.0 0C.2 0yy.0 0NV.1 0hh.0 0e2.0 0S1.0 0e1.0 0NW.0 0XV.0 0NW.1 0X1.6 0X1.7 0soff.1 0Ut.1 sw2.1 0soff.0 1D.0 1D.1 0HH.0 "
-         "0HH.1 0aoff.0 0rn.0 sT4.0 0df.0 scol.11 0dd.0 0FR.1 0dj.0 1SF.0 1SF.1 1far.0 sjn.1 1SI.0 1uF.0 1SI.1 1vF.0 1WF.0 1cF.0 sw2.2 "
-         "1KF0.0 1KF1.0 1uI.0 1kF.0 1vI.0 1zc.0 1kF.1 1cI.0 1m2.0 1tot.0 1m2.1 1J0.0 1moff.0 1kI.1 1kI.0 1D.7 1D.6 1FR.0 1D.8 1C.2 1PM.0 "
-         "1NV.0 1ifo.0 1C.4 1NV.1 1S2.0 1hh.0 1NW.0 1e1.0 1XV.0 1e2.0 1NW.1 1X2.6 1X2.7 1soff.1 2D.2 1soff.0 1aoff.0 2D.0 2D.1 1HH.0 1HH.1 "
-         "1rn.0 1df.0 1dj.0 2C.1 1dd.0 1FR.1 2C.0 2SF.0 2SF.1 2far.0 2SI.0 2uF.0 2SI.1 2vF.0 2cF.0 2KF0.0 2KF1.0 2kF.0 2vI.0 2kF.1 2cI.0 "
-         "2m2.0 2moff.0 2tot.0 2kI.1 2kI.0 2D.6 2Ut.0 2FR.0 2J0.0 2D.7 2Ut.1 2D.8 2PM.0 2ifo.0 2Ut.2 2NV.1 2NW.0 2HH.0 2HH.1 2NW.1 2rn.0 "
-         "2df.0 2hh.0 2dd.0 2PM.1 2FR.1 2e1.0 2XV.0 2yo.0 2ifo.1 2Y.6 2Y.4 2t3.0 2t4.0 2t5.0 2t2.0 2Y.7 2ynb.0 2ynb.1",
-    "a": "sni.0 shi.0 scol.13 scol.14 scol.2 scol.3 scol.16 scol.15 scol.12 scol.21 sbas.1 sS0.0 sX0.1 scol.5 sbas.3 scol.8 sNi.0 sab.0 "
-         "scol.6 sX0.2 sX0.6 sX0.5 sbas.0 sca.1 0D.2 sdj.0 sW.2 sW.3 0A.1 0A.0 sIB.0 0A.2 0A.3 sNW.4 0AJ.0 sNW.6 0sh.0 0AJ.1 0AJ.2 0KI1.0 "
-         "scol.7 sNW.5 0Q.0 0DD.0 0DD.1 0Q.1 sRR.3 sNW.7 0c1.0 0NV.0 0c2.0 0em.0 0X1.2 0si.0 0Q.2 0X1.3 0X1.4 scol.10 0XV.1 0Ut.0 sRR.2 "
-         "sRR.0 scol.17 sRR.1 sphn.1 1D.2 1D.4 0Ut.2 1A.0 1A.1 1A.2 0qa.0 1A.3 1AJ.1 1AJ.0 1sh.0 1AJ.2 1WI.0 1C.1 1C.0 1KI1.0 1KI0.0 1DD.0 "
-         "1Q.1 1Q.2 1DD.1 1Q.0 1C.3 1c1.0 1c2.0 1yy.0 1X2.2 1em.0 1si.0 1X2.4 1X2.3 1XV.1 1Ut.0 2D.4 1Ut.1 1Ut.2 2A.0 2A.1 2A.2 1qa.0 2A.3 "
-         "2AJ.0 2AJ.1 2WF.0 2AJ.2 2uI.0 2WI.0 2sh.0 2KI1.0 2KI0.0 2Q.0 2DD.0 2Q.1 2DD.1 2Q.2 2C.2 2NV.0 2C.4 2Y.0 2yy.0 2C.3 2qa.0 2em.0 "
-         "2si.0 2Y.1 2Y.2 2Y.3 2Y.5 2XV.1 2out.2",
-    "p": "sP4.0 sP4.1 sP4.2 sP7.0 sP5.0 sP3.0 sP0.0 sP1.0 sP3.1 0P2.0 0P7.0 sP0.1 sP1.1 0P3.0 sP1.2 0P3.1 0P3.2 sP1.3 sP0.2 0P5.0 0P1.0 "
-         "sP0.3 0P4.0 0P1.1 0P4.1 0P5.1 0P4.2 0P2.1 0P2.2 0P7.1 sP0.4 0P3.3 0P5.2 0P2.3 0P0.0 0P6.0 0P1.2 0P0.1 0P3.4 0P7.2 0P7.3 0P6.1 "
-         "0P4.3 0P5.3 0P6.2 0P4.4 0P4.5 0P4.6 1P3.0 1P3.1 1P3.2 1P7.0 1P2.0 1P1.0 1P5.0 1P4.0 1P1.1 1P4.1 1P4.2 1P5.1 1P7.1 1P2.1 1P3.3 "
-         "1P2.2 1P5.2 1P2.3 1P0.0 1P6.0 1P1.2 1P0.1 1P7.2 1P3.4 1P7.3 1P4.3 1P6.1 1P5.3 1P6.2 1P4.4 1P4.5 1P4.6 2P3.0 2P3.1 2P3.2 2P7.0 "
-         "2P2.0 2P1.0 2P5.0 2P4.0 2P4.1 2P4.2 2P2.1 2P5.1 2P2.2 2P7.1 2P6.0 2P3.3 2P6.1 2P4.3 2P5.2 2P2.3 2P6.2 2P4.4 2P0.0 2P4.5 2P5.3 "
-         "2P0.1 2P4.6 2P1.1 2P7.2 2P5.4 2P7.3 2P3.4 2P3.5 2P3.6",
-    "g": "spi.0 siu.0 sdg.0 sca.0 sdg.1 son.0 sc16.0 sW.0 sO8.0 sX0.0 sD.2 sc128.0 sO6.0 sX0.3 sTri.0 sO7.0 sW.1 sM2.0 snn.0 sM2.1 sKF0.0 "
-         "0D.3 0D.5 sinc.0 sNW.0 sM1.0 sT5.0 sM1.1 sM2.2 sw2.0 sM1.2 sM2.3 sM2.4 sM1.3 sM2.5 sT2.0 sM2.6 sM1.4 sM2.7 sM1.5 sM1.6 sM1.7 "
-         "sHH.0 sM1.8 sphn.0 sM1.9 sinc.1 sM1.10 0X1.1 0X1.5 sinc.2 sM2.8 sM2.9 sM1.11 sT5.1 sM2.10 sM2.11 1D.3 1D.5 0NW.2 1X2.1 1X2.5 "
-         "2D.3 2D.5 1NW.2 2X3.1",
-    "s": "sxr.0 sxr.1 sX0.4 sKI1.0 sNW.1 sKF1.0 sX1.0 0X1.0 sKI0.0 sW.5 sX3.0 0W.0 0XB.0 sX2.0 0XB.1 1X2.0 sX3.1 1XB.0 1XB.1 1W.0 2X3.0 "
-         "2out.1 2out.0",
-}
-OLD1 = {
-    "v": "sD.0 son.0 spi.6 spi.5 spi.2 spi.4 spi.1 spi.3 scol.0 spw.0 scol.5 sh0.0 sM0.0 sdg.4 scol.3 sti.0 sti.3 sti.2 sdg.7 sE.0 sPb.0 "
-         "sdg.2 sdg.6 sti.1 sdg.3 sIm.0 scol.19 sPb.1 sdg.5 sSI.0 sTm.0 sT3.1 sT3.0 spw.2 syo.0 sBm.0 sFR.0 sbas.4 sW.0 sX0.5 0SF.0 sBP.0 "
-         "ssoff.0 ssoff.1 0D.0 0D.1 0D.4 scol.9 sA0.0 sIB.0 0SF.1 sca.1 sNW.2 saoff.0 sdj.0 sw0.0 0C.1 0D.2 0WF.0 0D.3 sW.4 0uF.0 0C.0 "
-         "0vF.0 0cF.0 sNW.4 sw1.0 sW.1 spw.1 scol.20 sjn.0 0far.0 0SI.1 0SI.0 scol.6 sNW.3 0kF.1 0kF.0 0m2.0 0vI.0 0moff.0 0cI.0 0DE.2 "
-         "0kI.1 0tot.0 0kI.0 0FR.0 0J0.0 0DE.0 0DE.1 scol.22 spw.3 0PM.0 0C.4 0C.2 0ifo.0 sNW.7 0C.3 0NV.1 0hh.0 sh1.0 0NW.0 0e1.0 0XV.0 "
-         "0NW.1 0X1.5 0S1.0 0X1.7 0soff.0 sRR.2 0soff.1 sw2.1 sRR.1 0aoff.0 0HH.0 0HH.1 1D.0 1D.1 0rn.0 1D.4 0df.0 1D.2 1D.3 0dd.0 0FR.1 "
-         "1C.0 sjn.1 1SF.1 1SF.0 1far.0 1SI.0 1WF.0 1SI.1 scol.11 1uF.0 1vF.0 1cF.0 1KF1.0 1vI.0 1cI.0 1kF.1 1kF.0 1kI.0 1m2.0 1tot.0 "
-         "1moff.0 1kI.1 1J0.0 1DE.2 1DE.0 1DE.1 1PM.0 1C.2 1ifo.0 1C.3 1FR.0 1yy.0 1C.4 1hh.0 sw2.2 1si.0 1e1.0 1XV.0 1NV.1 1X2.5 1NW.0 "
-         "1X2.7 1NW.1 1Ut.2 1soff.0 1HH.0 1HH.1 2D.1 1soff.1 1rn.0 2D.0 1df.0 2D.2 2D.3 2D.4 1dd.0 1aoff.0 1FR.1 2SF.0 1dj.0 2SF.1 2far.0 "
-         "2WF.0 2SI.0 2uF.0 2SI.1 2vF.0 2cF.0 2uI.0 2vI.0 2kF.0 2cI.0 2tot.0 2kF.1 2kI.0 2m2.0 2kI.1 2moff.0 2FR.0 2J0.0 2DE.0 2DD.1 2DE.1 "
-         "2Ut.0 2DE.2 2PM.0 2ifo.0 2C.0 2NV.1 2C.2 2NW.0 2HH.0 2HH.1 2NW.1 2rn.0 2df.0 2hh.0 2PM.1 2dd.0 2FR.1 2yo.0 2e1.0 2Y.2 2XV.0 2Y.4 "
-         "2t3.0 2t4.0 2ifo.1 2t5.0 2Y.7 2ynb.0 2ynb.1",
-    "a": "sni.0 shi.0 scol.1 scol.15 scol.2 scol.16 sS0.0 scol.4 scol.12 sX0.1 sab.0 scol.8 sX0.2 sbas.7 scol.18 sNi.0 sbas.6 sX0.6 sbas.1 "
-         "scol.13 sN4.0 sbas.0 sbas.2 sbas.3 sbas.5 snn.1 sZ.0 scol.14 0A.0 sW.3 0A.1 0A.4 sW.2 0AJ.0 0AJ.1 0A.2 scol.21 0AJ.2 scol.10 "
-         "0A.3 0KF0.0 0KF1.0 0sh.0 sNW.6 scol.7 0uI.0 0WI.0 0KI1.0 0KI0.0 sNW.5 0DD.0 0Q.0 0DD.1 0Q.1 0Q.2 0NV.0 0yy.0 sT4.0 0em.0 0X1.2 "
-         "0si.0 0X1.3 0X1.4 sRR.0 sRR.3 0XV.1 0Ut.0 0Ut.1 0Ut.2 sI32.0 1A.0 0dj.0 1A.1 scol.17 1A.4 0qa.0 1A.2 1A.3 1AJ.1 1AJ.0 1AJ.2 "
-         "1WI.0 1uI.0 1sh.0 1KF0.0 1KI0.0 1KI1.0 1C.1 1DD.0 1Q.0 1DD.1 1Q.2 1Ut.0 1Q.1 sphn.1 1X2.2 1em.0 1NV.0 1X2.3 1X2.4 1XV.1 1S2.0 "
-         "1Ut.1 2A.1 2C.1 1qa.0 2A.0 2A.2 2A.3 2A.4 2AJ.0 2AJ.2 2AJ.1 2KF0.0 2KF1.0 2WI.0 2KI0.0 2sh.0 2KI1.0 2Q.0 2DD.0 2Q.1 2Q.2 2Ut.1 "
-         "2NV.0 2Ut.2 2C.3 2yy.0 2C.4 2Y.0 2qa.0 2em.0 2si.0 2Y.1 2Y.5 2Y.6 2Y.3 2XV.1 2t2.0 2out.2",
-    "p": "sP4.0 sP4.1 sP4.2 sP5.0 sP7.0 sP3.0 sP3.1 sP1.0 sP0.0 sP1.1 0P3.0 0P2.0 sP0.1 0P7.0 sP1.2 0P3.1 0P4.0 0P2.1 0P3.2 sP0.2 0P4.1 "
-         "sP1.3 0P5.0 0P4.2 0P1.0 0P2.2 sP0.3 0P5.1 0P7.1 0P3.3 sP0.4 0P5.2 0P2.3 0P6.0 0P7.2 0P0.0 0P1.1 0P0.1 0P3.4 0P5.3 0P6.1 0P7.3 "
-         "0P6.2 0P4.3 0P4.4 0P4.5 0P4.6 1P3.0 1P3.1 1P3.2 1P2.0 1P7.0 1P1.0 1P5.0 1P4.0 1P5.1 1P4.1 1P4.2 1P7.1 1P3.3 1P2.1 1P6.0 1P2.2 "
-         "1P5.2 1P0.0 1P2.3 1P1.1 1P4.3 1P0.1 1P3.4 1P6.1 1P7.2 1P4.4 1P6.2 1P5.3 1P4.5 1P7.3 1P4.6 2P3.0 2P3.1 2P3.2 2P2.0 2P7.0 2P2.1 "
-         "2P5.0 2P2.2 2P1.0 2P5.1 2P4.0 2P4.1 2P4.2 2P7.1 2P3.3 2P6.0 2P5.2 2P2.3 2P6.1 2P4.3 2P6.2 2P4.4 2P5.3 2P4.5 2P0.0 2P4.6 2P1.1 "
-         "2P7.2 2P5.4 2P0.1 2P7.3 2P3.4 2P3.5 2P3.6",
-    "g": "spi.0 snn.0 sSF.0 siu.0 sc16.0 sdg.1 sdg.0 sKF0.0 sX0.0 sca.0 sxr.2 sT5.0 sO6.0 sD.2 sO7.0 sX0.3 sO8.0 sD.1 sM1.0 sM1.1 sphn.0 "
-         "sTri.0 sM1.2 sc128.0 sT2.0 sM1.3 sM2.0 sNW.0 sinc.0 sM2.1 sM2.2 sM2.3 sinc.2 sM2.4 sM2.5 sM1.4 sM2.6 sM1.5 sM2.7 sinc.1 sT5.1 "
-         "sM1.6 sM2.8 sM1.7 0X1.1 sM1.8 sM1.9 sM2.9 sw2.0 sM1.10 sM1.11 0X1.6 sM2.10 sM2.11 sHH.0 0NW.2 1X2.1 1X2.6 1NW.2 2X3.1",
-    "s": "sxr.1 sxr.0 sX0.4 sKI1.0 sX2.0 sX3.1 sXB.2 sKF1.0 sKI0.0 sNW.1 sX1.0 sXB.0 sXB.1 0X1.0 sW.5 0XB.0 0XB.1 0XB.2 1X2.0 0XB.4 0XB.3 "
-         "0W.0 1XB.1 sX3.0 1XB.3 1W.0 1XB.4 1XB.0 2X3.0 1XB.2 2out.1 2out.0",
+    "v": "sD.0 spi.4 spi.2 spi.1 spi.6 spi.3 spi.5 spw.1 scol.0 sSF.0 spw.2 sM0.0 sE.0 sdg.4 sIm.0 sti.0 sdg.2 sti.3 sh0.0 sti.1 sPb.1 "
+         "sti.2 sPb.0 sdg.7 sdg.5 sdg.3 sdg.6 sT3.0 sT3.1 syo.0 sG.0 sTm.0 sBm.0 sh1.0 spw.3 sbas.3 ssoff.0 scol.18 sbas.0 sNb.0 sD.1 "
+         "scol.19 sX0.6 ssoff.1 scol.20 saoff.0 sA0.0 sBP.0 sN4.0 scol.22 0SF.0 sw0.0 sdj.0 sw1.0 0D.1 0SF.1 0D.0 0D.2 0D.4 0D.3 sNW.2 "
+         "0uF.0 sjn.0 0C.0 sNW.4 sw0.1 sI32.0 0vF.0 sNi.0 0far.0 0cF.0 0SI.1 0SI.0 sBh.0 sNW.6 0WF.0 0uI.0 0KF1.0 0vI.0 0KF0.0 0cI.0 0kF.1 "
+         "0kF.0 0m2.0 0tot.0 0zc.0 0KI0.0 0m2.1 0kI.0 0moff.0 0J0.0 0kI.1 0D.5 0DD.1 0D.6 0D.7 0FR.0 0C.3 0PM.0 0Ut.0 0ifo.0 0C.4 0yy.0 "
+         "0NV.0 0S1.0 0NW.0 0hh.0 0NW.1 0si.0 0e1.0 0X1.6 0soff.0 0X1.7 0HH.0 0HH.1 1A.1 0rn.0 0soff.1 0aoff.0 0dd.0 0dj.0 0FR.1 sT4.0 "
+         "1SF.0 1SF.1 1D.3 1A.5 1A.3 1D.4 1uF.0 1D.5 1A.7 1A.8 sw2.1 1WF.0 1C.0 1vF.0 1cF.0 1far.0 1SI.0 1SI.1 1kF.0 1kF.1 sjn.1 1uI.0 "
+         "1m2.0 1vI.0 1zc.0 1cI.0 1m2.1 1tot.0 1moff.0 1J0.0 1kI.0 1kI.1 1D.6 1D.7 1Ut.0 1C.3 1D.8 1PM.0 1FR.0 1ifo.0 1Ut.1 1yy.0 1S2.0 "
+         "1hh.0 1Ut.2 1NW.0 1e1.0 1NW.1 1X2.6 1HH.0 1X2.7 1soff.0 1HH.1 2A.2 1rn.0 1soff.1 1dd.0 1aoff.0 1FR.1 1dj.0 2SF.0 2SF.1 2D.3 2A.3 "
+         "2A.4 2A.5 2D.4 2D.5 2A.7 2A.8 2vF.0 2WF.0 2cF.0 sw2.2 2C.0 2far.0 2kF.0 2SI.0 2m2.0 2SI.1 2moff.0 2kF.1 2D.6 2vI.0 2WI.0 2cI.0 "
+         "2Ut.0 2kI.1 2kI.0 2tot.0 2C.2 2D.7 2J0.0 2D.8 2FR.0 2PM.0 2HH.0 2ifo.0 2HH.1 2yy.0 2PM.1 2rn.0 2hh.0 2dd.0 2ifo.1 2FR.1 2NW.0 "
+         "2yo.0 2NW.1 2Y.6 2Y.5 2e1.0 2Y.7 2Y.8 2t3.0 2t4.0 2t5.0 2ynb.0 2ynb.1",
+    "a": "sni.0 shi.0 scol.1 scol.12 scol.5 scol.14 spw.4 scol.15 scol.2 scol.3 sbas.1 sbas.2 scol.16 sNa.0 sbas.4 scol.13 sS0.0 scol.4 "
+         "scol.6 scol.9 sbas.7 scol.21 sab.0 sca.1 scol.8 sX0.2 sbas.5 sX0.5 sbas.6 sFR.0 sIB.0 sX0.1 snn.1 spw.5 sZ.0 sRR.1 scol.7 sW.2 "
+         "0A.1 sW.3 0A.0 sW.4 0A.2 0A.4 0A.3 0AJ.1 0AJ.0 0C.1 sNW.3 0WI.0 0sh.0 0KI1.0 sNW.5 0DD.0 0Q.0 0Q.1 0Q.2 0C.2 0c1.0 sNW.7 0c2.0 "
+         "0NV.1 0Ut.1 0XV.0 0X1.4 0Ut.2 0XV.1 sTn.0 0em.0 scol.17 scol.10 sphn.1 sRR.3 sRR.2 sRR.0 1A.0 1A.2 1D.0 1D.1 1D.2 1A.4 1A.6 "
+         "1AJ.0 1AJ.1 1KF0.0 1KF1.0 scol.11 1sh.0 1WI.0 1C.1 1KI0.0 1KI1.0 1DD.0 1Q.0 1Q.1 1DD.1 1C.2 1Q.2 1c1.0 1c2.0 1NV.1 1NV.0 1C.4 "
+         "1XV.0 1si.0 1X2.4 1em.0 1XV.1 2A.0 2A.1 2D.2 2D.0 2D.1 2uF.0 2A.6 2AJ.1 2AJ.0 2KF0.0 2KF1.0 2sh.0 2C.1 2Q.0 2uI.0 2Q.1 2KI1.0 "
+         "2KI0.0 2Q.2 2Ut.1 2DD.0 2DD.1 2Ut.2 2C.3 2C.4 2XV.0 2NV.0 2NV.1 2Y.0 2Y.1 2si.0 2Y.2 2Y.3 2Y.4 2XV.1 2em.0 2t2.0 2out.2",
+    "p": "sP4.0 sP4.1 sP4.2 sP5.0 sP3.0 sP7.0 sP3.1 sP0.0 sP1.0 sP0.1 0P7.0 sP1.1 0P3.0 sP1.2 0P3.1 0P3.2 sP1.3 0P2.0 sP0.2 0P5.0 0P1.0 "
+         "0P4.0 0P5.1 0P4.1 0P1.1 0P7.1 sP0.3 0P2.1 0P2.2 0P3.3 0P6.0 sP0.4 0P5.2 0P7.2 0P2.3 0P6.1 0P4.2 0P0.0 0P4.3 0P6.2 0P3.4 0P5.3 "
+         "0P4.4 0P7.3 0P4.5 1P0.0 1P1.0 1P5.0 1P7.0 1P2.0 1P3.0 1P3.1 1P3.2 1P3.3 1P3.4 1P4.0 1P1.1 1P5.1 1P4.1 1P1.2 1P7.1 1P5.2 1P2.1 "
+         "1P3.5 1P6.0 1P2.2 1P5.3 1P6.1 1P4.2 1P2.3 1P6.2 1P7.2 1P0.1 1P4.3 1P3.6 1P4.4 1P5.4 1P7.3 1P4.5 2P5.0 2P0.0 2P1.0 2P7.0 2P2.0 "
+         "2P3.0 2P3.1 2P3.2 2P3.3 2P3.4 2P4.0 2P4.1 2P2.1 2P1.1 2P5.1 2P2.2 2P6.0 2P7.1 2P5.2 2P6.1 2P4.2 2P3.5 2P6.2 2P4.3 2P5.3 2P4.4 "
+         "2P2.3 2P5.4 2P4.5 2P0.1 2P1.2 2P3.6 2P5.5 2P0.2 2P7.2 2P7.3 2P3.7 2P3.8 2P3.9",
+    "g": "spi.0 spw.0 sSI.0 siu.0 sxr.2 sinc.1 sdg.1 sdg.0 sc16.0 sca.0 sX0.0 son.0 snn.0 sO7.0 sO6.0 sO8.0 sX0.3 sW.1 sM2.0 sW.0 sKF0.0 "
+         "sD.2 sinc.0 sD.3 sM2.1 sM1.0 sT2.0 sM1.1 sM2.2 sNW.0 sTri.0 sc128.0 sM2.3 sM1.2 sM1.3 sM2.4 sinc.2 sM1.4 sM2.5 sT5.0 sphn.0 "
+         "sM1.5 sM1.6 sM1.7 sM2.6 sM1.8 sM1.9 sM2.7 0X1.2 sw2.0 sM2.8 0X1.3 0X1.5 sM2.9 sHH.0 sM1.10 sT5.1 sM2.10 sM2.11 sM1.11 0NW.2 "
+         "1X2.2 1X2.3 1X2.5 1NW.2 2X3.1",
+    "s": "sxr.0 sxr.1 sX0.4 sXB.0 sXB.2 sXB.1 0X1.1 sNW.1 sX1.0 0X1.0 sKF1.0 sKI0.0 sKI1.0 sW.5 sX2.0 sX3.0 sX3.1 0XB.0 0XB.1 0XB.2 0W.0 "
+         "1X2.0 1X2.1 1XB.0 1XB.1 1XB.2 1W.0 2X3.0 2out.1 2out.0",
 }
 
 
@@ -183,7 +150,7 @@ def build(g, T, topo, core, rank):
         return put(ts_(o, a, s1, op0, s2, op1), o, a, s1, s2)
 
     def tt(o, a, b, op):
-        return put({"v": lambda: g.vector.tensor_tensor(ap(o), side(a), ap(b), op)}, o, a, b)
+        return put({"v": lambda: g.vector.tensor_tensor(side(o), side(a), ap(b), op)}, o, a, b)
 
     def cp(o, a):
         return put(cp_(o, a), o, a)
@@ -311,6 +278,7 @@ def build(g, T, topo, core, rank):
     ts(R("T3", 136, 272), R("M0", 0, 136), C(9), ALU.is_equal, C(10), ALU.mult)
     lin(R("T4"), R("T3"), scale=-BIG)
     ts(R("Tm"), R("M0"), 15.0, ALU.is_equal)
+    lin(R("Tn"), R("Tm"), scale=-1.0)
     keep(R("T2"), R("Tm"), ALU.is_ge, 1, -1, 16, 0)
     keep(R("T5"), R("Tm"), ALU.is_ge, 3, -1, 16, 0)
     keep(R("T5"), R("T5"), ALU.is_ge, -2, 1, -16, 0)
@@ -318,6 +286,8 @@ def build(g, T, topo, core, rank):
     lin(R("N4"), Im, scale=-4096.0)
     lin(R("IB"), Im, scale=BIG)
     lin(R("I32"), Im)
+    lin(R("Na"), Im, scale=-2.0 * OD)
+    lin(R("Nb"), Im, scale=float(V + 2 * OD - 2 * GO))
     act(R("ab"), R("M0", 0, 128), ACT.Abs, bias=-7.5)
     ts(R("Bm"), R("ab"), 8.0, ALU.is_lt)
     keep(R("Tri"), R("Bm"), ALU.is_ge, 0, -1, 16, 1)
@@ -335,6 +305,7 @@ def build(g, T, topo, core, rank):
     ts(R("A0"), R("M0", 0, 128), 0.0, ALU.is_equal, float(OD), ALU.mult)
     ts(R("w0"), R("M0", 0, 128), 0.0, ALU.is_equal, C(14), ALU.mult)
     ts(R("w1"), R("M0", 0, 128), 1.0, ALU.is_equal, C(15), ALU.mult)
+    tt(R("w0"), R("w0"), R("w1"), ALU.add)
     keep(R("w2", 0, 128), R("Bm"), ALU.is_equal, -3, 0, 0, 1)
     ts(R("w2", 128, 256), R("M0", 0, 128), 2.0, ALU.is_equal, C(16), ALU.mult)
     ts(R("w2", 256, 384), R("M0", 0, 128), 3.0, ALU.is_equal, C(17), ALU.mult)
@@ -350,6 +321,7 @@ def build(g, T, topo, core, rank):
               R("HH", 128, 136), R("KF0", 0, 320)):
         fill(o, 0)
     fill(R("D", JK + 1, JK + 2), -0.25)
+    fill(R("G"), -1)
     fill(R("D", H, OD), 100)
     fill(R("D", GO, XW), 100)
     for k in range(4):
@@ -368,7 +340,10 @@ def build(g, T, topo, core, rank):
     fill(R("pw", 0, 24), 2)
     fill(R("pw", 24, 48), 0.5)
     scan(R("pw", 48, 72), R("pw", 0, 24), R("SI", 100, 124), ALU.mult, ALU.add, 0.5)
-    scan(R("pw", 72, 96), R("pw", 24, 48), R("SF", 100, 124), ALU.mult, ALU.add, 1.0)
+    scan(R("pw", 72, 96), R("pw", 24, 48), R("SF", 100, 124), ALU.mult, ALU.add, 2.0)
+    lin(R("pw", 71, 72), R("pw", 71, 72), scale=-1.0)
+    lin(R("pw", 95, 96), R("pw", 95, 96), scale=0.75)
+    lin(R("Bh"), R("Bm"), scale=1.0 / 32)
     for k in range(4):
         for h in range(2):
             lin(R("bas", 2 * k + h, 192, 8), R("pw", 48, 72), bias=E(8), scale=E(k + 3 * h if k < 3 else 6 + h))
@@ -415,9 +390,7 @@ def build(g, T, topo, core, rank):
     lin(R("FR"), P(4, 0, 192), scale=1.0 / H)
     for k in range(2):
         copy(R("X0", k * 768, (k + 1) * 768), [R("xr"), R("yo", 48 * k, 48 * k + 48)])
-    for lo, hi, way in CUT:
-        if way == "t" and lo < H:
-            dma("s", R("XB", lo, hi), R("X0", lo, hi))
+    xb = [dma("s", R("XB", lo, hi), R("X0", lo, hi)) for lo, hi in EVEN]
     for b in (1, 0):
         o = P(7 - 2 * b, 0, 96)
         mm([(o, Im, R("c16", 96 * b, 96 * b + 96))] + [(o, rows(b, h), dg(k, h)) for k in range(8) for h in range(2)])
@@ -467,31 +440,45 @@ def build(g, T, topo, core, rank):
             scan(R("k" + n, 320 * b, 320 * b + 320), R("inc", 320 * r, 320 * r + 320), R(K, 0, 320), ALU.add, ALU.max)
         k0, k1 = R("k" + n, 0, 320), R("k" + n, 320, 640)
         num = [(R("w2", 0, 128), k0), (R("w2", 128, 256), k1), (R("w2", 256, 384), k1)] * (r == RO - 1)
-        mm([(P(d, 192, 512), m, x) for m, x in [(R("A0"), k0), (R("w0"), k1), (R("w1"), k1)] + num])
+        mm([(P(d, 192, 512), m, x) for m, x in [(R("A0"), k0), (R("w0"), k1)] + num])
         lin(R("DD", 320 * (n == "F"), 320 * (n == "F") + 320), P(d, 192, 512), bias=C(13), scale=1 / (128 * z))
+
+    def nexts(X, lo, hi):
+        return [R(X), R("soff", lcol(lo), lcol(lo) + (hi - lo) // 16)]
 
     for r in range(RO):
         X, Xn, last = "X%d" % r, "X%d" % (r + 1), r == RO - 1
         now[:] = [str(r), {}]
         nth("F", "FR", r)
-        for lo, hi, way in CUT:
-            nx = [R(X), R("soff", lcol(lo), lcol(lo) + (hi - lo) // 16)]
-            if way == "t":
-                tt(R("D", lo, hi), nx, R("XB", lo, hi) if r or lo < H else R("xr", 2 * (lo - OD) + 1, 2 * (hi - OD), 2), ALU.subtract)
+        odd = [(lo, lo + 512) for lo in range(OD, JK, 512)] if r else [(OD, OD + 768), (OD + 768, JK)]
+        parts = LEN1 if r else LEN0
+        for k, (lo, hi) in enumerate(odd):
+            if r:
+                o = P((0, 1, 5)[k], 0, 512)
+                copy(R("A", lo, hi), nexts(X, lo, hi))
+                mm([(o, Ni, R(X, lo, hi)), (o, Im, R("A", lo, hi))])
+                copy(R("D", lo, hi), o)
             else:
-                put({**ts_(R("D", lo, hi), nx, -1.0, ALU.mult), **act_(R("D", lo, hi), nx, ACT.Identity, scale=-1.0)}, R("D", lo, hi), nx)
-                dma("g", R("D", lo, hi), R(X, lo, hi), acc=True)
-            act(R("A", lo, hi), R("D", lo, hi), ACT.Abs)
-        for lo, hi in LEN:
-            o = P(3, lcol(lo), lcol(lo) + (hi - lo) // 16)
-            mm([(P(3, 0, 192), Im, R("D", GO - 192, GO))] * (lo == OD) + [(o, sel(p), R("A", lo + p, hi, 16)) for p in range(16)]
-               + [(P(3, 0, 192), R("N4"), R("FR"))] * (hi == H), lo == OD, hi == H)
-        for lo in range(0, H, 512):
-            act(R("AJ", lo, lo + 512), [R("D", H, XW), R("aoff", lo // 16, lo // 16 + 32)], ACT.Abs, scale=4096.0)
+                tt(R("D", lo, hi), nexts(X, lo, hi), R("xr", 2 * (lo - OD) + 1, 2 * (hi - OD), 2), ALU.subtract)
+        for lo, hi in EVEN:
+            tt(R("D", lo, hi), nexts(X, lo, hi), R("XB", lo, hi), ALU.subtract)
+        for lo, hi in odd + list(EVEN):
+            o, a = R("A", lo, hi), R("D", lo, hi)
+            if any(x <= lo < y and f for x, y, f in parts):
+                put({**ts_(o, a, 0.0, ALU.max, 2.0, ALU.mult), **act_(o, a, ACT.Relu, scale=2.0)}, o, a)
+            else:
+                act(o, a, ACT.Abs)
+        for k, (lo, hi, f) in enumerate(parts):
+            o, init = P(3, lcol(lo), lcol(lo) + (hi - lo) // 16), [(P(3, 0, 192), Im, R("D", GO - 192, GO))] * (k == 0)
+            if f:
+                mm(init + [(o, sel(p, "Tn"), R("D", lo + p, hi, 16)) for p in range(16)], k == 0, False)
+            mm(init * (not f) + [(o, sel(p), R("A", lo + p, hi, 16)) for p in range(16)]
+               + [(P(3, 0, 192), R("N4"), R("FR"))] * (hi == H), k == 0 and not f, hi == H)
+        for lo, hi in ((0, 1024), (1024, H)):
+            act(R("AJ", lo, hi), [R("D", H, XW), R("aoff", lo // 16, hi // 16)], ACT.Abs, scale=4096.0)
         ts(R("far"), P(3, 0, 192), 440.5, ALU.is_gt)
         act(R("sh"), P(3, 0, 96), ACT.Sign, bias=-239.5)
-        mm([(P(4, 0, 96), Im, R("D", GO - 96, GO))] + [(P(4, 0, 64), sel(p), R("AJ", p, 1024, 16)) for p in range(16)], stop=False)
-        mm([(P(4, 64, 96), sel(p), R("AJ", 1024 + p, H, 16)) for p in range(16)], False, False)
+        mm([(P(4, 0, 96), sel(p), R("AJ", p, H, 16)) for p in range(16)], stop=False)
         mm([(P(4, 0, 96), R("IB"), R("sh"))], start=False)
         nth("I", "far", r)
         tt(R("m2"), P(4, 0, 96), R("dj"), ALU.max)
@@ -502,16 +489,19 @@ def build(g, T, topo, core, rank):
             ts(R("moff"), R("m2"), MT, ALU.subtract)
         for lo in (OD, OD + 768):
             clip(R("C", lo, lo + 768), R("D", lo, lo + 768))
-        dma("s", R(Xn, H, JK), R(X, H, JK))
+        dma("s", R(Xn, H, JK), R(X, H, JK), after=xb)
+        if not last:
+            dma("s", R(Xn, 0, 1024), R(X, 0, 1024), after=xb)
         dma("g", R(Xn, OD, JK), R("C", OD, JK), acc=True)
         for k in range(3):
             lo, hi, o = 512 * k, 512 * k + 512, P(k % 2, 0, 512)
-            neg = any(c[0] <= lo < c[1] and c[2] == "d" for c in CUT)
-            de = R("D", lo, hi)
-            tt(de, [R("D", H, XW), R("moff", lo // 16, hi // 16)], de, ALU.subtract if neg else ALU.add)
-            clip(R("C", lo, hi), de)
-            mm([(o, Im, R(X, lo, hi)), (o, Im, R("C", lo, hi))])
-            copy(R("Y", 2 * lo, 2 * hi, 2) if last else R(Xn, lo, hi), o)
+            tt(R("D", lo, hi), [R("D", H, XW), R("moff", lo // 16, hi // 16)], R("D", lo, hi), ALU.add)
+            clip(R("C", lo, hi), R("D", lo, hi))
+            if last or k == 2:
+                mm([(o, Im, R(X, lo, hi)), (o, Im, R("C", lo, hi))])
+                copy(R("Y", 2 * lo, 2 * hi, 2) if last else R(Xn, lo, hi), o)
+            elif k == 1:
+                dma("g", R(Xn, 0, hi), R("C", 0, hi), acc=True)
         if not last:
             lin(R("c1"), [R("D", 0, H), R("h1")], bias=192.0, scale=0.55)
             act(R("c2"), R("c1"), ACT.Sign, bias=-192.0)
@@ -527,73 +517,64 @@ def build(g, T, topo, core, rank):
         lin(R("yy"), [R("D", 0, GO), oi], bias=-0.25, scale=0.5)
         ts(R("hh"), R("yy"), MAGIC, ALU.add, MAGIC, ALU.subtract)
         clip(R("si"), R("hh"))
-        tt(R("XV", 0, 320), [R(X, 0, GO), oi], R("si"), ALU.add)
-        act(R("em"), R("yy"), ACT.Abs, bias=0.25)
-        if last:
-            ts(R("e1"), R("em"), 0.5, ALU.is_equal)
-        else:
-            ts(R("e1"), R("em"), 0.3, ALU.is_gt)
-            ts(R("e2"), R("em"), 0.7, ALU.is_gt, -1.0, ALU.mult)
-        mm([(P(3, 192, 512), Im, R(n, 0, 320)) for n in ("XV", "hh", "e1") + ("e2",) * (not last)])
+        copy(R("XV", 0, 320), [R(X, 0, GO), oi])
+        ts(R("e1"), R("yy"), 0.5, ALU.add, MAGIC, ALU.add)
+        act(R("em"), R("e1"), ACT.Sign, bias=-MAGIC)
+        mm([(P(3, 192, 512), Im, R(n, 0, 320)) for n in ("XV", "hh")])
         copy(R("XV", 320, 640), P(3, 192, 512))
         if not last:
-            cp([R(Xn, 0, GO), oi], R("XV", 0, 320))
-            cp([R(Xn, 0, GO), of], R("XV", 320, 640))
-            for lo, hi, way in CUT:
-                if way == "t":
-                    dma("s", R("XB", lo, hi), R(Xn, lo, hi))
+            tt([R(Xn, 0, GO), oi], R("XV", 0, 320), R("si"), ALU.add)
+            tt([R(Xn, 0, GO), of], R("XV", 320, 640), R("em"), ALU.add)
+            xb = [dma("s", R("XB", lo, hi), R(Xn, lo, hi)) for lo, hi in EVEN]
         for k in range(3):
             lo, hi, o = 512 * k, 512 * k + 512, P(6, 512 * (k % 2), 512 * (k % 2) + 512)
             copy(R("Q", lo, hi), [R("W"), R("moff", lo // 16, hi // 16)])
             turn(o, R("Q", lo, hi))
             copy(R("Ut", lo, hi), o)
-            mm([(P(4, 128, 256), R("Ut", j, j + 128), R("Ut", j, j + 128)) for j in range(lo, hi, 128)], k == 0, k == 2)
-        mm([(P(2, 0, 320), Im, R("DD", 320, 640)), (P(2, 0, 320), Ni, R("DD", 0, 320))])
+            mm([(P(4, 128, 256), R("Bh"), R("Bm"))] * (k == 0)
+               + [(P(4, 128, 256), R("Ut", j, j + 128), R("Ut", j, j + 128)) for j in range(lo, hi, 128)], k == 0, k == 2)
+        mm([(P(2, 0, 320), Ni, R("DD", 320, 640)), (P(2, 0, 320), Im, R("DD", 0, 320))])
         copy(R("NV", 0, 320), P(2, 0, 320))
-        if NVA:
-            copy(R("G"), [R("NW"), oi])
-            mm([(P(2, 0, 320), Im, R("G")), (P(2, 0, 320), Ni, R("DD", 320, 640)), (P(2, 0, 320), Im, R("DD", 0, 320))])
-            copy(R("NV", 320, 640), P(2, 0, 320))
-        else:
-            tt(R("NV", 320, 640), [R("NW"), oi], R("NV", 0, 320), ALU.subtract)
-        cp([R("NW"), oi], R("NV", 0, 320))
-        cp([R("NW"), of], R("NV", 320, 640))
+        copy(R("NV", 320, 640), [R("NW"), oi])
+        tt([R("NW"), oi], R("NV", 0, 320), R("G"), ALU.mult)
+        tt([R("NW"), of], R("NV", 0, 320), R("NV", 320, 640), ALU.add)
         if not last:
             ev, od = P(7, 0, 96), P(5, 0, 96)
             mm([(ev, Im, R("c16", 0, 96))] + [(ev, sel(p, "T2"), R("Q", p, H, 16)) for p in range(16)], stop=False)
             mm([(od, Im, R("c16", 96, 192))] + [(od, sel(p, "T2"), R("NW", OD + p, JK, 16)) for p in range(16)])
             mm([(ev, sel(p, "T2"), R("NW", p, H, 16)) for p in range(16)], start=False)
             pointers()
-            dma("g", R("NW", 0, H), R("Q"), acc=True)
-            dma("s", R("W", 16, OD), R("NW", OD, JK), parts=2)
+            dma("g", R("NW", 0, H), R("Q"), acc=True, after=xb)
+            dma("s", R("W", 16, OD), R("NW", OD, JK), parts=2, after=xb)
         tt(R("HH", 0, 128), P(4, 128, 256), R("M1"), ALU.mult)
         tt(R("HH", 136, 264), P(4, 128, 256), R("M2"), ALU.mult)
         mm([(P(4, 256, 352), R("HH", 2, 130), R("RR")), (P(4, 256, 352), R("HH", 130, 258), R("RR"))])
-        ts(R("rn"), P(4, 256, 352), 2.0 ** 23, ALU.add, 2.0 ** 23, ALU.subtract)
-        tt(R("df"), P(4, 256, 352), R("rn"), ALU.subtract)
-        act(R("qa"), R("df"), ACT.Abs, bias=2.0 ** -25 - 0.25)
-        ts(R("dd"), R("qa"), 0.25, ALU.is_gt)
+        ts(R("rn"), P(4, 256, 352), -0.5, ALU.add)
+        ts(R("dd"), R("rn"), 1, ALU.bitwise_and)
         tt(R("FR", 96, 192), R("FR", 96, 192), R("dd"), ALU.add)
 
     mm([(P(5, 96, 192), Im, R("c16", 96, 192)), (P(5, 96, 192), R("IB"), R("FR", 96, 192))])
     ts(R("yo"), P(5, 96, 192), C(19), ALU.add, float(GO - H), ALU.min)
-    for h in range(2):
-        o = P(7, 96 * h, 96 * h + 96)
-        mm([(o, R("I32"), R("phn", 96 * h, 96 * h + 96))] + [(o, sel(p, "T2"), R("Q", 8 * h + p // 2, H, 16)) for p in range(0, 16, 2)]
-           + [(o, sel(p, "T2"), R("NW", OD * (p % 2) + 8 * h + p // 2, OD * (p % 2) + H, 16)) for p in range(16)])
-    ts(R("t3"), P(7, 0, 192), float(OD), ALU.is_ge, 1.0 - 2 * OD, ALU.mult)
-    ts(R("t4"), P(7, 0, 192), float(GO), ALU.is_ge, float(V + 2 * OD - 1 - 2 * GO), ALU.mult)
-    ts(R("t5"), P(7, 0, 192), float(GO), ALU.max, -1.0, ALU.mult)
-    lin(R("t2"), P(7, 0, 192), bias=float(GO), scale=2.0)
-    mm([(P(3, 0, 192), R("I32"), R(n)) for n in ("t3", "t4", "t5", "t2")], stop=False)
-    mm([(P(3, 96 * h, 96 * h + 96), R("T4", 136 * h + 1 - b, 136 * h + 129 - b), R("FR", 96 * b, 96 * b + 96)) for h in range(2) for b in range(2)], start=False)
+    mm([(P(7, 0, 192), R("I32"), R("phn"))]
+       + [(P(7, 96 * h, 96 * h + 96), sel(p, "T2"), R("Q", 8 * h + p // 2, H, 16)) for h in range(2) for p in range(0, 16, 2)], stop=False)
+    mm([(P(7, 96 * h, 96 * h + 96), sel(p, "T2"), R("NW", OD * (p % 2) + 8 * h + p // 2, OD * (p % 2) + H, 16))
+        for h in range(2) for p in range(16)], start=False)
+    lin(R("t2"), P(7, 0, 192), scale=2.0)
+    ts(R("t3"), P(7, 0, 192), float(OD), ALU.is_ge)
+    ts(R("t4"), P(7, 0, 192), float(GO), ALU.is_ge)
+    ts(R("t5"), P(7, 0, 192), float(GO), ALU.subtract, 0.0, ALU.max)
+    mm([(P(3, 0, 192), R("I32"), R("t2"))], stop=False)
+    mm([(P(3, 0, 192), m, R(n)) for m, n in ((R("Na"), "t3"), (Im, "t3"), (R("Nb"), "t4"), (Ni, "t4"), (Ni, "t5"))], False, False)
+    mm([(P(3, 96 * h, 96 * h + 96), R("T4", 136 * h + 1 - b, 136 * h + 129 - b), R("FR", 96 * b, 96 * b + 96))
+        for h in range(2) for b in range(2)], start=False)
     for h in range(2):
         ts(R("ynb", h, 192, 2), P(3, 96 * h, 96 * h + 96), -1.0, ALU.max)
     dma("s", lambda: T.yn[:], R("ynb"))
     for k in range(NQ):
         w = V // NQ
         copy(R("Y", w * k + 1, w * k + w, 2), [R("X3", H, XW), R("yo", w // 32 * k, w // 32 * (k + 1))])
-    cp([R("Y"), R("ifo", 40, 80)], R("XV"))
+    tt([R("Y"), R("ifo", 40, 60)], R("XV", 0, 320), R("si"), ALU.add)
+    tt([R("Y"), R("ifo", 60, 80)], R("XV", 320, 640), R("em"), ALU.add)
     for k in range(2):
         dma("sa"[k], lambda k=k: T.yx[:, H * k:H * k + H], R("Y", H * k, H * k + H))
     return ops
@@ -602,7 +583,7 @@ def build(g, T, topo, core, rank):
 def depend(ops):
     acc, deps, last = {}, [], {}
     for i, op in enumerate(ops):
-        d = {j: "order" for j in op[4]}
+        d = {j: "data" for j in op[4]}
         for rs, w in ((op[1], False), (op[2], True)):
             for r in rs:
                 for j, x, w2 in acc.get(r[0], ()):

from concourse.bass import DstId, RemoteDMATransfer
from concourse.mybir import AluOpType, ActivationFunctionType

V, H, L, CAP, RO = 3072, 1536, 96, 320, 3
SHIFTS = (1, 3)
OD = H + 16
JK = OD + H
GO = JK + 2 * CAP
XW = GO + 2 * L
WW = OD + 16
KWW = 3168
BIG = float(2 ** 20)
bf, f32, i32, u16 = "bfloat16", "float32", "int32", "uint16"

SB = {
    "xr": (V + 16, bf), "X0": (XW, bf), "X1": (XW, bf), "X2": (XW, bf), "X3": (XW, bf), "Y": (V + 2 * CAP, bf), "XB": (H, bf),
    "D": (XW, bf), "NW": (GO, bf), "A": (JK, bf), "AJ": (H, bf), "C": (JK, bf), "Q": (H, bf), "W": (WW, bf), "Ut": (H, bf),
    "KI0": (KWW, f32), "KI1": (KWW, f32), "KF0": (KWW, f32), "KF1": (KWW, f32),
    "kI": (640, bf), "kF": (640, bf), "WI": (192, f32), "WF": (192, f32), "SI": (208, bf), "SF": (208, bf),
    "DD": (640, bf), "uI": (8, f32), "uF": (8, f32), "vI": (8, f32), "vF": (8, f32),
    "cI": (8, u16), "cF": (8, u16), "J0": (40, bf), "PM": (80, f32), "ifo": (80, u16),
    "tot": (8, f32), "far": (192, bf), "FR": (192, bf), "dd": (96, i32), "sh": (96, bf), "m2": (96, f32), "moff": (96, u16),
    "soff": (192, u16), "aoff": (96, u16), "dj": (96, f32), "HH": (272, f32), "rn": (96, i32), "zc": (96, f32),
    "c1": (192, bf), "c2": (192, bf), "yy": (320, f32), "hh": (320, bf), "e1": (320, f32), "em": (320, bf), "si": (320, bf),
    "G": (320, bf), "XV": (640, bf), "NV": (640, bf), "S0": (192, bf), "S1": (192, bf), "S2": (192, bf),
    "ni": (192, i32), "hi": (12, i32), "h0": (12, u16), "h1": (12, u16), "ti": (4 * 192, i32), "dg": (8 * 192, bf), "Z": (2 * 192, bf),
    "t2": (192, f32), "t3": (192, bf), "t4": (192, bf), "t5": (192, bf), "yo": (96, u16), "ynb": (192, f32),
    "iu": (144, bf), "M0": (144, bf), "pi": (8, i32), "col": (40, f32), "E": (16, f32), "on": (144, bf),
    "Tm": (144, bf), "Tn": (144, bf), "T2": (144, bf), "T5": (144, bf), "Pb": (272, bf), "T3": (272, bf), "T4": (272, bf),
    "Bm": (128, bf), "Bh": (128, bf), "Tri": (128, bf), "Im": (144, bf), "Ni": (128, bf), "N4": (128, bf), "IB": (128, bf),
    "Na": (128, bf), "Nb": (128, bf), "I32": (128, f32), "A0": (128, bf), "ab": (128, bf), "w0": (128, bf), "w1": (128, bf),
    "w2": (3 * 128, bf), "c16": (192, bf), "c128": (192, bf), "phn": (192, f32), "nn": (40, f32), "jn": (80, f32), "ca": (16, bf),
    "inc": (960, f32), "O6": (144, bf), "O7": (144, bf), "O8": (144, bf), "BP": (128, bf), "M1": (128, bf), "M2": (128, bf),
    "pw": (96, f32), "bas": (192, bf), "RR": (96, f32),
}
SCRATCH = {k: ("sbuf", [128, n], d) for k, (n, d) in SB.items()}
for _b in (0, 1, 2, 3, 4, 5, 7):
    SCRATCH["P%d" % _b] = ("psum", [128, 512], f32)
SCRATCH["P6"] = ("psum", [128, 1024], bf)
NDMA = 48
SEMAPHORES = ["cv", "ca", "cp", "cg", "sent", "arr0", "arr1", "arr2"] + ["d%d" % i for i in range(NDMA)]
ALU, ACT = AluOpType, ActivationFunctionType
MAGIC = 12582912.0
MT = 440.5 * 4096 - BIG
EVEN = ((0, 768), (768, 1280), (1280, H))
LEN0 = ((OD, JK, 0), (0, 768, 0), (768, H, 0))
LEN1 = ((OD, JK, 1), (0, 768, 0), (768, H, 1))
NQ = 4
PLAN = {
    "v": "sD.0 spi.4 spi.2 spi.1 spi.6 spi.3 spi.5 spw.1 scol.0 sSF.0 spw.2 sM0.0 sE.0 sdg.4 sIm.0 sti.0 sdg.2 sti.3 sh0.0 sti.1 sPb.1 "
         "sti.2 sPb.0 sdg.7 sdg.5 sdg.3 sdg.6 sT3.0 sT3.1 syo.0 sG.0 sTm.0 sBm.0 sh1.0 spw.3 sbas.3 ssoff.0 scol.18 sbas.0 sNb.0 sD.1 "
         "scol.19 sX0.6 ssoff.1 scol.20 saoff.0 sA0.0 sBP.0 sN4.0 scol.22 0SF.0 sw0.0 sdj.0 sw1.0 0D.1 0SF.1 0D.0 0D.2 0D.4 0D.3 sNW.2 "
         "0uF.0 sjn.0 0C.0 sNW.4 sw0.1 sI32.0 0vF.0 sNi.0 0far.0 0cF.0 0SI.1 0SI.0 sBh.0 sNW.6 0WF.0 0uI.0 0KF1.0 0vI.0 0KF0.0 0cI.0 0kF.1 "
         "0kF.0 0m2.0 0tot.0 0zc.0 0KI0.0 0m2.1 0kI.0 0moff.0 0J0.0 0kI.1 0D.5 0DD.1 0D.6 0D.7 0FR.0 0C.3 0PM.0 0Ut.0 0ifo.0 0C.4 0yy.0 "
         "0NV.0 0S1.0 0NW.0 0hh.0 0NW.1 0si.0 0e1.0 0X1.6 0soff.0 0X1.7 0HH.0 0HH.1 1A.1 0rn.0 0soff.1 0aoff.0 0dd.0 0dj.0 0FR.1 sT4.0 "
         "1SF.0 1SF.1 1D.3 1A.5 1A.3 1D.4 1uF.0 1D.5 1A.7 1A.8 sw2.1 1WF.0 1C.0 1vF.0 1cF.0 1far.0 1SI.0 1SI.1 1kF.0 1kF.1 sjn.1 1uI.0 "
         "1m2.0 1vI.0 1zc.0 1cI.0 1m2.1 1tot.0 1moff.0 1J0.0 1kI.0 1kI.1 1D.6 1D.7 1Ut.0 1C.3 1D.8 1PM.0 1FR.0 1ifo.0 1Ut.1 1yy.0 1S2.0 "
         "1hh.0 1Ut.2 1NW.0 1e1.0 1NW.1 1X2.6 1HH.0 1X2.7 1soff.0 1HH.1 2A.2 1rn.0 1soff.1 1dd.0 1aoff.0 1FR.1 1dj.0 2SF.0 2SF.1 2D.3 2A.3 "
         "2A.4 2A.5 2D.4 2D.5 2A.7 2A.8 2vF.0 2WF.0 2cF.0 sw2.2 2C.0 2far.0 2kF.0 2SI.0 2m2.0 2SI.1 2moff.0 2kF.1 2D.6 2vI.0 2WI.0 2cI.0 "
         "2Ut.0 2kI.1 2kI.0 2tot.0 2C.2 2D.7 2J0.0 2D.8 2FR.0 2PM.0 2HH.0 2ifo.0 2HH.1 2yy.0 2PM.1 2rn.0 2hh.0 2dd.0 2ifo.1 2FR.1 2NW.0 "
         "2yo.0 2NW.1 2Y.6 2Y.5 2e1.0 2Y.7 2Y.8 2t3.0 2t4.0 2t5.0 2ynb.0 2ynb.1",
    "a": "sni.0 shi.0 scol.1 scol.12 scol.5 scol.14 spw.4 scol.15 scol.2 scol.3 sbas.1 sbas.2 scol.16 sNa.0 sbas.4 scol.13 sS0.0 scol.4 "
         "scol.6 scol.9 sbas.7 scol.21 sab.0 sca.1 scol.8 sX0.2 sbas.5 sX0.5 sbas.6 sFR.0 sIB.0 sX0.1 snn.1 spw.5 sZ.0 sRR.1 scol.7 sW.2 "
         "0A.1 sW.3 0A.0 sW.4 0A.2 0A.4 0A.3 0AJ.1 0AJ.0 0C.1 sNW.3 0WI.0 0sh.0 0KI1.0 sNW.5 0DD.0 0Q.0 0Q.1 0Q.2 0C.2 0c1.0 sNW.7 0c2.0 "
         "0NV.1 0Ut.1 0XV.0 0X1.4 0Ut.2 0XV.1 sTn.0 0em.0 scol.17 scol.10 sphn.1 sRR.3 sRR.2 sRR.0 1A.0 1A.2 1D.0 1D.1 1D.2 1A.4 1A.6 "
         "1AJ.0 1AJ.1 1KF0.0 1KF1.0 scol.11 1sh.0 1WI.0 1C.1 1KI0.0 1KI1.0 1DD.0 1Q.0 1Q.1 1DD.1 1C.2 1Q.2 1c1.0 1c2.0 1NV.1 1NV.0 1C.4 "
         "1XV.0 1si.0 1X2.4 1em.0 1XV.1 2A.0 2A.1 2D.2 2D.0 2D.1 2uF.0 2A.6 2AJ.1 2AJ.0 2KF0.0 2KF1.0 2sh.0 2C.1 2Q.0 2uI.0 2Q.1 2KI1.0 "
         "2KI0.0 2Q.2 2Ut.1 2DD.0 2DD.1 2Ut.2 2C.3 2C.4 2XV.0 2NV.0 2NV.1 2Y.0 2Y.1 2si.0 2Y.2 2Y.3 2Y.4 2XV.1 2em.0 2t2.0 2out.2",
    "p": "sP4.0 sP4.1 sP4.2 sP5.0 sP3.0 sP7.0 sP3.1 sP0.0 sP1.0 sP0.1 0P7.0 sP1.1 0P3.0 sP1.2 0P3.1 0P3.2 sP1.3 0P2.0 sP0.2 0P5.0 0P1.0 "
         "0P4.0 0P5.1 0P4.1 0P1.1 0P7.1 sP0.3 0P2.1 0P2.2 0P3.3 0P6.0 sP0.4 0P5.2 0P7.2 0P2.3 0P6.1 0P4.2 0P0.0 0P4.3 0P6.2 0P3.4 0P5.3 "
         "0P4.4 0P7.3 0P4.5 1P0.0 1P1.0 1P5.0 1P7.0 1P2.0 1P3.0 1P3.1 1P3.2 1P3.3 1P3.4 1P4.0 1P1.1 1P5.1 1P4.1 1P1.2 1P7.1 1P5.2 1P2.1 "
         "1P3.5 1P6.0 1P2.2 1P5.3 1P6.1 1P4.2 1P2.3 1P6.2 1P7.2 1P0.1 1P4.3 1P3.6 1P4.4 1P5.4 1P7.3 1P4.5 2P5.0 2P0.0 2P1.0 2P7.0 2P2.0 "
         "2P3.0 2P3.1 2P3.2 2P3.3 2P3.4 2P4.0 2P4.1 2P2.1 2P1.1 2P5.1 2P2.2 2P6.0 2P7.1 2P5.2 2P6.1 2P4.2 2P3.5 2P6.2 2P4.3 2P5.3 2P4.4 "
         "2P2.3 2P5.4 2P4.5 2P0.1 2P1.2 2P3.6 2P5.5 2P0.2 2P7.2 2P7.3 2P3.7 2P3.8 2P3.9",
    "g": "spi.0 spw.0 sSI.0 siu.0 sxr.2 sinc.1 sdg.1 sdg.0 sc16.0 sca.0 sX0.0 son.0 snn.0 sO7.0 sO6.0 sO8.0 sX0.3 sW.1 sM2.0 sW.0 sKF0.0 "
         "sD.2 sinc.0 sD.3 sM2.1 sM1.0 sT2.0 sM1.1 sM2.2 sNW.0 sTri.0 sc128.0 sM2.3 sM1.2 sM1.3 sM2.4 sinc.2 sM1.4 sM2.5 sT5.0 sphn.0 "
         "sM1.5 sM1.6 sM1.7 sM2.6 sM1.8 sM1.9 sM2.7 0X1.2 sw2.0 sM2.8 0X1.3 0X1.5 sM2.9 sHH.0 sM1.10 sT5.1 sM2.10 sM2.11 sM1.11 0NW.2 "
         "1X2.2 1X2.3 1X2.5 1NW.2 2X3.1",
    "s": "sxr.0 sxr.1 sX0.4 sXB.0 sXB.2 sXB.1 0X1.1 sNW.1 sX1.0 0X1.0 sKF1.0 sKI0.0 sKI1.0 sW.5 sX2.0 sX3.0 sX3.1 0XB.0 0XB.1 0XB.2 0W.0 "
         "1X2.0 1X2.1 1XB.0 1XB.1 1XB.2 1W.0 2X3.0 2out.1 2out.0",
}


def R(n, lo=0, hi=None, st=1):
    return (n, lo, SB[n][0] if hi is None else hi, st)


def cnt(r):
    return (r[2] - r[1] + r[3] - 1) // r[3]


def lcol(s):
    return s // 16 if s < OD else 96 + (s - OD) // 16


def build(g, T, topo, core, rank):
    ops = []
    now = ["s", {}]

    def ap(r):
        if r[3] == 1:
            return T[r[0]][:, r[1]:r[2]]
        return T[r[0]][:, r[1]:r[2]:r[3]]

    def add(alt, rd, wr, kind="c", after=()):
        w = wr[0][0] if wr else "out"
        now[1][w] = now[1].get(w, -1) + 1
        ops.append([alt, list(rd), list(wr), kind, list(after), "%s%s.%d" % (now[0], w, now[1][w])])
        return len(ops) - 1

    def sc(x):
        return ap(x) if isinstance(x, tuple) else x

    def side(x):
        return ap(x[0]).indirect(ap(x[1])) if isinstance(x, list) else ap(x)

    def regs(*xs):
        out = []
        for x in xs:
            if isinstance(x, list):
                out += x
            elif isinstance(x, tuple):
                out.append(x)
        return out

    def put(alt, o, *ins):
        return add(alt, regs(*ins) + ([o[1]] if isinstance(o, list) else []), [o[0]] if isinstance(o, list) else [o])

    def ts_(o, a, s1, op0, s2=None, op1=None):
        def fn():
            if op1 is None:
                return g.vector.tensor_scalar(ap(o), side(a), sc(s1), None, op0)
            return g.vector.tensor_scalar(ap(o), side(a), sc(s1), sc(s2), op0, op1)
        return {"v": fn}

    def cp_(o, a):
        return {"v": lambda: g.vector.tensor_copy(side(o), side(a))}

    def act_(o, a, func, bias=None, scale=None):
        def fn():
            kw = {}
            if bias is not None:
                kw["bias"] = sc(bias)
            if scale is not None:
                kw["scale"] = sc(scale)
            return g.scalar.activation(side(o), side(a), func, **kw)
        return {"a": fn}

    def ts(o, a, s1, op0, s2=None, op1=None):
        return put(ts_(o, a, s1, op0, s2, op1), o, a, s1, s2)

    def tt(o, a, b, op):
        return put({"v": lambda: g.vector.tensor_tensor(side(o), side(a), ap(b), op)}, o, a, b)

    def cp(o, a):
        return put(cp_(o, a), o, a)

    def scan(o, a, b, op0, op1, init=0.0):
        return put({"v": lambda: g.vector.tensor_tensor_scan(ap(o), ap(a), ap(b), init, op0, op1)}, o, a, b)

    def act(o, a, func, bias=None, scale=None):
        return put(act_(o, a, func, bias, scale), o, a, bias, scale)

    def copy(o, a, func=ACT.Copy):
        return put({**cp_(o, a), **act_(o, a, func)}, o, a)

    def lin(o, a, bias=0.0, scale=1.0):
        return put({**ts_(o, a, scale, ALU.mult, bias, ALU.add), **act_(o, a, ACT.Identity, bias, scale)}, o, a, bias, scale)

    def clip(o, a):
        return put({**ts_(o, a, 1.0, ALU.min, -1.0, ALU.max), **act_(o, a, ACT.Sign)}, o, a)

    def mm(lst, start=True, stop=True, each=None):
        def fn():
            ins, n = None, each or len(lst)
            for i, (o, l, r) in enumerate(lst):
                ins = g.tensor.matmul(ap(o), ap(l), ap(r), start and i % n == 0, stop and i % n == n - 1)
            return ins
        return add({"p": fn}, [x[1] for x in lst] + [x[2] for x in lst], [lst[0][0]])

    def turn(o, a):
        def fn():
            ins = None
            for k in range(0, cnt(a), 128):
                ins = g.tensor.transpose(ap(P(6, o[1] + k, o[1] + k + 128)), ap(R(a[0], a[1] + k, a[1] + k + 128)), ap(Im))
            return ins
        return add({"p": fn}, [a, Im], [o])

    def iota_(o, pat, base, cm):
        def fn():
            if SB[o[0]][1] == i32:
                return g.iota(ap(o), pat, base, cm)
            return g.iota(ap(o), pat, base, cm, allow_small_or_imprecise_dtypes=True)
        return {"g": fn}

    def iota(o, pat, base=0, cm=0):
        return put(iota_(o, pat, base, cm), o)

    def fill(o, val):
        return put({"v": lambda: g.vector.memset(ap(o), float(val)), **(iota_(o, [[0, cnt(o)]], val, 0) if val == int(val) else {})}, o)

    def keep(o, a, op, base, cp_, ci, cj, other=0.0):
        return put({"g": lambda: g.affine_select(ap(o), ap(a), [[ci, cnt(o) // 16], [cj, 16]], op, other, base, cp_)}, o, a)

    def dma(q, o, a, acc=False, after=(), parts=None):
        def fn():
            if parts:
                return [g.sync.dma_start(T[o[0]][p:p + parts, o[1]:o[2]], T[a[0]][p:p + parts, a[1]:a[2]]) for p in range(0, 128, 16)]
            x, y = ap(o) if isinstance(o, tuple) else o(), ap(a) if isinstance(a, tuple) else a()
            if acc:
                return [g.dma_start(x, y, accum_op=ALU.add)]
            return [{"s": g.sync, "a": g.scalar}[q].dma_start(x, y)]
        return add({q: fn}, regs(a) + (regs(o) if acc else []), regs(o), "dma", after)

    def P(b, lo, hi, st=1):
        return ("P%d" % b, lo, hi, st)

    def C(j, n=1):
        return R("col", j, j + n)

    def E(j, n=1):
        return R("E", j, j + n)

    def sel(p, n="Tm"):
        return R(n, 15 - p, 143 - p)

    def send(r):
        trs = []
        for b, s in enumerate(SHIFTS):
            dst = T.cores[(rank - s) % len(T.cores)]
            rid, pid = topo.addr(dst, core)
            en = topo.engines(core, dst)
            k = len(en) // 2
            trs.append((rid, pid, sum(1 << e for e in en[b * k:(b + 1) * k]), k))

        def fn():
            return g.remote_dma_fused(
                [RemoteDMATransfer(dst_ids=[DstId(rid=t[0], pnc=t[1])], dma_engine_mask=t[2], remote_sem=T.sem["arr%d" % r],
                                   src=ap(R("S%d" % r, b * L, (b + 1) * L)), dst=ap(R("X%d" % r, GO + b * L, GO + (b + 1) * L)))
                 for b, t in enumerate(trs)], local_sem=T.sem.sent)
        return add({"g": fn}, [R("S%d" % r)], [R("X%d" % r, GO, XW)], ("arr%d" % r, trs[0][3] + trs[1][3]))

    Im, Ni = R("Im", 0, 128), R("Ni")
    dma("a", R("hi"), lambda: T.head[:])
    dma("a", R("ni"), lambda: T.nxt[:])
    for k in range(2):
        dma("s", R("xr", k * H, (k + 1) * H), lambda k=k: T.x[:, k * H:(k + 1) * H])
    cp(R("h0"), R("hi"))
    g0 = [copy(R("S0"), [R("xr", 0, V), R("h0")])]
    s0 = send(0)
    ts(R("h1"), R("hi"), 0.5, ALU.mult)
    for k in range(2):
        copy(R("X0", OD + k * 768, OD + (k + 1) * 768), R("xr", k * H + 1, (k + 1) * H, 2))

    iota(R("pi", 0, 1), [[0, 1]], 0, 1)
    iota(R("iu"), [[1, 144]])
    iota(R("c16"), [[OD, 2], [16, 96]])
    iota(R("c128"), [[0, 2], [128, 96]], 128 * 129)
    iota(R("nn"), [[0, 2], [16, 20]])
    fill(R("on"), 1)
    iota(R("dg", 960, 1152), [[-16, 96], [0, 2]])
    iota(R("dg", 1152, 1344), [[0, 96], [-8, 2]])
    for j, m in enumerate((112, 15, 1, 14, 8, 7)):
        ts(R("pi", j + 1, j + 2), R("pi", 0, 1), m, ALU.bitwise_and)
    cp(C(0, 7), R("pi", 0, 7))
    row = C(2)
    ts(R("M0"), R("iu"), C(1), ALU.subtract)
    ts(R("E"), R("iu", 0, 16), row, ALU.is_equal)
    ts(R("Im"), R("iu"), C(0), ALU.is_equal)
    lin(C(7), C(4), bias=8.0, scale=0.5)
    lin(C(8), C(3), bias=1.0, scale=-1.0)
    ts(R("Pb", 0, 136), R("M0", 0, 136), C(7), ALU.is_equal, C(8), ALU.mult)
    ts(R("Pb", 136, 272), R("M0", 0, 136), C(7), ALU.is_equal, C(3), ALU.mult)
    lin(C(9), C(6), bias=1.0, scale=2.0)
    lin(C(10), C(5), scale=0.125)
    lin(C(11), C(5), bias=1.0, scale=-0.125)
    ts(R("T3", 0, 136), R("M0", 0, 136), C(9), ALU.is_equal, C(11), ALU.mult)
    ts(R("T3", 136, 272), R("M0", 0, 136), C(9), ALU.is_equal, C(10), ALU.mult)
    lin(R("T4"), R("T3"), scale=-BIG)
    ts(R("Tm"), R("M0"), 15.0, ALU.is_equal)
    lin(R("Tn"), R("Tm"), scale=-1.0)
    keep(R("T2"), R("Tm"), ALU.is_ge, 1, -1, 16, 0)
    keep(R("T5"), R("Tm"), ALU.is_ge, 3, -1, 16, 0)
    keep(R("T5"), R("T5"), ALU.is_ge, -2, 1, -16, 0)
    lin(Ni, Im, scale=-1.0)
    lin(R("N4"), Im, scale=-4096.0)
    lin(R("IB"), Im, scale=BIG)
    lin(R("I32"), Im)
    lin(R("Na"), Im, scale=-2.0 * OD)
    lin(R("Nb"), Im, scale=float(V + 2 * OD - 2 * GO))
    act(R("ab"), R("M0", 0, 128), ACT.Abs, bias=-7.5)
    ts(R("Bm"), R("ab"), 8.0, ALU.is_lt)
    keep(R("Tri"), R("Bm"), ALU.is_ge, 0, -1, 16, 1)
    lin(R("nn"), R("nn"), bias=row)
    ts(R("jn", 0, 40), R("c16", 0, 40), row, ALU.add, float(JK), ALU.add)
    ts(R("jn", 40, 80), R("c16", 0, 40), row, ALU.add, float(V), ALU.add)
    fill(R("ca"), 0)
    lin(R("ca", 7, 13), R("c16", 0, 6), bias=-V / 4096, scale=-1.0 / 4096)
    lin(C(12), E(0), scale=-2048.0)
    lin(C(13), E(2), bias=C(12), scale=-4096.0)
    lin(C(14), E(15), bias=-float(OD), scale=16.0)
    lin(C(15), E(15), bias=1.0, scale=-16.0)
    lin(C(16), E(15), scale=32.0)
    lin(C(17), E(15), bias=1.0, scale=-32.0)
    ts(R("A0"), R("M0", 0, 128), 0.0, ALU.is_equal, float(OD), ALU.mult)
    ts(R("w0"), R("M0", 0, 128), 0.0, ALU.is_equal, C(14), ALU.mult)
    ts(R("w1"), R("M0", 0, 128), 1.0, ALU.is_equal, C(15), ALU.mult)
    tt(R("w0"), R("w0"), R("w1"), ALU.add)
    keep(R("w2", 0, 128), R("Bm"), ALU.is_equal, -3, 0, 0, 1)
    ts(R("w2", 128, 256), R("M0", 0, 128), 2.0, ALU.is_equal, C(16), ALU.mult)
    ts(R("w2", 256, 384), R("M0", 0, 128), 3.0, ALU.is_equal, C(17), ALU.mult)
    lin(C(18), row, scale=2.0)
    lin(C(19), row, bias=-float(H))
    lin(C(20), row, bias=MT - H)
    lin(C(21), C(3), scale=-float(OD))
    lin(C(22), C(4), scale=0.5)
    lin(C(23), C(3), bias=C(22), scale=float(OD))
    iota(R("phn"), [[8, 2], [16, 96]])
    lin(R("phn"), R("phn"), bias=C(23))
    for o in (R("SF"), R("SI"), R("D", JK, GO), R("xr", V, V + 16), R("X0", H, OD), R("NW", H, OD), R("W", 0, 16), R("W", OD, WW),
              R("HH", 128, 136), R("KF0", 0, 320)):
        fill(o, 0)
    fill(R("D", JK + 1, JK + 2), -0.25)
    fill(R("G"), -1)
    fill(R("D", H, OD), 100)
    fill(R("D", GO, XW), 100)
    for k in range(4):
        dma("s", R("X%d" % k, JK, GO), R("D", JK, GO), after=g0 if k == 0 else [s0])
    dma("s", R("X3", GO, XW), R("D", JK, JK + 2 * L), after=[s0])
    dma("s", R("NW", JK, GO), R("D", JK, GO), after=[s0])
    for n in ("KF1", "KI0", "KI1"):
        dma("s", R(n, 0, 320), R("KF0", 0, 320), after=g0)
    for r in range(RO):
        fill(R("inc", 320 * r, 320 * r + 320), 2 ** r)
    for j in (6, 7, 8):
        keep(R("O%d" % j), R("on"), ALU.is_equal, 16 - j - 256, 1, -16, 256)
    lin(C(24), row, bias=10.0)
    ts(C(25), row, 6.0, ALU.is_lt)
    ts(R("BP"), R("M0", 0, 128), C(24), ALU.is_equal, C(25), ALU.mult)
    fill(R("pw", 0, 24), 2)
    fill(R("pw", 24, 48), 0.5)
    scan(R("pw", 48, 72), R("pw", 0, 24), R("SI", 100, 124), ALU.mult, ALU.add, 0.5)
    scan(R("pw", 72, 96), R("pw", 24, 48), R("SF", 100, 124), ALU.mult, ALU.add, 2.0)
    lin(R("pw", 71, 72), R("pw", 71, 72), scale=-1.0)
    lin(R("pw", 95, 96), R("pw", 95, 96), scale=0.75)
    lin(R("Bh"), R("Bm"), scale=1.0 / 32)
    for k in range(4):
        for h in range(2):
            lin(R("bas", 2 * k + h, 192, 8), R("pw", 48, 72), bias=E(8), scale=E(k + 3 * h if k < 3 else 6 + h))
    for t in range(3):
        mm([(P(t % 2, a, 512, 8), m, R("bas", 64 * t, 64 * t + 64)) for a in range(8)
            for m in (R("BP"), sel(a, "O8"), sel((a + 1) % 8, "O6"), sel((a + 2) % 8, "O7"))], each=4)
        copy(R("W", 16 + 512 * t, 528 + 512 * t), P(t % 2, 0, 512))
    tt(C(26, 3), E(10, 3), E(13, 3), ALU.add)
    act(C(30), row, ACT.Abs, bias=-5.5)
    ts(C(29), C(30), 4.0, ALU.is_lt)
    for k in range(4):
        lin(R("RR", k, 96, 4), R("pw", 72, 96), scale=C(26 + k))
    for h in range(2):
        M = R("M%d" % (h + 1))
        keep(M, R("Bm"), ALU.is_ge, -10 - 3 * h, 1, -16, 0)
        keep(M, M, ALU.is_ge, 12 + 3 * h, -1, 16, 0)
        keep(M, M, ALU.is_ge, -2, 0, 0, 1)
        keep(M, M, ALU.is_ge, 9, 0, 0, -1)
        for a in range(8):
            keep(M, M, ALU.not_equal, -2 - (a + 1 + h) % 8 - 256 * (2 + a), 1, -16, 256, 1.0)

    def ti(k):
        return R("ti", 192 * k, 192 * k + 192)

    def dg(k, h=None):
        return R("dg", 192 * k, 192 * k + 192) if h is None else R("dg", 192 * k + h, 192 * k + 192, 2)

    def rows(b, h):
        return R("Pb", 136 * b + 8 - 8 * h, 136 * b + 136 - 8 * h)
    ts(ti(0), R("ni"), float(V), ALU.min, 0.0, ALU.max)
    ts(dg(7), R("ni"), 0.0, ALU.is_lt, float(H), ALU.mult)
    ts(dg(2), R("ni"), float(V), ALU.is_ge, float(GO - H), ALU.mult)
    ts(dg(4), R("ni"), float(V), ALU.subtract, 0.0, ALU.max)
    ts(ti(1), ti(0), 1, ALU.arith_shift_right, 4080, ALU.bitwise_and)
    ts(ti(2), ti(0), 1, ALU.bitwise_and)
    ts(ti(3), ti(0), 1, ALU.arith_shift_right, 15, ALU.bitwise_and)
    cp(dg(0), ti(1))
    ts(dg(1), ti(2), float(OD), ALU.mult, C(21), ALU.add)
    ts(dg(3), ti(3), C(22), ALU.subtract)
    for b in range(2):
        mm([(P(4, 96 * b, 96 * b + 96), rows(b, h), dg(7, h)) for h in range(2)])
    mm([(P(4, 192, 288), rows(0, h), dg(7, h)) for h in (0, 1, 0, 1)] + [(P(4, 192, 288), Im, R("c16", 0, 96))] * 2)
    ts(R("yo"), P(4, 192, 288), C(18), ALU.add, float(V), ALU.min)
    lin(R("FR"), P(4, 0, 192), scale=1.0 / H)
    for k in range(2):
        copy(R("X0", k * 768, (k + 1) * 768), [R("xr"), R("yo", 48 * k, 48 * k + 48)])
    xb = [dma("s", R("XB", lo, hi), R("X0", lo, hi)) for lo, hi in EVEN]
    for b in (1, 0):
        o = P(7 - 2 * b, 0, 96)
        mm([(o, Im, R("c16", 96 * b, 96 * b + 96))] + [(o, rows(b, h), dg(k, h)) for k in range(8) for h in range(2)])

    def pointers():
        ts(R("soff", 96, 192), P(5, 0, 96), row, ALU.add)
        ts(R("soff", 0, 96), P(7, 0, 96), row, ALU.add)
        ts(R("aoff"), P(7, 0, 96), C(19), ALU.add, 0.0, ALU.max)
        lin(R("dj"), P(7, 0, 96), bias=C(20))
    pointers()
    for h in range(2):
        o = P(3, 192 * h, 192 * h + 192)
        mm([(o, R("T3", 136 * h + 1 - b, 136 * h + 129 - b), dg(k)) for b, ks in enumerate(((0, 1, 2, 5, 7), (3, 4, 6))) for k in ks])
    copy(R("Z"), P(3, 0, 384))
    for t in range(6):
        b, c = 1 - t // 3, 64 * (t % 3)
        mm([(P((t + 1) % 2, p // 2, 512, 8), R("Im", 2 * (p % 8), 2 * (p % 8) + 128), R("Z", 192 * (p // 8) + c, 192 * (p // 8) + c + 64))
            for p in range(b, 16, 2)], each=1)
        copy(R("NW", OD * b + 8 * c, OD * b + 8 * c + 512), P((t + 1) % 2, 0, 512))
    dma("s", R("W", 16, OD), R("NW", OD, JK), parts=2)

    def nth(n, a, r):
        S, z = "S" + n, float(2 ** r)
        a0, a1, a2 = R(a, 0, 96), R(a, 96, 192), R(S, 112, 208)
        tt(a2, a0, a1, ALU.add)
        scan(R(S, 1, 97), a0, a1, ALU.add, ALU.add)
        d, k, w = (3, 5, 1) if n == "I" else (7, 7, 2)
        mm([(P(w, 0, 192), Ni, R("c128")), (P(w, 0, 96), R("Tri"), a2), (P(w, 0, 96), Ni, a1), (P(w, 96, 192), R("Tri"), a2)])
        lin(R("W" + n), P(w, 0, 192), bias=z * (0.5 - 64), scale=-z)
        mm([(P(k, 384, 397), Im, R("ca", 0, 13))] + [(P(k, 384, 397), sel(p), R(S, p, 208, 16)) for p in range(16)])
        lin(R("u" + n, 0, 6), P(k, 391, 397), bias=row, scale=-4096.0)
        tt(R("v" + n, 0, 6), R("u" + n, 0, 6), P(k, 384, 390), ALU.max)
        cp(R("c" + n, 0, 6), R("v" + n, 0, 6))
        if n == "F":
            mm([(P(2, 192, 288), R("Bm"), R(S, 0, 96)), (P(2, 192, 288), R("Tri"), a2), (P(2, 192, 288), Ni, a1), (P(2, 192, 288), R("IB"), a0)])
            mm([(P(2, 288, 384), R("Bm"), R(S, 0, 96)), (P(2, 288, 384), R("Tri"), a2), (P(2, 288, 384), R("IB"), a1)])
        else:
            if r < RO - 1:
                mm([(P(1, 192, 288), R("Bm"), R(S, 0, 96)), (P(1, 192, 288), R("Tri"), a2), (P(1, 192, 288), Ni, a1), (P(1, 192, 288), R("N4"), a0)])
                ts(R("zc"), P(1, 192, 288), CAP + 0.5 - 4096, ALU.is_lt, OD + MT, ALU.add)
            mm([(P(5, 400, 401), R("Bm"), R(S, 96, 97))])
            ts(R("tot", 0, 1), P(5, 400, 401), float(CAP), ALU.min)
            ts(R("FR"), P(2, 192, 384), BIG, ALU.subtract, R("tot", 0, 1), ALU.is_gt)
        for b in range(2):
            K = "K%s%d" % (n, b)
            copy([R(K), R("c" + n, 0, 6)], R("W" + n, 96 * b, 96 * b + 96), ACT.Silu)
            scan(R("k" + n, 320 * b, 320 * b + 320), R("inc", 320 * r, 320 * r + 320), R(K, 0, 320), ALU.add, ALU.max)
        k0, k1 = R("k" + n, 0, 320), R("k" + n, 320, 640)
        num = [(R("w2", 0, 128), k0), (R("w2", 128, 256), k1), (R("w2", 256, 384), k1)] * (r == RO - 1)
        mm([(P(d, 192, 512), m, x) for m, x in [(R("A0"), k0), (R("w0"), k1)] + num])
        lin(R("DD", 320 * (n == "F"), 320 * (n == "F") + 320), P(d, 192, 512), bias=C(13), scale=1 / (128 * z))

    def nexts(X, lo, hi):
        return [R(X), R("soff", lcol(lo), lcol(lo) + (hi - lo) // 16)]

    for r in range(RO):
        X, Xn, last = "X%d" % r, "X%d" % (r + 1), r == RO - 1
        now[:] = [str(r), {}]
        nth("F", "FR", r)
        odd = [(lo, lo + 512) for lo in range(OD, JK, 512)] if r else [(OD, OD + 768), (OD + 768, JK)]
        parts = LEN1 if r else LEN0
        for k, (lo, hi) in enumerate(odd):
            if r:
                o = P((0, 1, 5)[k], 0, 512)
                copy(R("A", lo, hi), nexts(X, lo, hi))
                mm([(o, Ni, R(X, lo, hi)), (o, Im, R("A", lo, hi))])
                copy(R("D", lo, hi), o)
            else:
                tt(R("D", lo, hi), nexts(X, lo, hi), R("xr", 2 * (lo - OD) + 1, 2 * (hi - OD), 2), ALU.subtract)
        for lo, hi in EVEN:
            tt(R("D", lo, hi), nexts(X, lo, hi), R("XB", lo, hi), ALU.subtract)
        for lo, hi in odd + list(EVEN):
            o, a = R("A", lo, hi), R("D", lo, hi)
            if any(x <= lo < y and f for x, y, f in parts):
                put({**ts_(o, a, 0.0, ALU.max, 2.0, ALU.mult), **act_(o, a, ACT.Relu, scale=2.0)}, o, a)
            else:
                act(o, a, ACT.Abs)
        for k, (lo, hi, f) in enumerate(parts):
            o, init = P(3, lcol(lo), lcol(lo) + (hi - lo) // 16), [(P(3, 0, 192), Im, R("D", GO - 192, GO))] * (k == 0)
            if f:
                mm(init + [(o, sel(p, "Tn"), R("D", lo + p, hi, 16)) for p in range(16)], k == 0, False)
            mm(init * (not f) + [(o, sel(p), R("A", lo + p, hi, 16)) for p in range(16)]
               + [(P(3, 0, 192), R("N4"), R("FR"))] * (hi == H), k == 0 and not f, hi == H)
        for lo, hi in ((0, 1024), (1024, H)):
            act(R("AJ", lo, hi), [R("D", H, XW), R("aoff", lo // 16, hi // 16)], ACT.Abs, scale=4096.0)
        ts(R("far"), P(3, 0, 192), 440.5, ALU.is_gt)
        act(R("sh"), P(3, 0, 96), ACT.Sign, bias=-239.5)
        mm([(P(4, 0, 96), sel(p), R("AJ", p, H, 16)) for p in range(16)], stop=False)
        mm([(P(4, 0, 96), R("IB"), R("sh"))], start=False)
        nth("I", "far", r)
        tt(R("m2"), P(4, 0, 96), R("dj"), ALU.max)
        if last:
            ts(R("moff"), R("m2"), MT, ALU.subtract, float(OD), ALU.min)
        else:
            tt(R("m2"), R("m2"), R("zc"), ALU.min)
            ts(R("moff"), R("m2"), MT, ALU.subtract)
        for lo in (OD, OD + 768):
            clip(R("C", lo, lo + 768), R("D", lo, lo + 768))
        dma("s", R(Xn, H, JK), R(X, H, JK), after=xb)
        if not last:
            dma("s", R(Xn, 0, 1024), R(X, 0, 1024), after=xb)
        dma("g", R(Xn, OD, JK), R("C", OD, JK), acc=True)
        for k in range(3):
            lo, hi, o = 512 * k, 512 * k + 512, P(k % 2, 0, 512)
            tt(R("D", lo, hi), [R("D", H, XW), R("moff", lo // 16, hi // 16)], R("D", lo, hi), ALU.add)
            clip(R("C", lo, hi), R("D", lo, hi))
            if last or k == 2:
                mm([(o, Im, R(X, lo, hi)), (o, Im, R("C", lo, hi))])
                copy(R("Y", 2 * lo, 2 * hi, 2) if last else R(Xn, lo, hi), o)
            elif k == 1:
                dma("g", R(Xn, 0, hi), R("C", 0, hi), acc=True)
        if not last:
            lin(R("c1"), [R("D", 0, H), R("h1")], bias=192.0, scale=0.55)
            act(R("c2"), R("c1"), ACT.Sign, bias=-192.0)
            tt(R("S%d" % (r + 1)), [R(X, 0, H), R("h1")], R("c2"), ALU.add)
            send(r + 1)
        ts(R("J0"), R("nn"), R("tot", 0, 1), ALU.is_ge, BIG, ALU.mult)
        for k in range(1 + last):
            o = P(5, 420 + 40 * k, 460 + 40 * k)
            mm([(o, Im, R("J0"))] + [(o, sel(p, ("T2", "T5")[k]), R("DD", p, 640, 16)) for p in range(16)])
            tt(R("PM", 40 * k, 40 * k + 40), o, R("jn", 40 * k, 40 * k + 40), ALU.min)
            cp(R("ifo", 40 * k, 40 * k + 40), R("PM", 40 * k, 40 * k + 40))
        oi, of = R("ifo", 0, 20), R("ifo", 20, 40)
        lin(R("yy"), [R("D", 0, GO), oi], bias=-0.25, scale=0.5)
        ts(R("hh"), R("yy"), MAGIC, ALU.add, MAGIC, ALU.subtract)
        clip(R("si"), R("hh"))
        copy(R("XV", 0, 320), [R(X, 0, GO), oi])
        ts(R("e1"), R("yy"), 0.5, ALU.add, MAGIC, ALU.add)
        act(R("em"), R("e1"), ACT.Sign, bias=-MAGIC)
        mm([(P(3, 192, 512), Im, R(n, 0, 320)) for n in ("XV", "hh")])
        copy(R("XV", 320, 640), P(3, 192, 512))
        if not last:
            tt([R(Xn, 0, GO), oi], R("XV", 0, 320), R("si"), ALU.add)
            tt([R(Xn, 0, GO), of], R("XV", 320, 640), R("em"), ALU.add)
            xb = [dma("s", R("XB", lo, hi), R(Xn, lo, hi)) for lo, hi in EVEN]
        for k in range(3):
            lo, hi, o = 512 * k, 512 * k + 512, P(6, 512 * (k % 2), 512 * (k % 2) + 512)
            copy(R("Q", lo, hi), [R("W"), R("moff", lo // 16, hi // 16)])
            turn(o, R("Q", lo, hi))
            copy(R("Ut", lo, hi), o)
            mm([(P(4, 128, 256), R("Bh"), R("Bm"))] * (k == 0)
               + [(P(4, 128, 256), R("Ut", j, j + 128), R("Ut", j, j + 128)) for j in range(lo, hi, 128)], k == 0, k == 2)
        mm([(P(2, 0, 320), Ni, R("DD", 320, 640)), (P(2, 0, 320), Im, R("DD", 0, 320))])
        copy(R("NV", 0, 320), P(2, 0, 320))
        copy(R("NV", 320, 640), [R("NW"), oi])
        tt([R("NW"), oi], R("NV", 0, 320), R("G"), ALU.mult)
        tt([R("NW"), of], R("NV", 0, 320), R("NV", 320, 640), ALU.add)
        if not last:
            ev, od = P(7, 0, 96), P(5, 0, 96)
            mm([(ev, Im, R("c16", 0, 96))] + [(ev, sel(p, "T2"), R("Q", p, H, 16)) for p in range(16)], stop=False)
            mm([(od, Im, R("c16", 96, 192))] + [(od, sel(p, "T2"), R("NW", OD + p, JK, 16)) for p in range(16)])
            mm([(ev, sel(p, "T2"), R("NW", p, H, 16)) for p in range(16)], start=False)
            pointers()
            dma("g", R("NW", 0, H), R("Q"), acc=True, after=xb)
            dma("s", R("W", 16, OD), R("NW", OD, JK), parts=2, after=xb)
        tt(R("HH", 0, 128), P(4, 128, 256), R("M1"), ALU.mult)
        tt(R("HH", 136, 264), P(4, 128, 256), R("M2"), ALU.mult)
        mm([(P(4, 256, 352), R("HH", 2, 130), R("RR")), (P(4, 256, 352), R("HH", 130, 258), R("RR"))])
        ts(R("rn"), P(4, 256, 352), -0.5, ALU.add)
        ts(R("dd"), R("rn"), 1, ALU.bitwise_and)
        tt(R("FR", 96, 192), R("FR", 96, 192), R("dd"), ALU.add)

    mm([(P(5, 96, 192), Im, R("c16", 96, 192)), (P(5, 96, 192), R("IB"), R("FR", 96, 192))])
    ts(R("yo"), P(5, 96, 192), C(19), ALU.add, float(GO - H), ALU.min)
    mm([(P(7, 0, 192), R("I32"), R("phn"))]
       + [(P(7, 96 * h, 96 * h + 96), sel(p, "T2"), R("Q", 8 * h + p // 2, H, 16)) for h in range(2) for p in range(0, 16, 2)], stop=False)
    mm([(P(7, 96 * h, 96 * h + 96), sel(p, "T2"), R("NW", OD * (p % 2) + 8 * h + p // 2, OD * (p % 2) + H, 16))
        for h in range(2) for p in range(16)], start=False)
    lin(R("t2"), P(7, 0, 192), scale=2.0)
    ts(R("t3"), P(7, 0, 192), float(OD), ALU.is_ge)
    ts(R("t4"), P(7, 0, 192), float(GO), ALU.is_ge)
    ts(R("t5"), P(7, 0, 192), float(GO), ALU.subtract, 0.0, ALU.max)
    mm([(P(3, 0, 192), R("I32"), R("t2"))], stop=False)
    mm([(P(3, 0, 192), m, R(n)) for m, n in ((R("Na"), "t3"), (Im, "t3"), (R("Nb"), "t4"), (Ni, "t4"), (Ni, "t5"))], False, False)
    mm([(P(3, 96 * h, 96 * h + 96), R("T4", 136 * h + 1 - b, 136 * h + 129 - b), R("FR", 96 * b, 96 * b + 96))
        for h in range(2) for b in range(2)], start=False)
    for h in range(2):
        ts(R("ynb", h, 192, 2), P(3, 96 * h, 96 * h + 96), -1.0, ALU.max)
    dma("s", lambda: T.yn[:], R("ynb"))
    for k in range(NQ):
        w = V // NQ
        copy(R("Y", w * k + 1, w * k + w, 2), [R("X3", H, XW), R("yo", w // 32 * k, w // 32 * (k + 1))])
    tt([R("Y"), R("ifo", 40, 60)], R("XV", 0, 320), R("si"), ALU.add)
    tt([R("Y"), R("ifo", 60, 80)], R("XV", 320, 640), R("em"), ALU.add)
    for k in range(2):
        dma("sa"[k], lambda k=k: T.yx[:, H * k:H * k + H], R("Y", H * k, H * k + H))
    return ops


def depend(ops):
    acc, deps, last = {}, [], {}
    for i, op in enumerate(ops):
        d = {j: "data" for j in op[4]}
        for rs, w in ((op[1], False), (op[2], True)):
            for r in rs:
                for j, x, w2 in acc.get(r[0], ()):
                    if r[0] not in SB:
                        if not ("p" in op[0] and "p" in ops[j][0]):
                            d[j] = "data" if w or w2 else d.get(j, "bank")
                    elif (w or w2) and x[1] < r[2] and r[1] < x[2] and not (x[3] == r[3] and (x[1] - r[1]) % r[3]):
                        d[j] = "data"
        for rs, w in ((op[1], False), (op[2], True)):
            for r in rs:
                acc.setdefault(r[0], []).append((i, r, w))
        if "p" in op[0]:
            if op[2][0][0] in last:
                d.setdefault(last[op[2][0][0]], "order")
            last[op[2][0][0]] = i
        d.pop(i, None)
        deps.append(d)
    return deps


def arrange(ops, deps):
    at = {op[5]: i for i, op in enumerate(ops)}
    todo = {q: [at[w] for w in s.split()][::-1] for q, s in PLAN.items()}
    order, on = [], {}
    while len(order) < len(ops):
        q = next(q for q in todo if todo[q] and all(j in on for j in deps[todo[q][-1]]))
        order.append(todo[q].pop())
        on[order[-1]] = q
    return order, on


def rank_program(g, core, T, topo):
    rank = T.rank_of(core)
    if rank is None:
        return
    ops = build(g, T, topo, core, rank)
    deps = depend(ops)
    order, on = arrange(ops, deps)
    Q = {"v": g.vector, "a": g.scalar, "p": g.tensor, "g": g, "s": g.sync}
    mark, total, seen, nd = {}, {}, {q: {} for q in Q}, 0
    at, knew, by = {i: k for k, i in enumerate(order)}, {}, {}
    for i in order:
        op, q = ops[i], on[i]
        for j in sorted(deps[i], key=lambda j: -at[j]):
            s, v = mark[j]
            if seen[q].get(s, 0) >= v or (on[j] == q and (q == "p" or deps[i][j] != "data")):
                continue
            Q[q].wait_ge(T.sem[s], v)
            for x, y in list(knew[by[s, v]].items()) + [(s, v)]:
                seen[q][x] = max(seen[q].get(x, 0), y)
        knew[i] = dict(seen[q]) if op[3] in ("c", "dma") else {}
        ins = op[0][q]()
        if op[3] == "c":
            s = "c" + q
            total[s] = total.get(s, 0) + 1
            ins.then_inc(T.sem[s], 1)
            mark[i] = (s, total[s])
        elif op[3] == "dma":
            s = "d%d" % nd
            nd += 1
            total[s] = 16 * len(ins)
            for x in ins:
                x.then_inc(T.sem[s], 16)
            mark[i] = (s, total[s])
        else:
            mark[i] = op[3]
            total[op[3][0]] = op[3][1]
            total["sent"] = total.get("sent", 0) + op[3][1]
        by[mark[i]] = i
    for s in sorted(total):
        if seen["g"].get(s, 0) < total[s]:
            g.wait_ge(T.sem[s], total[s])
